import numpy as np, ml_dtypes
CORES = [48,51,52,55]
N = 4
BF = ml_dtypes.bfloat16
def gentries(a):
    return np.ascontiguousarray(a.reshape(8, 16, -1).transpose(0, 2, 1)).reshape(8, -1)
def gtable(e):
    e = np.asarray(e); return np.ascontiguousarray(e.reshape(8, -1, 16).transpose(0, 2, 1)).reshape(128, -1).astype(np.int32)
S, K, W, C, RO = 256, 16, 4096, 16, 6
def H(e, v):
    return ((e * v >> 5) + e + 37 * v) & (W - 1)
def U(x, w):
    return np.add.reduce(x * w, axis=-1, dtype=np.int32) & (W - 1)
def applies(d, x, least):
    return np.add.reduce(d > x, axis=-1, dtype=np.int32) >= least
def parts(rng):
    lev = rng.choice(np.array([96, 160, 256]), (N, 8, 1, W))
    d = (rng.random((N, 8, 16, W)) * lev).astype(np.int64)
    return d, rng.integers(0, W, (N, 8, S, K)), rng.integers(0, 256, (N, 8, 16, S)), rng.integers(1, 256, (N, 8, 16))
def pack(d, e, z, w):
    return {"dv": d.reshape(N, 128, W).astype(np.float32).astype(BF), "ef": np.stack([gtable(a.reshape(8, -1)) for a in e]),
            "zv": z.reshape(N, 128, S).astype(np.float32).astype(BF), "wt": w.reshape(N, 128, 1).astype(np.int32)}
def stage(rng, d, w, r, g):
    o = rng.permutation(16); w[r, g] = 1; w[r, g, o[:8]] = 255
    m = np.zeros(16, np.int64); m[o[:4]] = 255; m[o[8:12]] = 255
    q = np.zeros(16, np.int64); q[rng.permutation(o[:15])[:9]] = 255
    row = int(o[15]); one = np.zeros(16, np.int64); one[row] = 255
    d[r, g, :, 0] = m; d[r, g, :, W - 1] = q; d[r, g, :, H(W - 1, 255 * 1024 & (W - 1))] = 255
    d[r, g, :, H(0, 255)] = m + one; d[r, g, :, H(W - 1, 255)] = q + one
    return row
def setup_inputs(rng):
    return pack(*parts(rng))
def setup_inputs_corners(rng):
    d, e, z, w = parts(rng); i = np.arange(S); kk = np.arange(K)
    for r in range(N):
        for g in range(8):
            if (r + g) % 2 == 1:
                stage(rng, d, w, r, g)
                few = np.argsort(np.argsort(rng.random((16, 64)), axis=0), axis=0) < np.where(np.arange(64) % 4 == 1, 0, 7)
                d[r, g, :, 16:80] = few * rng.integers(1, 256, (16, 64))
                goal = rng.choice(np.array([0, 1, 2, K - 2, K - 1]), S)[:, None]
                cold = rng.integers(16, 80, (S, K))
                v = np.where((kk < goal) | (goal == 0), cold, np.where(kk == goal, W - 1, e[r, g])); v[:, 0] = 0
                m = i % 4 != 3
                e[r, g] = np.where(m[:, None], v, e[r, g]); z[r, g] = np.where(m, 0, z[r, g])
            else:
                e[r, g, ::4] = e[r, g, ::4, :1]; e[r, g, 1::4] = (W - 1) * rng.integers(0, 2, e[r, g, 1::4].shape)
                z[r, g, :, 5::8] = 255; z[r, g, :, 6::8] = 0
    return pack(d, e, z, w)
def setup_inputs_ends(rng):
    p = rng.choice(np.array([0.0, 0.25, 0.5, 0.75, 0.9, 1.0]), (N, 8, 1, W)); d = 255 * (rng.random((N, 8, 16, W)) < p).astype(np.int64)
    d[..., 2::4] = rng.integers(0, 256, d[..., 2::4].shape)
    p = rng.choice(np.array([0.0, 0.1, 0.3, 0.5, 1.0]), (N, 8, 1, S)); z = 255 * (rng.random((N, 8, 16, S)) < p).astype(np.int64)
    z[..., 2::5] = rng.integers(0, 256, z[..., 2::5].shape)
    e = (W - 1) * rng.integers(0, 2, (N, 8, S, K)); w = np.where(rng.random((N, 8, 16)) < 0.5, 1, 255)
    for r in range(N):
        for g in range(8):
            if r < 2:
                row = stage(rng, d, w, r, g); z[r, g] = 0; z[r, g, row] = 255 * rng.integers(0, 2, S); z[r, g, row, 0] = 255; z[r, g, row, S - 1] = 0
                e[r, g, :, 0] = 0; e[r, g, :, 1:3] = 2 + 4 * rng.integers(0, W // 4, (S, 2)); e[r, g, :, K - 1] = W - 1
            elif (r == N - 1 and g == 7) or (r == N - 2 and g == 6):
                w[r, g] = 255; z[r, g, :, 1] = 255; z[r, g, :, S - 1] = 255; z[r, g, :, 3] = 0
            else:
                w[r, g, 13:15] = 1; w[r, g, 15] = 255
                for j in (1, S - 1):
                    z[r, g, :, j] = 0; z[r, g, 13:, j] = 255; e[r, g, j, 0] = W - 1; e[r, g, j, K - 1] = W - 1
    z[0, 7, :, S - 1] = 255
    return pack(d, e, z, w)
def setup_inputs_full(rng):
    d, e, z, w = parts(rng); i = np.arange(S); kk = np.arange(K); quiet = int(rng.integers(0, N)); turn = int(rng.integers(0, 8))
    for r in range(N):
        for g in range(8):
            kind = (5, 1, 5, 3)[g % 4] if r == quiet else (g + 3 * r + turn) % 8
            if kind == 1:
                o = np.argsort(np.argsort(rng.random((16, S)), axis=0), axis=0)
                z[r, g] = np.where(o < rng.integers(9, 17, S), 255, z[r, g])
            elif kind == 2:
                stage(rng, d, w, r, g)
                few = np.argsort(np.argsort(rng.random((16, 64)), axis=0), axis=0) < np.where(np.arange(64) % 4 == 1, 0, 7)
                d[r, g, :, 16:80] = few * rng.integers(1, 256, (16, 64))
                goal = rng.integers(4, K, S)[:, None]
                v = np.where(kk < goal, rng.integers(16, 80, (S, K)), np.where(kk == goal, W - 1, e[r, g])); v[:, 0] = 0
                m = i % 8 != 5
                e[r, g] = np.where(m[:, None], v, e[r, g]); z[r, g] = np.where(m, 0, z[r, g])
            elif kind == 3 or kind == 6:
                d[r, g] = rng.integers(160, 256, (16, W)); z[r, g] = rng.integers(100, 160, (16, S))
                if kind == 6: d[r, g] = np.where(rng.random(W) < 0.04, rng.integers(0, 100, (16, W)), d[r, g])
            elif kind == 4:
                w[r, g] = 255; half = (rng.permutation(16) < 8)[:, None]
                low = half ^ (rng.random(S) < 0.5)
                z[r, g] = np.where(low, rng.integers(0, 5, (16, S)), rng.integers(251, 256, (16, S)))
                t = rng.random(W); top = np.where(t < 0.3, half, np.where(t < 0.6, ~half, t < 0.85))
                v = np.where(top, rng.integers(251, 256, (16, W)), rng.integers(0, 5, (16, W)))
                d[r, g] = np.where((t >= 0.6) & (t < 0.85), 255, v)
            elif kind == 5:
                e[r, g] = e[r, g, :, :1]
            elif kind == 7:
                w[r, g] = 255; z[r, g] = rng.integers(244, 255, (16, S))
                o = np.argsort(np.argsort(rng.random((16, W)), axis=0), axis=0)
                d[r, g] = np.where((o < rng.integers(8, 17, W)) & (rng.random(W) < 0.6), 255, d[r, g])
    return pack(d, e, z, w)
def setup_inputs_spread(rng):
    d = (np.exp2(8 * rng.random((N, 8, 1, W))) * rng.random((N, 8, 16, W))).astype(np.int64)
    z = (np.exp2(8 * rng.random((N, 8, 1, S))) * rng.random((N, 8, 16, S))).astype(np.int64)
    e = np.minimum((np.exp2((W.bit_length() - 1) * rng.random((N, 8, S, K))) * rng.random((N, 8, S, K))).astype(np.int64), W - 1)
    e = np.where(rng.random((N, 8, S, 1)) < 0.5, W - 1 - e, e)
    w = np.minimum(1 + (np.exp2(8 * rng.random((N, 8, 16))) * rng.random((N, 8, 16))).astype(np.int64), 255)
    return pack(np.minimum(d, 255), e, np.minimum(z, 255), w)
def setup_inputs_ties(rng):
    d, e, z, w = parts(rng)
    d = rng.choice(np.array([0, 0, 100, 252]), (N, 8, 1, W)) + rng.integers(0, 4, d.shape)
    z = rng.choice(np.array([0, 100, 100, 252]), (N, 8, 1, S)) + rng.integers(0, 4, z.shape)
    e[:, :, ::4] = e[:, :, ::4, :1]; e[:, :, 1::4] = rng.choice(np.array([0, 1, W - 2, W - 1]), e[:, :, 1::4].shape)
    e[:, :, 2::4, K // 2:] = e[:, :, 2::4, :K // 2]
    return pack(d, e, z, w)
def check_inputs(d):
    bad = []
    for k, lo, hi in (("dv", 0, 255), ("ef", 0, W - 1), ("zv", 0, 255), ("wt", 1, 255)):
        x = np.asarray(d[k]).astype(np.float32)
        if not np.all((x >= lo) & (x <= hi) & (x == np.floor(x))): bad.append("range of " + k)
    return bad
def reference(dv, ef, zv, wt):
    g2 = np.arange(8)[:, None]; g3 = g2[:, :, None]; kk = np.arange(K - 1)
    D = [np.ascontiguousarray(a.astype(np.float32).astype(np.int32).reshape(8, 16, W).transpose(0, 2, 1)) for a in dv]
    E = [gentries(a).astype(np.int32).reshape(8, S, K) for a in ef]
    z = [np.ascontiguousarray(a.astype(np.float32).astype(np.int32).reshape(8, 16, S).transpose(0, 2, 1)) for a in zv]
    w = wt.astype(np.int32).reshape(N, 8, 1, 1, 16)
    A = [0] * N
    for t in range(RO):
        name = []
        for r in range(N):
            least = 8 + (A[r] & 1); e = E[r]; x = z[r][:, :, None, :]
            n = H(e, U(x, w[r]))
            d = D[r][g3, n]
            a = applies(d, x, least)
            zk = np.where(a[..., None], np.abs(x - d), x); z0 = zk[:, :, :1]
            b = applies(D[r][g3, H(e[:, :, :1], U(zk, w[r]))], zk, least)
            c = applies(D[r][g3, H(e, U(z0, w[r]))], z0, least)
            ok = (b != a[:, :, :1]) & (c == a); ok[:, :, 0] = False
            s = np.argmax(ok, axis=2)
            name.append(np.take_along_axis(n, s[:, :, None], 2)[:, :, 0])
            z[r] = np.take_along_axis(zk, s[:, :, None, None], 2)[:, :, 0]
            E[r] = np.concatenate([np.take_along_axis(e, kk + (kk >= s[:, :, None]), 2), np.zeros((8, S, 1), np.int32)], axis=2)
            A[r] = int(np.count_nonzero(s))
        for r in range(N):
            q = (r - 1 - t % (N - 1)) % N
            E[r][:, :, K - 1] = name[q]
            col = C * np.arange(S) + (name[q] & (C - 1))
            D[r][g2, col] = (D[r][g2, col] + z[q]) >> 1
    return {"yd": np.stack([a.transpose(0, 2, 1).reshape(128, W) for a in D]).astype(np.float32).astype(BF),
            "ye": np.stack([gtable(a.reshape(8, -1)) for a in E]).astype(np.float32),
            "yz": np.stack([a.transpose(0, 2, 1).reshape(128, S) for a in z]).astype(np.float32).astype(BF)}

@@ -1,0 +1,667 @@
+import numpy as np
+from concourse.mybir import dt, AluOpType, AxisListType, ActivationFunctionType
+
+RO = 6
+BIG = 2.0 ** 18
+A_S = ((12, 14), (14, 16))
+A_V = ((0, 1), (1, 3), (3, 5), (5, 7), (7, 9), (9, 11), (11, 12))
+M_S = ()
+A_C = ((1, 9, 0), (9, 16, 0))
+C_C = ((1, 9, 1), (9, 16, 1))
+C_H = ((1, 5), (5, 16))
+B_H = ((1, 9), (9, 16))
+B_C = ((1, 9, 0), (9, 16, 0))
+
+SCRATCH = {
+    "XI": ("sbuf", [128, 8, 32], "int32"), "XJ": ("sbuf", [128, 8, 32], "int32"),
+    "YI": ("sbuf", [128, 8, 32], "float32"), "YJ": ("sbuf", [128, 8, 32], "float32"),
+    "XF": ("sbuf", [128, 256], "float32"), "RT": ("sbuf", [128, 256], "float32"),
+    "wti": ("sbuf", [128, 1], "int32"), "wtf": ("sbuf", [128, 1], "float32"),
+    "DD": ("sbuf", [128, 4096], "bfloat16"),
+    "AB0": ("sbuf", [128, 5120], "bfloat16"), "AB1": ("sbuf", [128, 5120], "bfloat16"),
+    "df0": ("sbuf", [128, 4096], "bfloat16"), "df1": ("sbuf", [128, 4096], "bfloat16"),
+    "ma": ("sbuf", [128, 4096], "bfloat16"), "mb": ("sbuf", [128, 4096], "bfloat16"), "mc": ("sbuf", [128, 4096], "bfloat16"),
+    "dg": ("sbuf", [128, 4096], "bfloat16"), "dc": ("sbuf", [128, 4096], "bfloat16"),
+    "db": ("sbuf", [128, 4096], "bfloat16"),
+    "OV": ("sbuf", [128, 2048], "bfloat16"), "OS": ("sbuf", [128, 2048], "bfloat16"), "WW": ("sbuf", [128, 2048], "bfloat16"),
+    "on8": ("sbuf", [128, 8], "float32"), "b8a": ("sbuf", [128, 8], "float32"), "b8": ("sbuf", [128, 8], "float32"),
+    "wb8": ("sbuf", [128, 8], "float32"), "on16": ("sbuf", [128, 16], "float32"),
+    "one": ("sbuf", [128, 256], "bfloat16"), "ID": ("sbuf", [128, 128], "bfloat16"), "nID": ("sbuf", [128, 128], "bfloat16"),
+    "I22": ("sbuf", [128, 128], "bfloat16"), "IP": ("sbuf", [128, 128], "bfloat16"), "IN": ("sbuf", [128, 128], "bfloat16"),
+    "NBV": ("sbuf", [128, 128], "bfloat16"), "NBS": ("sbuf", [128, 128], "bfloat16"),
+    "KC": ("sbuf", [128, 256], "bfloat16"), "KI": ("sbuf", [128, 256], "float32"),
+    "sl": ("sbuf", [128, 16], "int32"), "sl16": ("sbuf", [128, 16], "int32"), "it0": ("sbuf", [128, 16], "int32"),
+    "it1": ("sbuf", [128, 16], "int32"), "it2": ("sbuf", [128, 16], "int32"),
+    "EB0": ("sbuf", [128, 272], "float32"), "EB1": ("sbuf", [128, 272], "float32"),
+    "y1": ("sbuf", [128, 256], "float32"),
+    "ui": ("sbuf", [128, 64], "int32"), "va": ("sbuf", [128, 64], "int32"), "vx": ("sbuf", [128, 64], "float32"),
+    "x1": ("sbuf", [128, 256], "float32"), "x2": ("sbuf", [128, 256], "int32"), "nn": ("sbuf", [128, 256], "int32"),
+    "nu": ("sbuf", [128, 256], "uint16"),
+    "uic": ("sbuf", [128, 16], "int32"), "vac": ("sbuf", [128, 16], "int32"), "vxc": ("sbuf", [128, 64], "float32"),
+    "x1c": ("sbuf", [128, 256], "float32"), "x2c": ("sbuf", [128, 256], "int32"), "nc": ("sbuf", [128, 256], "int32"),
+    "ncu": ("sbuf", [128, 256], "uint16"),
+    "uib": ("sbuf", [128, 256], "int32"), "vab": ("sbuf", [128, 256], "int32"), "vxb": ("sbuf", [128, 256], "float32"),
+    "x1b": ("sbuf", [128, 256], "float32"), "x2b": ("sbuf", [128, 256], "int32"), "nb": ("sbuf", [128, 256], "int32"),
+    "nbu": ("sbuf", [128, 256], "uint16"),
+    "na0": ("sbuf", [128, 16], "bfloat16"), "nax": ("sbuf", [128, 256], "bfloat16"), "s0": ("sbuf", [128, 256], "bfloat16"),
+    "q0": ("sbuf", [128, 256], "float32"), "q1": ("sbuf", [128, 256], "float32"), "q2": ("sbuf", [128, 256], "float32"),
+    "c0": ("sbuf", [128, 16], "float32"), "c1": ("sbuf", [128, 16], "float32"),
+    "cd": ("sbuf", [128, 256], "float32"), "tr": ("sbuf", [128, 128], "float32"),
+    "t64": ("sbuf", [128, 64], "float32"), "t32": ("sbuf", [128, 32], "float32"), "ci": ("sbuf", [128, 16], "int32"),
+    "m1": ("sbuf", [128, 16], "int32"), "m2": ("sbuf", [128, 16], "int32"), "mu": ("sbuf", [128, 16], "uint16"),
+    "g0": ("sbuf", [128, 16], "bfloat16"), "gj": ("sbuf", [128, 16], "float32"), "ac": ("sbuf", [128, 1], "float32"),
+    "ai": ("sbuf", [128, 1], "int32"), "ap1": ("sbuf", [128, 1], "int32"), "tb": ("sbuf", [128, 1], "float32"),
+    "tb2": ("sbuf", [128, 1], "float32"),
+    "kp": ("sbuf", [128, 16], "int32"), "lt": ("sbuf", [128, 16], "float32"), "th": ("sbuf", [128, 64], "bfloat16"),
+    "k1": ("sbuf", [128, 16], "int32"), "k2": ("sbuf", [128, 16], "int32"), "cu": ("sbuf", [128, 16], "uint16"),
+    "ds": ("sbuf", [128, 256], "int32"), "dh": ("sbuf", [128, 256], "int32"),
+    "pE": ("psum", [128, 512], "float32"), "pF": ("psum", [128, 512], "float32"), "pA": ("psum", [128, 512], "float32"),
+    "pU": ("psum", [128, 512], "float32"), "pB": ("psum", [128, 512], "float32"), "pC": ("psum", [128, 512], "float32"),
+    "pG": ("psum", [128, 512], "float32"), "pH": ("psum", [128, 512], "float32"),
+}
+for _t in range(RO):
+    SCRATCH["zl%d" % _t] = ("sbuf", [128, 256], "bfloat16")
+    SCRATCH["nl%d" % _t] = ("sbuf", [128, 16], "int32")
+    SCRATCH["ns%d" % _t] = ("sbuf", [128, 16], "int32")
+PSUM = ("pE", "pF", "pA", "pU", "pB", "pC", "pG", "pH")
+SEMAPHORES = ["qv", "qs", "qt", "qg"]
+for _t in range(RO):
+    SEMAPHORES += ["an%d" % _t, "az%d" % _t, "ln%d" % _t, "lz%d" % _t]
+SEMAPHORES += ["dm%d" % _i for _i in range(40)]
+
+BONUS = {"ca": -8000, "m0": 12000, "de": -8000, "b": -8000, "hc": 12000, "am": 2000, "hs": 2000, "a0": 8000, "hb": 0, "qu": 16000,
+         "nm": 8000, "up": 4000, "q0": 12000, "as": 2000, "tl": -2000, "h2": 2000}
+CY = 0.83 * 1.25
+GA = 1.56
+CT = 0.42 * 1.2
+WAKE = 60.0
+NET_N, NET_Z = 2200.0, 2600.0
+
+
+def build(T, core, topo):
+    A = AluOpType
+    F = ActivationFunctionType
+    rank = T.rank_of(core)
+    ops = []
+    ndma = [0]
+    cls = ["-"]
+
+    def ap(r):
+        if len(r) == 4:
+            return T[r[0]][:, r[1]:r[2]:r[3]]
+        return T[r[0]][:, r[1]:r[2]]
+
+    def add(q, fn, rd, wr, cost, kind="c", lat=0.0, sem=None, after=None):
+        ops.append({"q": q, "fn": fn, "rd": [r[:3] for r in rd], "wr": [r[:3] for r in wr], "cost": cost, "kind": kind,
+                    "lat": lat, "sem": sem, "after": after, "cls": cls[0]})
+        return len(ops) - 1
+
+    def width(r):
+        return len(range(*r[1:])) if len(r) == 4 else r[2] - r[1]
+
+    def two(*rs):
+        return all(r[0] not in PSUM and SCRATCH[r[0]][2] in ("bfloat16", "uint16") for r in rs)
+
+    def cost1(n, fast):
+        return 55 + CY * max(64, n * (0.5 if fast else 1.0))
+
+    def tt(o, a, b, op):
+        f = 1 if (a[0] in PSUM or b[0] in PSUM) else 2
+        add("v", lambda e: e.tensor_tensor(ap(o), ap(a), ap(b), op), [a, b], [o], 55 + CY * max(64, f * width(o)))
+
+    def ts(o, a, s1, op0, s2=None, op1=None):
+        rd = [a]
+        v1 = s1
+        if isinstance(s1, tuple):
+            rd.append(s1)
+        if op1 is None:
+            add("v", lambda e: e.tensor_scalar(ap(o), ap(a), ap(s1) if isinstance(s1, tuple) else s1, None, op0), rd, [o],
+                cost1(width(o), two(o, a)))
+        else:
+            add("v", lambda e: e.tensor_scalar(ap(o), ap(a), ap(s1) if isinstance(s1, tuple) else s1, s2, op0, op1), rd, [o],
+                cost1(width(o), two(o, a)))
+
+    def cp(o, a):
+        add("v", lambda e: e.tensor_copy(ap(o), ap(a)), [a], [o], cost1(width(o), two(o, a)))
+
+    def fill(o, c):
+        add("v", lambda e: e.memset(ap(o), c), [], [o], cost1(width(o), two(o)))
+
+    def gtt(o, win, off, b, op):
+        add("v", lambda e: e.tensor_tensor(ap(o), ap(win).indirect(ap(off)), ap(b), op), [win, off, b], [o],
+            50 + CY * GA * width(o))
+
+    def gcp(o, win, off):
+        add("v", lambda e: e.tensor_copy(ap(o), ap(win).indirect(ap(off))), [win, off], [o], 50 + CY * GA * width(o))
+
+    def scat(win, off, a):
+        add("v", lambda e: e.tensor_copy(ap(win).indirect(ap(off)), ap(a)), [off, a], [win], 50 + CY * 3.5 * width(a))
+
+    def act(o, a, func, bias=None, scale=None, acc=None):
+        kw = {}
+        rd = [a]
+        if bias is not None:
+            kw["bias"] = bias
+        sc = isinstance(scale, tuple)
+        if sc:
+            rd.append(scale)
+
+        def fn(e):
+            k = dict(kw)
+            if scale is not None:
+                k["scale"] = ap(scale) if sc else scale
+            if acc is not None:
+                k["accum_out"] = ap(acc)
+            return e.activation(ap(o), ap(a), func, **k)
+        add("s", fn, rd, [o] + ([acc] if acc is not None else []), 80 + CY * max(64, width(o)))
+
+    def gact(o, win, off):
+        add("s", lambda e: e.activation(ap(o), ap(win).indirect(ap(off)), F.Copy), [win, off], [o], 65 + CY * GA * width(o))
+
+    def mms(lst):
+        def fn(e):
+            r = None
+            for o, l, x, st, sp in lst:
+                r = e.matmul(ap(o), ap(l), ap(x), st, sp)
+            return r
+        wr = {}
+        for o, l, x, st, sp in lst:
+            lo, hi = wr.get(o[0], (o[1], o[2]))
+            wr[o[0]] = (min(lo, o[1]), max(hi, o[2]))
+        rd = {}
+        for o, l, x, st, sp in lst:
+            for y in (l, x):
+                lo, hi = rd.get(y[0], (y[1], y[2]))
+                rd[y[0]] = (min(lo, y[1]), max(hi, y[2]))
+        add("t", fn, [(k, v[0], v[1]) for k, v in rd.items()], [(k, v[0], v[1]) for k, v in wr.items()],
+            60 + CT * sum(max(64, width(x)) for o, l, x, st, sp in lst))
+
+    def sums(o, mat, buf, lo, hi, extra=()):
+        lst = [(o, (mat, 128 * p, 128 * p + 128), (buf, lo + p, hi, 16)) for p in range(16)] + [(o, l, x) for l, x in extra]
+        mms([(a, b, c, i == 0, i == len(lst) - 1) for i, (a, b, c) in enumerate(lst)])
+
+    def gop(fn, rd, wr, cost):
+        add("g", fn, rd, wr, cost)
+
+    def dma(q, out_fn, in_fn, rd, wr, lat):
+        s = "dm%d" % ndma[0]
+        ndma[0] += 1
+        return add(q, lambda e: e.dma_start(out_fn(), in_fn()), rd, wr, 70.0, kind="dma", lat=lat, sem=s)
+
+    def send(t, what, src, dstname, dst, cost, lat):
+        rid, pid, _e = topo.addr(dst)
+        m = topo.mask(core, dst)
+        i = add("g", lambda e: e.remote_dma(T[dstname][:, 0:SCRATCH[dstname][1][1]], ap(src), T.sem["a%s%d" % (what, t)],
+                                            T.sem["l%s%d" % (what, t)], pid, rid, m), [src], [], cost, kind="send", lat=lat,
+                sem="l%s%d" % (what, t))
+        return i
+
+    def arrive(t, what, dstname, after, lat):
+        add("n%d%s" % (t, what), None, [], [(dstname, 0, SCRATCH[dstname][1][1])], lat, kind="arr", sem="a%s%d" % (what, t),
+            after=after)
+
+    IDr = ("ID", 0, 128)
+
+    dma("y", lambda: T.wti[:, 0:1], lambda: T.wt[:, 0:1], [], [("wti", 0, 1)], 1900)
+    dma("y", lambda: T.XI[:], lambda: T.ef[:], [], [("XI", 0, 256)], 2000)
+    dma("y", lambda: T.AB0[:, 768:1024], lambda: T.zv[:], [], [("AB0", 768, 1024)], 2000)
+    dma("s", lambda: T.XJ[:], lambda: T.ef[:], [], [("XJ", 0, 256)], 2000)
+    dma("s", lambda: T.DD[:], lambda: T.dv[:], [], [("DD", 0, 4096)], 5000)
+
+    def swap(q, dst, src, gi, h, dd):
+        o = gi ^ 1
+        dma(q, lambda: T[dst][16 * gi:16 * gi + 16, :, 16 * (1 - h):16 * (1 - h) + 16],
+            lambda: T[src][16 * o:16 * o + 16, :, 16 * h:16 * h + 16], [(src, 0, 256)], [(dst, 32 * gi + 1000, 32 * gi + 1032)], 1900)
+    ops[3]["wr"].append(("XJ", 1000, 1256))
+    for gi in range(8):
+        swap("y" if gi % 2 else "s", "XJ", "XI", gi, gi % 2, None)
+
+    fill(("on8", 0, 8), 1.0)
+    fill(("one", 0, 256), 1.0)
+    gop(lambda e: e.affine_select(T.b8a[:, 0:8], T.on8[:, 0:8], [[-16, 8]], A.is_ge, 0.0, 0, 1), [("on8", 0, 8)], [("b8a", 0, 8)], 190)
+    gop(lambda e: e.affine_select(T.b8[:, 0:8], T.b8a[:, 0:8], [[16, 8]], A.is_ge, 0.0, 15, -1), [("b8a", 0, 8)], [("b8", 0, 8)], 190)
+    gop(lambda e: e.affine_select(T.ID[:, 0:128], T.one[:, 0:128], [[-1, 128]], A.is_equal, 0.0, 0, 1), [("one", 0, 128)], [IDr], 400)
+    gop(lambda e: e.iota(T.KI[:, 0:256], [[1, 16], [0, 16]], 4, 0, allow_small_or_imprecise_dtypes=True), [], [("KI", 0, 256)], 600)
+    gop(lambda e: e.iota(T.it0[:, 0:16], [[0, 16]], 0, 1), [], [("it0", 0, 16)], 180)
+    gop(lambda e: e.iota(T.it1[:, 0:16], [[16, 16]], 0, 0), [], [("it1", 0, 16)], 180)
+    fill(("WW", 0, 2048), 0.0)
+    fill(("OV", 0, 2048), 0.0)
+    fill(("on16", 0, 16), 1.0)
+    cp(("wtf", 0, 1), ("wti", 0, 1))
+    ts(("wb8", 0, 8), ("b8", 0, 8), ("wtf", 0, 1), A.mult)
+    for j in range(8):
+        act(("WW", 16 * j, 16 * j + 1936, 129), ("on16", 0, 16), F.Copy, scale=("wb8", j, j + 1))
+        ops[-1]["wr"] = [("WW", 3000 + j, 3001 + j)]
+        ops[-1]["rd"] += [("WW", 0, 2048)]
+        ts(("OV", 16 * j, 16 * j + 1936, 129), ("on16", 0, 16), ("b8", j, j + 1), A.mult, BIG, A.mult)
+        ops[-1]["wr"] = [("OV", 3000 + j, 3001 + j)]
+        ops[-1]["rd"] += [("OV", 0, 2048)]
+    act(("OS", 0, 2048), ("OV", 0, 2048), F.Copy, scale=0.5)
+    ops[-1]["rd"] += [("OV", 3000, 3008)]
+    ts(("nID", 0, 128), IDr, -1.0, A.mult)
+    ts(("I22", 0, 128), IDr, 2.0 ** 22, A.mult)
+    ts(("IP", 0, 128), IDr, 2.0 ** 14, A.mult)
+    ts(("IN", 0, 128), IDr, -2.0 ** 14, A.mult)
+    ts(("pC", 256, 512), ("KI", 0, 256), 4096.0, A.mult)
+    fill(("pC", 256, 272), 3 * 4096.0)
+    ts(("KC", 0, 256), ("KI", 0, 256), -0.5, A.add)
+    fill(("KC", 0, 16), 23.5)
+    ts(("it2", 0, 16), ("it0", 0, 16), 15, A.bitwise_and)
+    tt(("sl", 0, 16), ("it2", 0, 16), ("it1", 0, 16), A.add)
+    ts(("sl16", 0, 16), ("sl", 0, 16), 16, A.mult)
+    fill(("tb", 0, 1), -7.5 * BIG)
+
+    def bias_mats():
+        act(("tb2", 0, 1), ("tb", 0, 1), F.Identity, bias=8.0 * BIG)
+        act(("NBV", 0, 128), IDr, F.Copy, scale=("tb", 0, 1))
+        act(("NBS", 0, 128), IDr, F.Copy, scale=("tb2", 0, 1))
+    bias_mats()
+    for b in range(8):
+        add("v", (lambda b: lambda e: e.tensor_scalar(T.XF[:, 32 * b:32 * b + 32], T.XJ[:, b], 1184.0, None, A.add))(b),
+            [("XJ", 0, 256), ("XJ", 1000, 1256)], [("XF", 32 * b, 32 * b + 32)], cost1(32, False))
+    add("v", lambda e: e.transpose(T.RT[:, 0:256], T.XF[:, 0:256]), [("XF", 0, 256)], [("RT", 0, 256)], cost1(256, False))
+
+    def blk(k):
+        return 0 if k == 0 else 16 - k
+    for k in range(16):
+        b = blk(k)
+        o, a = ("EB0", 16 + 16 * b, 32 + 16 * b), ("RT", k, 256, 16)
+        if k % 2:
+            act(o, a, F.Copy)
+        else:
+            cp(o, a)
+    act(("EB0", 0, 16), ("RT", 1, 256, 16), F.Copy)
+
+    def wrefs(mat):
+        ops[-1]["rd"].append((mat, 3000, 3008))
+    C2 = -6722560.0
+
+    def effects(eb):
+        act(("pE", 0, 256), (eb, 16, 272), F.Copy)
+        act(("pF", 0, 256), (eb, 16, 272), F.Identity, bias=C2, scale=2080.0)
+
+    def first_effect(eb):
+        act(("pE", 272, 288), (eb, 16, 32), F.Copy)
+        act(("pE", 288, 304), (eb, 16, 32), F.Copy)
+        act(("pE", 304, 336), ("pE", 272, 304), F.Copy)
+        act(("pE", 336, 400), ("pE", 272, 336), F.Copy)
+        act(("pE", 400, 512), ("pE", 272, 384), F.Copy)
+        act(("pF", 272, 512), ("pE", 272, 512), F.Identity, bias=C2, scale=2080.0)
+
+    for t in range(RO):
+        AB, AN = "AB%d" % (t % 2), "AB%d" % ((t + 1) % 2)
+        EB, EN = "EB%d" % (t % 2), "EB%d" % ((t + 1) % 2)
+        DF = "df%d" % (t % 2)
+        D = ("DD", 0, 4096)
+        cls[0] = "hs"
+        act((AB, 512, 768), (AB, 768, 1024), F.Copy)
+        act((AB, 0, 512), (AB, 512, 1024), F.Copy)
+        sums(("pU", 256, 320), "WW", AB, 0, 1024)
+        wrefs("WW")
+        cp(("ui", 0, 64), ("pU", 256, 320))
+        ts(("va", 0, 64), ("ui", 0, 64), 4095, A.bitwise_and)
+        ts(("vx", 0, 64), ("va", 0, 64), -2048.0, A.add)
+        if t > 0:
+            nl = ("nl%d" % (t - 1), 0, 16)
+            ts((EB, 32, 48), nl, 1184.0, A.add)
+            ts(("k1", 0, 16), nl, 15, A.bitwise_and)
+            tt(("k2", 0, 16), ("k1", 0, 16), ("sl16", 0, 16), A.add)
+            cp(("cu", 0, 16), ("k2", 0, 16))
+        cls[0] = "ef"
+        effects(EB)
+        first_effect(EB)
+        cls[0] = "hs"
+        for j in range(4):
+            tt(("x1", 64 * j, 64 * j + 64), ("pE", 64 * j, 64 * j + 64), ("vx", 0, 64), A.mult)
+        tt(("x2", 0, 256), ("pF", 0, 256), ("x1", 0, 256), A.add)
+        ts(("nn", 0, 256), ("x2", 0, 256), 5, A.arith_shift_right, 4095, A.bitwise_and)
+        cp(("nu", 0, 256), ("nn", 0, 256))
+        cls[0] = "q0"
+        tt(("q0", 0, 256), ("pC", 256, 512), ("nn", 0, 256), A.add)
+        cls[0] = "up"
+        if t > 0:
+            gtt(("ds", 0, 256), D, ("cu", 0, 16), ("zl%d" % (t - 1), 0, 256), A.add)
+            ts(("dh", 0, 256), ("ds", 0, 256), 1, A.arith_shift_right)
+            scat(D, ("cu", 0, 16), ("dh", 0, 256))
+
+        def gather_a(lo, hi):
+            gtt((DF, 256 * lo, 256 * hi), D, ("nu", 16 * lo, 16 * hi), (AB, 1024 - 256 * (hi - lo), 1024), A.subtract)
+
+        def absd(lo, hi):
+            act((AB, 1024 + 256 * lo, 1024 + 256 * hi), (DF, 256 * lo, 256 * hi), F.Abs)
+
+        def mask_a(lo, hi):
+            if lo in M_S:
+                act(("ma", 256 * lo, 256 * hi), (DF, 256 * lo, 256 * hi), F.Sign, bias=-0.5)
+            else:
+                ts(("ma", 256 * lo, 256 * hi), (DF, 256 * lo, 256 * hi), 0.0, A.is_gt)
+
+        def count(bank, buf, lo, hi, sgn, extra=()):
+            if sgn:
+                sums((bank, 16 * lo, 16 * hi), "OS", buf, 256 * lo, 256 * hi, [(("NBS", 0, 128), ("one", 0, 16 * (hi - lo)))] + list(extra))
+            else:
+                sums((bank, 16 * lo, 16 * hi), "OV", buf, 256 * lo, 256 * hi, [(("NBV", 0, 128), ("one", 0, 16 * (hi - lo)))] + list(extra))
+                wrefs("OV")
+
+        def sums_u(lo, hi):
+            sums(("pU", 16 * lo, 16 * hi), "WW", AB, 1024 + 256 * lo, 1024 + 256 * hi)
+            wrefs("WW")
+        cls[0] = "a0"
+        gather_a(0, 1)
+        absd(0, 1)
+        sums_u(0, 1)
+        cls[0] = "m0"
+        mask_a(0, 1)
+        count("pA", "ma", 0, 1, 0 in M_S)
+        cls[0] = "hc"
+        cp(("uic", 0, 16), ("pU", 0, 16))
+        ts(("vac", 0, 16), ("uic", 0, 16), 4095, A.bitwise_and)
+        ts(("vxc", 0, 16), ("vac", 0, 16), -2048.0, A.add)
+        cp(("vxc", 16, 32), ("vxc", 0, 16))
+        cp(("vxc", 32, 64), ("vxc", 0, 32))
+        for c, d in C_H:
+            for lo in range(c, d, 4):
+                hi = min(lo + 4, d)
+                tt(("x1c", 16 * lo, 16 * hi), ("pE", 16 * lo, 16 * hi), ("vxc", 0, 16 * (hi - lo)), A.mult)
+            c, d = 16 * c, 16 * d
+            tt(("x2c", c, d), ("pF", c, d), ("x1c", c, d), A.add)
+            ts(("nc", c, d), ("x2c", c, d), 5, A.arith_shift_right, 4095, A.bitwise_and)
+            cp(("ncu", c, d), ("nc", c, d))
+            cls[0] = "h2"
+        cls[0] = "m0"
+        ts(("na0", 0, 16), ("pA", 0, 16), 0.0, A.is_lt)
+        mms([(("pA", 256 + 16 * b, 272 + 16 * b), IDr, ("na0", 0, 16), True, True) for b in range(1, 16)])
+        act(("nax", 16, 256), ("pA", 272, 512), F.Copy)
+        act(("s0", 16, 256), ("nax", 16, 256), F.Identity, bias=-1.0, scale=2.0)
+        ts(("c0", 0, 16), ("na0", 0, 16), -4096.0, A.mult, 4096.0, A.add)
+        tt(("c1", 0, 16), ("c0", 0, 16), ("q0", 0, 16), A.add)
+        nslot = [0]
+
+        def apart(buf, off, lo, hi, other):
+            bank = ("pG", "pH")[nslot[0] % 2]
+            nslot[0] += 1
+            gact((buf, 256 * lo, 256 * hi), D, (off, 16 * lo, 16 * hi))
+            for i, b in enumerate(range(lo, hi)):
+                mms([((bank, 256 * i, 256 * i + 256), IDr, (buf, 256 * b, 256 * b + 256), True, False),
+                     ((bank, 256 * i, 256 * i + 256), ("nID", 0, 128), other(b), False, True)])
+            return (bank, 0, 256 * (hi - lo))
+        for lo, hi in A_S:
+            cls[0] = "as"
+            p = apart("dg", "nu", lo, hi, lambda b: (AB, 768, 1024))
+            act((AB, 1024 + 256 * lo, 1024 + 256 * hi), p, F.Abs)
+            if lo in M_S:
+                act(("ma", 256 * lo, 256 * hi), p, F.Sign, bias=-0.5)
+            else:
+                ts(("ma", 256 * lo, 256 * hi), p, 0.0, A.is_gt)
+        for lo, hi in A_V[1:]:
+            cls[0] = "av"
+            gather_a(lo, hi)
+            absd(lo, hi)
+            cls[0] = "am"
+            mask_a(lo, hi)
+
+        def hash_b(lo, hi):
+            c = 16 * lo
+            d = 16 * hi
+            sums_u(lo, hi)
+            cp(("uib", c, d), ("pU", c, d))
+            ts(("vab", c, d), ("uib", c, d), 4095, A.bitwise_and)
+            ts(("vxb", c, d), ("vab", c, d), -2048.0, A.add)
+            tt(("x1b", c, d), ("pE", 256 + c, 256 + d), ("vxb", c, d), A.mult)
+            tt(("x2b", c, d), ("pF", 256 + c, 256 + d), ("x1b", c, d), A.add)
+            ts(("nb", c, d), ("x2b", c, d), 5, A.arith_shift_right, 4095, A.bitwise_and)
+            cp(("nbu", c, d), ("nb", c, d))
+        cls[0] = "cs"
+        for lo, hi, sgn in C_C:
+            if sgn:
+                for b in range(lo, hi, 2):
+                    p = apart("dc", "ncu", b, min(b + 2, hi), lambda b: (AB, 1024, 1280))
+                    act(("mc", 256 * b, 256 * min(b + 2, hi)), p, F.Sign, bias=-0.5)
+            else:
+                for b in range(lo, hi):
+                    gtt(("mc", 256 * b, 256 * b + 256), D, ("ncu", 16 * b, 16 * b + 16), (AB, 1024, 1280), A.is_gt)
+            count("pC", "mc", lo, hi, sgn, [(("I22", 0, 128), ("nax", 16 * lo, 16 * hi))])
+        for lo, hi in B_H:
+            cls[0] = "hb"
+            hash_b(lo, hi)
+            cls[0] = "b"
+            for c, d, sgn in B_C:
+                if c < lo or c >= hi:
+                    continue
+                st = 2 if sgn else 4
+                for q in range(c, d, st):
+                    r = min(q + st, d)
+                    if sgn:
+                        p = apart("db", "nbu", q, r, lambda b: (AB, 1024 + 256 * b, 1280 + 256 * b))
+                        act(("mb", 256 * q, 256 * r), p, F.Sign, bias=-0.5)
+                    else:
+                        gtt(("mb", 256 * q, 256 * r), D, ("nbu", 16 * q, 16 * r), (AB, 1024 + 256 * q, 1024 + 256 * r), A.is_gt)
+        cls[0] = "ca"
+        for lo, hi, sgn in A_C:
+            count("pA", "ma", lo, hi, sgn)
+        for lo, hi in B_H:
+            tt(("q1", 16 * lo, 16 * hi), ("pA", 16 * lo, 16 * hi), ("q0", 16 * lo, 16 * hi), A.min)
+        cls[0] = "de"
+        for lo, hi in B_H:
+            c = 16 * lo
+            d = 16 * hi
+            tt(("q2", c, d), ("pC", c, d), ("q1", c, d), A.min)
+        for lo, hi, sgn in B_C:
+            c = 16 * lo
+            d = 16 * hi
+            count("pB", "mb", lo, hi, sgn)
+            z = ("pU", 256 + c, 256 + d)
+            tt(z, ("pB", c, d), ("s0", c, d), A.mult)
+            tt(("cd", c, d) if lo < 9 else z, z, ("q2", c, d), A.min)
+        cls[0] = "tl"
+        tt(("tr", 112, 128), ("c1", 0, 16), ("cd", 128, 144), A.max)
+        tt(("tr", 0, 112), ("pU", 400, 512), ("cd", 16, 128), A.max)
+        tt(("t64", 0, 64), ("tr", 0, 64), ("tr", 64, 128), A.max)
+        tt(("t32", 0, 32), ("t64", 0, 32), ("t64", 32, 64), A.max)
+        tt(("ci", 0, 16), ("t32", 0, 16), ("t32", 16, 32), A.max)
+        ns = "ns%d" % t
+        dst = T.cores[(rank + 1 + t % 3) % len(T.cores)]
+        ts((ns, 0, 16), ("ci", 0, 16), 4095, A.bitwise_and)
+        i = send(t, "n", (ns, 0, 16), "nl%d" % t, dst, 900.0, 1500.0)
+        arrive(t, "n", "nl%d" % t, i, NET_N)
+        ts(("m1", 0, 16), ("ci", 0, 16), 4, A.arith_shift_right, 0x1F00, A.bitwise_and)
+        tt(("m2", 0, 16), ("m1", 0, 16), ("sl", 0, 16), A.add)
+        cp(("mu", 0, 16), ("m2", 0, 16))
+        gcp((AN, 768, 1024), (AB, 0, 5120), ("mu", 0, 16))
+        i = send(t, "z", (AN, 768, 1024), "zl%d" % t, dst, 900.0, 1700.0)
+        arrive(t, "z", "zl%d" % t, i, NET_Z)
+        if t == RO - 1:
+            dma("y", lambda: T.yz[:], lambda: T[AN][:, 768:1024], [(AN, 768, 1024)], [], 2000)
+        cls[0] = "nt"
+        if t < RO - 1:
+            ts(("g0", 0, 16), ("ci", 0, 16), 20480.0, A.is_ge)
+            mms([(("pU", 384, 400), ("one", 0, 128), ("g0", 0, 16), True, True)])
+            act(("gj", 0, 16), ("pU", 384, 400), F.Copy, acc=("ac", 0, 1))
+            cp(("ai", 0, 1), ("ac", 0, 1))
+            ts(("ap1", 0, 1), ("ai", 0, 1), 1, A.bitwise_and)
+            ts(("tb", 0, 1), ("ap1", 0, 1), -BIG, A.mult, -7.5 * BIG, A.add)
+            bias_mats()
+        cls[0] = "qu"
+        ts(("kp", 0, 16), ("ci", 0, 16), 12, A.arith_shift_right)
+        ts(("lt", 0, 16), ("ci", 0, 16), 20480.0, A.is_lt, 32.0, A.mult)
+        tt(("th", 0, 16), ("kp", 0, 16), ("lt", 0, 16), A.max)
+        act(("th", 16, 32), ("th", 0, 16), F.Copy)
+        act(("th", 32, 64), ("th", 0, 32), F.Copy)
+        for off, m, n in ((0, "IP", "IN"), (256, "IN", "IP")):
+            lst = []
+            for b in range(0, 256, 64):
+                o = ("pB", off + b, off + b + 64)
+                lst.append((o, (m, 0, 128), ("KC", b, b + 64), True, False))
+                lst.append((o, (n, 0, 128), ("th", 0, 64), False, True))
+            mms(lst)
+        tt(("y1", 0, 256), ("pB", 0, 256), (EB, 16, 272), A.min)
+        tt(("pB", 256, 512), ("pB", 256, 512), (EB, 0, 256), A.min)
+        tt((EN, 16, 32), ("pB", 256, 272), ("y1", 0, 16), A.max)
+        tt((EN, 48, 272), ("pB", 288, 512), ("y1", 32, 256), A.max)
+        act((EN, 0, 16), (EN, 256, 272), F.Copy)
+
+    cls[0] = "up"
+    nl = ("nl%d" % (RO - 1), 0, 16)
+    EB = "EB%d" % (RO % 2)
+    D = ("DD", 0, 4096)
+    ts(("k1", 0, 16), nl, 15, A.bitwise_and)
+    tt(("k2", 0, 16), ("k1", 0, 16), ("sl16", 0, 16), A.add)
+    cp(("cu", 0, 16), ("k2", 0, 16))
+    ts((EB, 32, 48), nl, 1184.0, A.add)
+    gtt(("ds", 0, 256), D, ("cu", 0, 16), ("zl%d" % (RO - 1), 0, 256), A.add)
+    ts(("dh", 0, 256), ("ds", 0, 256), 1, A.arith_shift_right)
+    scat(D, ("cu", 0, 16), ("dh", 0, 256))
+    dma("s", lambda: T.yd[:], lambda: T.DD[:], [D], [], 5000)
+    for k in range(16):
+        b = blk(k)
+        o, a = ("RT", k, 256, 16), (EB, 16 + 16 * b, 32 + 16 * b)
+        if k % 2:
+            act(o, a, F.Copy)
+        else:
+            cp(o, a)
+        ops[-1]["wr"] = [("RT", 3000 + k, 3001 + k)]
+    add("v", lambda e: e.transpose(T.XF[:, 0:256], T.RT[:, 0:256]), [("RT", 3000, 3016)], [("XF", 0, 256)], cost1(256, False))
+    for b in range(8):
+        add("v", (lambda b: lambda e: e.tensor_scalar(T.YI[:, b], T.XF[:, 32 * b:32 * b + 32], -1184.0, None, A.add))(b),
+            [("XF", 32 * b, 32 * b + 32)], [("YI", 32 * b, 32 * b + 32)], cost1(32, False))
+        add("s", (lambda b: lambda e: e.activation(T.YJ[:, b], T.XF[:, 32 * b:32 * b + 32], F.Identity, bias=-1184.0))(b),
+            [("XF", 32 * b, 32 * b + 32)], [("YJ", 32 * b, 32 * b + 32), ("YJ", 1000 + 32 * b, 1032 + 32 * b)], 80 + CY * 64)
+    for gi in range(8):
+        o = gi ^ 1
+        h = gi % 2
+        dma("y", (lambda gi, o, h: lambda: T.YJ[16 * gi:16 * gi + 16, :, 16 * (1 - h):16 * (1 - h) + 16])(gi, o, h),
+            (lambda gi, o, h: lambda: T.YI[16 * o:16 * o + 16, :, 16 * h:16 * h + 16])(gi, o, h),
+            [("YI", 0, 256), ("YJ", 0, 256)], [("YJ", 2000 + gi, 2001 + gi)], 1900)
+    dma("y", lambda: T.ye[:], lambda: T.YJ[:], [("YJ", 0, 256), ("YJ", 2000, 2008)], [], 2000)
+    return ops
+
+
+def depend(ops):
+    hist = {}
+    deps = []
+    for i, op in enumerate(ops):
+        need = set()
+        for rw, regs in ((0, op["rd"]), (1, op["wr"])):
+            for name, lo, hi in regs:
+                bank = name in PSUM
+                for j, jw, jlo, jhi in hist.get(name, ()):
+                    if ((jw or rw) and jlo < hi and lo < jhi) or (bank and ops[j]["q"] != op["q"]):
+                        need.add(j)
+        for name, lo, hi in op["wr"]:
+            if name not in PSUM:
+                hist[name] = [x for x in hist.get(name, []) if not (lo <= x[2] and x[3] <= hi)]
+        for rw, regs in ((0, op["rd"]), (1, op["wr"])):
+            for name, lo, hi in regs:
+                hist.setdefault(name, []).append((i, rw, lo, hi))
+                if name in PSUM and len(hist[name]) > 160:
+                    hist[name] = hist[name][-160:]
+        need.discard(i)
+        deps.append(sorted(need))
+    return deps
+
+
+def schedule(ops, deps):
+    n = len(ops)
+    succ = [[] for _ in range(n)]
+    alld = []
+    for i in range(n):
+        d = list(deps[i])
+        if ops[i]["after"] is not None:
+            d.append(ops[i]["after"])
+        alld.append(d)
+        for j in d:
+            succ[j].append(i)
+    pri = [0.0] * n
+    for i in range(n - 1, -1, -1):
+        m = 0.0
+        for j in succ[i]:
+            m = max(m, pri[j] + WAKE)
+        pri[i] = m + ops[i]["cost"] + ops[i]["lat"]
+    pri = [pri[i] + BONUS.get(ops[i]["cls"], 0.0) for i in range(n)]
+    left = [len(d) for d in alld]
+    est = [0.0] * n
+    free = {}
+    ready = {}
+    for i in range(n):
+        if left[i] == 0:
+            ready.setdefault(ops[i]["q"], []).append(i)
+    order = []
+    start = [0.0] * n
+    while len(order) < n:
+        best = None
+        for q, lst in ready.items():
+            if not lst:
+                continue
+            f = free.get(q, 0.0)
+            t0 = max(f, min(est[i] for i in lst))
+            c = max((i for i in lst if est[i] <= t0), key=lambda i: pri[i])
+            if best is None or (t0, -pri[c]) < best[0]:
+                best = ((t0, -pri[c]), q, c)
+        (t0, _p), q, c = best
+        ready[q].remove(c)
+        start[c] = t0
+        order.append(c)
+        free[q] = t0 + ops[c]["cost"]
+        for j in succ[c]:
+            e = t0 + ops[c]["cost"] + (0.0 if ops[j]["after"] == c else ops[c]["lat"] + WAKE)
+            est[j] = max(est[j], e)
+            left[j] -= 1
+            if left[j] == 0:
+                ready.setdefault(ops[j]["q"], []).append(j)
+    return order, start, max(start[i] + ops[i]["cost"] + ops[i]["lat"] for i in range(n))
+
+
+def emit(g, T, ops, deps, order):
+    eng = {"v": g.vector, "s": g.scalar, "t": g.tensor, "g": g, "y": g.sync}
+    qsem = {"v": "qv", "s": "qs", "t": "qt", "g": "qg"}
+    count = {}
+    know = {q: {} for q in eng}
+    waited = {}
+    total = {}
+    clock = [None] * len(ops)
+    token = [None] * len(ops)
+    for i in order:
+        op = ops[i]
+        q = op["q"]
+        if op["kind"] == "arr":
+            token[i] = (op["sem"], 16)
+            clock[i] = {op["sem"]: 16}
+            total[op["sem"]] = 16
+            continue
+        K = know[q]
+        ds = sorted(deps[i], key=lambda j: -sum(clock[j].values()))
+        for j in ds:
+            s, v = token[j]
+            if K.get(s, 0) >= v:
+                continue
+            eng[q].wait_ge(T.sem[s], v)
+            waited[s] = max(waited.get(s, 0), v)
+            for a, b in clock[j].items():
+                if K.get(a, 0) < b:
+                    K[a] = b
+        ins = op["fn"](eng[q])
+        if op["kind"] == "c":
+            s = qsem[q]
+            count[s] = count.get(s, 0) + 1
+            ins.then_inc(T.sem[s], 1)
+            token[i] = (s, count[s])
+        else:
+            if op["kind"] == "dma":
+                ins.then_inc(T.sem[op["sem"]], 16)
+            token[i] = (op["sem"], 16)
+        total[token[i][0]] = token[i][1]
+        c = dict(K)
+        c[token[i][0]] = token[i][1]
+        clock[i] = c
+    for s, v in total.items():
+        if waited.get(s, 0) < v:
+            g.wait_ge(T.sem[s], v)
+
+
+def rank_program(g, core, T, topo):
+    if T.rank_of(core) is None:
+        return
+    ops = build(T, core, topo)
+    deps = depend(ops)
+    order, start, span = schedule(ops, deps)
+    emit(g, T, ops, deps, order)

@@ -2,80 +2,90 @@ import numpy as np
 from concourse.mybir import dt, AluOpType, AxisListType, ActivationFunctionType
 
 RO = 6
-BIG = 2.0 ** 18
-A_S = ((12, 14), (14, 16))
-A_V = ((0, 1), (1, 3), (3, 5), (5, 7), (7, 9), (9, 11), (11, 12))
-M_S = ()
-A_C = ((1, 9, 0), (9, 16, 0))
-C_C = ((1, 9, 1), (9, 16, 1))
-C_H = ((1, 5), (5, 16))
-B_H = ((1, 9), (9, 16))
-B_C = ((1, 9, 0), (9, 16, 0))
+W1 = 2.0 ** 23
+UNITS = (256 * W1, 128 * W1, 64 * W1)
+SQ = 2.0 ** 14
+C2 = -6722560.0
+
+
+def magic(step):
+    return 1.5 * 2.0 ** 23 * step
+
+
+A_V = ((1, 5, "v"), (5, 8, "v"))
+A_S = ((8, 12, "s"), (12, 16, "s"))
+C_V = ((1, 5), (5, 6))
+C_S = ((6, 8), (8, 12))
+C_LATE = (8, 12)
+C_LAST = (12, 16)
+B_V = ((1, 5), (5, 8), (8, 12), (12, 16))
+B_H = ((1, 8), (8, 16))
+G_CONV = ()
+BANKS = ("pG", "pH", "pW", "pC", "pG", "pH", "pG", "pH", "pG", "pH")
+PIECES = ((1, 8), (8, 16))
+ORDER = ("abc", "ab")
+COUNTS = {"a": ((1, 8), (8, 16)), "b": ((1, 8), (8, 16)), "c": ((1, 8),)}
+SEQ = {"v": ("tl tl tl tl tn tz tn tz qu qu tz qu qu qu hs hs up hs hy hs up hy up hy a0 av0 av1 m0 am0 hc hy hc am1 hc hc cv0 hb0 cv1 "
+             "hb0 hb0 hb0 b0 b0 hb1 hb1 hb1 hb1 b1 b1 cl v0 v1 v0 ct ct").split(),
+       "s": ("tz qu hs zr li up ly zr nt as0 a0 av0 hc av1 as0 m0 hb0 as1 as0 as1 as1 sg0 sg0 hb1 sg1 cs0 sg1 cs1 cs0 cs1 v0 cs1 "
+             "v1").split(),
+       "t": ("tl qu hs qu hs nt hs up up as0 hc hc hc m0 hb0 as0 hb0 as1 as1 ca0 hb1 hb1 cb0 ca1 cs0 cs1 cc0 cs1 cb1 v0 ct v1").split()}
+TAIL = ("tl", "tz", "tn", "qu", "nt")
 
 SCRATCH = {
-    "XI": ("sbuf", [128, 8, 32], "int32"), "XJ": ("sbuf", [128, 8, 32], "int32"),
-    "YI": ("sbuf", [128, 8, 32], "float32"), "YJ": ("sbuf", [128, 8, 32], "float32"),
-    "XF": ("sbuf", [128, 256], "float32"), "RT": ("sbuf", [128, 256], "float32"),
+    "XJ": ("sbuf", [128, 8, 32], "int32"), "XF": ("sbuf", [128, 8, 32], "float32"), "XE": ("sbuf", [128, 256], "float32"),
     "wti": ("sbuf", [128, 1], "int32"), "wtf": ("sbuf", [128, 1], "float32"),
     "DD": ("sbuf", [128, 4096], "bfloat16"),
     "AB0": ("sbuf", [128, 5120], "bfloat16"), "AB1": ("sbuf", [128, 5120], "bfloat16"),
-    "df0": ("sbuf", [128, 4096], "bfloat16"), "df1": ("sbuf", [128, 4096], "bfloat16"),
+    "ZR": ("sbuf", [128, 1024], "bfloat16"), "df": ("sbuf", [128, 4096], "bfloat16"),
     "ma": ("sbuf", [128, 4096], "bfloat16"), "mb": ("sbuf", [128, 4096], "bfloat16"), "mc": ("sbuf", [128, 4096], "bfloat16"),
     "dg": ("sbuf", [128, 4096], "bfloat16"), "dc": ("sbuf", [128, 4096], "bfloat16"),
-    "db": ("sbuf", [128, 4096], "bfloat16"),
-    "OV": ("sbuf", [128, 2048], "bfloat16"), "OS": ("sbuf", [128, 2048], "bfloat16"), "WW": ("sbuf", [128, 2048], "bfloat16"),
     "on8": ("sbuf", [128, 8], "float32"), "b8a": ("sbuf", [128, 8], "float32"), "b8": ("sbuf", [128, 8], "float32"),
-    "wb8": ("sbuf", [128, 8], "float32"), "on16": ("sbuf", [128, 16], "float32"),
-    "one": ("sbuf", [128, 256], "bfloat16"), "ID": ("sbuf", [128, 128], "bfloat16"), "nID": ("sbuf", [128, 128], "bfloat16"),
-    "I22": ("sbuf", [128, 128], "bfloat16"), "IP": ("sbuf", [128, 128], "bfloat16"), "IN": ("sbuf", [128, 128], "bfloat16"),
-    "NBV": ("sbuf", [128, 128], "bfloat16"), "NBS": ("sbuf", [128, 128], "bfloat16"),
-    "KC": ("sbuf", [128, 256], "bfloat16"), "KI": ("sbuf", [128, 256], "float32"),
-    "sl": ("sbuf", [128, 16], "int32"), "sl16": ("sbuf", [128, 16], "int32"), "it0": ("sbuf", [128, 16], "int32"),
-    "it1": ("sbuf", [128, 16], "int32"), "it2": ("sbuf", [128, 16], "int32"),
-    "EB0": ("sbuf", [128, 272], "float32"), "EB1": ("sbuf", [128, 272], "float32"),
-    "y1": ("sbuf", [128, 256], "float32"),
-    "ui": ("sbuf", [128, 64], "int32"), "va": ("sbuf", [128, 64], "int32"), "vx": ("sbuf", [128, 64], "float32"),
-    "x1": ("sbuf", [128, 256], "float32"), "x2": ("sbuf", [128, 256], "int32"), "nn": ("sbuf", [128, 256], "int32"),
-    "nu": ("sbuf", [128, 256], "uint16"),
-    "uic": ("sbuf", [128, 16], "int32"), "vac": ("sbuf", [128, 16], "int32"), "vxc": ("sbuf", [128, 64], "float32"),
-    "x1c": ("sbuf", [128, 256], "float32"), "x2c": ("sbuf", [128, 256], "int32"), "nc": ("sbuf", [128, 256], "int32"),
-    "ncu": ("sbuf", [128, 256], "uint16"),
-    "uib": ("sbuf", [128, 256], "int32"), "vab": ("sbuf", [128, 256], "int32"), "vxb": ("sbuf", [128, 256], "float32"),
-    "x1b": ("sbuf", [128, 256], "float32"), "x2b": ("sbuf", [128, 256], "int32"), "nb": ("sbuf", [128, 256], "int32"),
-    "nbu": ("sbuf", [128, 256], "uint16"),
-    "na0": ("sbuf", [128, 16], "bfloat16"), "nax": ("sbuf", [128, 256], "bfloat16"), "s0": ("sbuf", [128, 256], "bfloat16"),
-    "q0": ("sbuf", [128, 256], "float32"), "q1": ("sbuf", [128, 256], "float32"), "q2": ("sbuf", [128, 256], "float32"),
-    "c0": ("sbuf", [128, 16], "float32"), "c1": ("sbuf", [128, 16], "float32"),
-    "cd": ("sbuf", [128, 256], "float32"), "tr": ("sbuf", [128, 128], "float32"),
-    "t64": ("sbuf", [128, 64], "float32"), "t32": ("sbuf", [128, 32], "float32"), "ci": ("sbuf", [128, 16], "int32"),
-    "m1": ("sbuf", [128, 16], "int32"), "m2": ("sbuf", [128, 16], "int32"), "mu": ("sbuf", [128, 16], "uint16"),
-    "g0": ("sbuf", [128, 16], "bfloat16"), "gj": ("sbuf", [128, 16], "float32"), "ac": ("sbuf", [128, 1], "float32"),
-    "ai": ("sbuf", [128, 1], "int32"), "ap1": ("sbuf", [128, 1], "int32"), "tb": ("sbuf", [128, 1], "float32"),
-    "tb2": ("sbuf", [128, 1], "float32"),
-    "kp": ("sbuf", [128, 16], "int32"), "lt": ("sbuf", [128, 16], "float32"), "th": ("sbuf", [128, 64], "bfloat16"),
-    "k1": ("sbuf", [128, 16], "int32"), "k2": ("sbuf", [128, 16], "int32"), "cu": ("sbuf", [128, 16], "uint16"),
-    "ds": ("sbuf", [128, 256], "int32"), "dh": ("sbuf", [128, 256], "int32"),
-    "pE": ("psum", [128, 512], "float32"), "pF": ("psum", [128, 512], "float32"), "pA": ("psum", [128, 512], "float32"),
-    "pU": ("psum", [128, 512], "float32"), "pB": ("psum", [128, 512], "float32"), "pC": ("psum", [128, 512], "float32"),
-    "pG": ("psum", [128, 512], "float32"), "pH": ("psum", [128, 512], "float32"),
+    "OB": ("sbuf", [128, 144], "bfloat16"), "UT": ("sbuf", [128, 512], "float32"), "AT": ("sbuf", [128, 256], "bfloat16"),
+    "W16": ("sbuf", [128, 24], "bfloat16"), "O8": ("sbuf", [128, 8], "bfloat16"),
+    "one": ("sbuf", [128, 256], "bfloat16"), "neg": ("sbuf", [128, 128], "bfloat16"),
+    "ID": ("sbuf", [128, 128], "bfloat16"), "nID": ("sbuf", [128, 128], "bfloat16"), "hID": ("sbuf", [128, 128], "bfloat16"),
+    "I32": ("sbuf", [128, 128], "float32"), "nI32": ("sbuf", [128, 128], "float32"),
+    "LV": ("sbuf", [128, 1600], "bfloat16"), "BL": ("sbuf", [128, 128], "bfloat16"), "CB": ("sbuf", [128, 1040], "bfloat16"),
+    "it": ("sbuf", [128, 256], "int32"), "iu": ("sbuf", [128, 256], "int32"), "kf": ("sbuf", [128, 256], "float32"),
+    "SL": ("sbuf", [128, 256], "bfloat16"), "nSL": ("sbuf", [128, 256], "bfloat16"),
+    "QP": ("sbuf", [128, 256], "bfloat16"), "QN": ("sbuf", [128, 256], "bfloat16"), "qc": ("sbuf", [128, 1], "float32"),
+    "HF": ("sbuf", [128, 256], "float32"), "CL": ("sbuf", [128, 128], "bfloat16"), "CR": ("sbuf", [128, 16], "bfloat16"),
+    "pi": ("sbuf", [128, 1], "int32"), "pj": ("sbuf", [128, 1], "int32"), "pf": ("sbuf", [128, 1], "float32"),
+    "ER": ("sbuf", [128, 2, 256], "float32"),
+    "VA": ("sbuf", [128, 256], "bfloat16"), "VC": ("sbuf", [128, 256], "bfloat16"),
+    "xa": ("sbuf", [128, 256], "int32"), "na": ("sbuf", [128, 256], "int32"), "ua": ("sbuf", [128, 256], "uint16"),
+    "xc": ("sbuf", [128, 256], "int32"), "nc": ("sbuf", [128, 256], "int32"), "uc": ("sbuf", [128, 256], "uint16"),
+    "xb": ("sbuf", [128, 256], "int32"), "nb": ("sbuf", [128, 256], "int32"), "ub": ("sbuf", [128, 256], "uint16"),
+    "val": ("sbuf", [128, 256], "float32"), "t1": ("sbuf", [128, 64], "float32"), "t2": ("sbuf", [128, 64], "float32"),
+    "t3": ("sbuf", [128, 64], "float32"), "t4": ("sbuf", [128, 32], "float32"), "ci": ("sbuf", [128, 16], "int32"),
+    "m1": ("sbuf", [128, 16], "int32"), "mu": ("sbuf", [128, 16], "uint16"), "ni": ("sbuf", [128, 16], "int32"),
+    "TH": ("sbuf", [128, 32], "bfloat16"), "TT": ("sbuf", [128, 128], "bfloat16"), "ac": ("sbuf", [128, 1], "float32"),
+    "y1": ("sbuf", [128, 256], "float32"), "cu": ("sbuf", [128, 16], "uint16"), "DG": ("sbuf", [128, 256], "bfloat16"),
+    "dh": ("sbuf", [128, 256], "int32"),
 }
+PSUM = ("pR1", "pR2", "pC", "pW", "pU1", "pU2", "pG", "pH")
+for _p in PSUM:
+    SCRATCH[_p] = ("psum", [128, 512], "float32")
+for _t in range(RO + 1):
+    SCRATCH["EL%d" % _t] = ("sbuf", [128, 2, 256], "float32")
 for _t in range(RO):
-    SCRATCH["zl%d" % _t] = ("sbuf", [128, 256], "bfloat16")
-    SCRATCH["nl%d" % _t] = ("sbuf", [128, 16], "int32")
-    SCRATCH["ns%d" % _t] = ("sbuf", [128, 16], "int32")
-PSUM = ("pE", "pF", "pA", "pU", "pB", "pC", "pG", "pH")
+    SCRATCH["hl%d" % _t] = ("sbuf", [128, 256], "bfloat16")
+    SCRATCH["hs%d" % _t] = ("sbuf", [128, 256], "bfloat16")
+    SCRATCH["ns%d" % _t] = ("sbuf", [128, 16], "float32")
 SEMAPHORES = ["qv", "qs", "qt", "qg"]
 for _t in range(RO):
     SEMAPHORES += ["an%d" % _t, "az%d" % _t, "ln%d" % _t, "lz%d" % _t]
-SEMAPHORES += ["dm%d" % _i for _i in range(40)]
+SEMAPHORES += ["dm%d" % _i for _i in range(24)]
 
-BONUS = {"ca": -8000, "m0": 12000, "de": -8000, "b": -8000, "hc": 12000, "am": 2000, "hs": 2000, "a0": 8000, "hb": 0, "qu": 16000,
-         "nm": 8000, "up": 4000, "q0": 12000, "as": 2000, "tl": -2000, "h2": 2000}
-CY = 0.83 * 1.25
-GA = 1.56
-CT = 0.42 * 1.2
-WAKE = 60.0
-NET_N, NET_Z = 2200.0, 2600.0
+PLAN = {"f": 1.1, "G": 1.56, "SC": 3.8, "wake": 60.0, "issue": 700.0, "net_n": 2000.0, "net_z": 2300.0, "fv": 55.0, "fs": 70.0,
+        "ft": 40.0, "mm": 5.0, "ahead": 300.0}
+
+
+def cost(op, P):
+    fix, cyc, ga, sc, te = op["c"]
+    fix = P.get(fix, fix) + (P["mm"] * len(op["fn"]) if op["q"] == "t" else 0.0)
+    return fix + P["f"] * (0.83 * (cyc + P["G"] * ga + P["SC"] * sc) + 0.42 * te), P.get(op["lat"], op["lat"])
 
 
 def build(T, core, topo):
@@ -85,454 +95,483 @@ def build(T, core, topo):
     ops = []
     ndma = [0]
     cls = ["-"]
+    rnd = [0]
+
+    def full(r):
+        return (tuple(r) + (1, 0, 128)[len(r) - 3:]) if len(r) < 6 else r
+
+    def on(r, p0, p1):
+        return full(r)[:4] + (p0, p1)
 
     def ap(r):
-        if len(r) == 4:
-            return T[r[0]][:, r[1]:r[2]:r[3]]
-        return T[r[0]][:, r[1]:r[2]]
+        b, lo, hi, st, p0, p1 = full(r)
+        sh = SCRATCH[b][1]
+        if len(sh) == 3:
+            pl = lo // sh[2]
+            return T[b][p0:p1, pl, lo - pl * sh[2]:hi - pl * sh[2]:st]
+        return T[b][p0:p1, lo:hi:st]
 
-    def add(q, fn, rd, wr, cost, kind="c", lat=0.0, sem=None, after=None):
-        ops.append({"q": q, "fn": fn, "rd": [r[:3] for r in rd], "wr": [r[:3] for r in wr], "cost": cost, "kind": kind,
-                    "lat": lat, "sem": sem, "after": after, "cls": cls[0]})
+    def add(q, fn, rd, wr, c, kind="c", lat=0.0, sem=None, after=None):
+        ops.append({"q": q, "fn": fn, "rd": [full(r) for r in rd], "wr": [full(r) for r in wr], "c": c, "kind": kind,
+                    "lat": lat, "sem": sem, "after": after, "cls": cls[0], "round": rnd[0], "soft": [] if after is None else [after]})
         return len(ops) - 1
 
     def width(r):
-        return len(range(*r[1:])) if len(r) == 4 else r[2] - r[1]
+        return len(range(*full(r)[1:4]))
 
-    def two(*rs):
-        return all(r[0] not in PSUM and SCRATCH[r[0]][2] in ("bfloat16", "uint16") for r in rs)
-
-    def cost1(n, fast):
-        return 55 + CY * max(64, n * (0.5 if fast else 1.0))
+    def cyc(o, *rs):
+        two = all(r[0] not in PSUM and SCRATCH[r[0]][2] in ("bfloat16", "uint16") for r in (o,) + rs)
+        return ("fv", max(64, width(o) * (0.5 if two else 1.0)), 0, 0, 0)
 
     def tt(o, a, b, op):
         f = 1 if (a[0] in PSUM or b[0] in PSUM) else 2
-        add("v", lambda e: e.tensor_tensor(ap(o), ap(a), ap(b), op), [a, b], [o], 55 + CY * max(64, f * width(o)))
+        add("v", [lambda e: e.tensor_tensor(ap(o), ap(a), ap(b), op)], [a, b], [o], ("fv", max(64, f * width(o)), 0, 0, 0))
 
     def ts(o, a, s1, op0, s2=None, op1=None):
-        rd = [a]
-        v1 = s1
-        if isinstance(s1, tuple):
-            rd.append(s1)
-        if op1 is None:
-            add("v", lambda e: e.tensor_scalar(ap(o), ap(a), ap(s1) if isinstance(s1, tuple) else s1, None, op0), rd, [o],
-                cost1(width(o), two(o, a)))
-        else:
-            add("v", lambda e: e.tensor_scalar(ap(o), ap(a), ap(s1) if isinstance(s1, tuple) else s1, s2, op0, op1), rd, [o],
-                cost1(width(o), two(o, a)))
-
-    def cp(o, a):
-        add("v", lambda e: e.tensor_copy(ap(o), ap(a)), [a], [o], cost1(width(o), two(o, a)))
-
-    def fill(o, c):
-        add("v", lambda e: e.memset(ap(o), c), [], [o], cost1(width(o), two(o)))
-
-    def gtt(o, win, off, b, op):
-        add("v", lambda e: e.tensor_tensor(ap(o), ap(win).indirect(ap(off)), ap(b), op), [win, off, b], [o],
-            50 + CY * GA * width(o))
-
-    def gcp(o, win, off):
-        add("v", lambda e: e.tensor_copy(ap(o), ap(win).indirect(ap(off))), [win, off], [o], 50 + CY * GA * width(o))
-
-    def scat(win, off, a):
-        add("v", lambda e: e.tensor_copy(ap(win).indirect(ap(off)), ap(a)), [off, a], [win], 50 + CY * 3.5 * width(a))
-
-    def act(o, a, func, bias=None, scale=None, acc=None):
-        kw = {}
-        rd = [a]
-        if bias is not None:
-            kw["bias"] = bias
-        sc = isinstance(scale, tuple)
-        if sc:
-            rd.append(scale)
+        cols = [s for s in (s1, s2) if isinstance(s, tuple)]
 
         def fn(e):
-            k = dict(kw)
+            x, y = [ap(s) if isinstance(s, tuple) else s for s in (s1, s2)]
+            if op1 is None:
+                return e.tensor_scalar(ap(o), ap(a), x, None, op0)
+            return e.tensor_scalar(ap(o), ap(a), x, y, op0, op1)
+        add("v", [fn], [a] + cols, [o], cyc(o, a))
+
+    def cp(o, a):
+        add("v", [lambda e: e.tensor_copy(ap(o), ap(a))], [a], [o], cyc(o, a))
+
+    def fill(o, c):
+        add("v", [lambda e: e.memset(ap(o), c)], [], [o], cyc(o))
+
+    def gtt(o, win, off, b, op):
+        add("v", [lambda e: e.tensor_tensor(ap(o), ap(win).indirect(ap(off)), ap(b), op)], [win, off, b], [o],
+            ("fv", 0, width(o), 0, 0))
+
+    def gts(o, win, off, s):
+        add("v", [lambda e: e.tensor_scalar(ap(o), ap(win).indirect(ap(off)), s, None, A.mult)], [win, off], [o],
+            ("fv", 0, width(o), 0, 0))
+
+    def scat(win, off, a):
+        add("v", [lambda e: e.tensor_copy(ap(win).indirect(ap(off)), ap(a))], [off, a], [win], ("fv", 0, 0, width(a), 0))
+
+    def act(o, a, func, bias=None, scale=None, acc=None):
+        def fn(e):
+            k = {}
+            if bias is not None:
+                k["bias"] = bias
             if scale is not None:
-                k["scale"] = ap(scale) if sc else scale
+                k["scale"] = scale
             if acc is not None:
                 k["accum_out"] = ap(acc)
             return e.activation(ap(o), ap(a), func, **k)
-        add("s", fn, rd, [o] + ([acc] if acc is not None else []), 80 + CY * max(64, width(o)))
+        add("s", [fn], [a], [o] + ([acc] if acc is not None else []), ("fs", max(64, width(o)), 0, 0, 0))
 
     def gact(o, win, off):
-        add("s", lambda e: e.activation(ap(o), ap(win).indirect(ap(off)), F.Copy), [win, off], [o], 65 + CY * GA * width(o))
+        add("s", [lambda e: e.activation(ap(o), ap(win).indirect(ap(off)), F.Copy)], [win, off], [o], ("fs", 0, width(o), 0, 0))
 
-    def mms(lst):
-        def fn(e):
-            r = None
-            for o, l, x, st, sp in lst:
-                r = e.matmul(ap(o), ap(l), ap(x), st, sp)
-            return r
-        wr = {}
-        for o, l, x, st, sp in lst:
-            lo, hi = wr.get(o[0], (o[1], o[2]))
-            wr[o[0]] = (min(lo, o[1]), max(hi, o[2]))
-        rd = {}
-        for o, l, x, st, sp in lst:
-            for y in (l, x):
-                lo, hi = rd.get(y[0], (y[1], y[2]))
-                rd[y[0]] = (min(lo, y[1]), max(hi, y[2]))
-        add("t", fn, [(k, v[0], v[1]) for k, v in rd.items()], [(k, v[0], v[1]) for k, v in wr.items()],
-            60 + CT * sum(max(64, width(x)) for o, l, x, st, sp in lst))
+    def mms(lst, first=True, last=True):
+        fns = [(lambda o, l, x, st, sp: lambda e: e.matmul(ap(o), ap(l), ap(x), st, sp))(
+            o, l, x, first and i == 0, last and i == len(lst) - 1) for i, (o, l, x) in enumerate(lst)]
+        te = sum(max(min(64, width(l)), width(x)) * (4 if SCRATCH[x[0]][2] == "float32" else 1) for o, l, x in lst)
+        rd = sorted(set(full(r) for o, l, x in lst for r in (l, x)))
+        add("t", fns, rd, sorted(set(full(o) for o, l, x in lst)), ("ft", 0, 0, 0, te))
+        if len(lst) == 1 and not last:
+            ops[-1]["cls"] = "op"
 
-    def sums(o, mat, buf, lo, hi, extra=()):
-        lst = [(o, (mat, 128 * p, 128 * p + 128), (buf, lo + p, hi, 16)) for p in range(16)] + [(o, l, x) for l, x in extra]
-        mms([(a, b, c, i == 0, i == len(lst) - 1) for i, (a, b, c) in enumerate(lst)])
+    def sums(o, band, buf, lo, hi):
+        return [(o, (band, 15 - p, 143 - p), (buf, lo + p, hi, 16)) for p in range(16)]
 
-    def gop(fn, rd, wr, cost):
-        add("g", fn, rd, wr, cost)
+    def sums_t(bank, o0, n, buf, lo, mat, nb=1, p0=0):
+        return [((bank, o0 + p, o0 + n, 16, p0, p0 + 16 * nb), (buf, lo + p, lo + 256 * nb, 16), mat) for p in range(16)]
 
-    def dma(q, out_fn, in_fn, rd, wr, lat):
+    lv = {}
+
+    def row(name, n, value, second=None):
+        c = sum(v[1] for v in lv.values())
+        lv[name] = (c, n)
+        if second is not None:
+            fill(("LV", c, c + n, 1, 0, 2), second)
+        fill(("LV", c, c + n, 1, 0, 1), value)
+
+    def const(o, sign, name, n=None, rows=1, at=0):
+        c = lv[name][0] + at
+        o = full(o)
+        return (o, ("one" if sign > 0 else "neg", 0, o[5] - o[4], 1, 0, rows), ("LV", c, c + width(o), 1, 0, rows))
+
+    def rounded(o, name):
+        return [const(o, 1, name), const(o, -1, name)]
+
+    def gop(fn, rd, wr, n, fix=170.0):
+        add("g", [fn], rd, wr, (fix, 2 * n, 0, 0, 0))
+
+    def iota(o, pattern, base, cm):
+        if SCRATCH[o[0]][2] == "int32":
+            gop(lambda e: e.iota(ap(o), pattern, base, cm), [], [o], width(o), 130.0)
+        else:
+            gop(lambda e: e.iota(ap(o), pattern, base, cm, allow_small_or_imprecise_dtypes=True), [], [o], width(o), 130.0)
+
+    def select(o, a, pattern, op, base, cm):
+        gop(lambda e: e.affine_select(ap(o), ap(a), pattern, op, 0.0, base, cm), [a], [o], width(o))
+
+    def dma(q, pairs, rd, wr, lat):
         s = "dm%d" % ndma[0]
         ndma[0] += 1
-        return add(q, lambda e: e.dma_start(out_fn(), in_fn()), rd, wr, 70.0, kind="dma", lat=lat, sem=s)
+        return add(q, [(lambda o, i: lambda e: e.dma_start(o, i))(o, i) for o, i in pairs], rd, wr, (60.0 * len(pairs), 0, 0, 0, 0),
+                   kind="dma", lat=lat, sem=s)
 
-    def send(t, what, src, dstname, dst, cost, lat):
+    def send(t, what, src, land, dst):
         rid, pid, _e = topo.addr(dst)
         m = topo.mask(core, dst)
-        i = add("g", lambda e: e.remote_dma(T[dstname][:, 0:SCRATCH[dstname][1][1]], ap(src), T.sem["a%s%d" % (what, t)],
-                                            T.sem["l%s%d" % (what, t)], pid, rid, m), [src], [], cost, kind="send", lat=lat,
-                sem="l%s%d" % (what, t))
-        return i
+        i = add("g", [lambda e: e.remote_dma(ap(land), ap(src), T.sem["a%s%d" % (what, t)], T.sem["l%s%d" % (what, t)], pid, rid, m)],
+                [src], [], ("issue", 0, 0, 0, 0), kind="send", lat=1500.0, sem="l%s%d" % (what, t))
+        add("n%d%s" % (t, what), None, [], [land], ("net_" + what, 0, 0, 0, 0), kind="arr", sem="a%s%d" % (what, t), after=i)
 
-    def arrive(t, what, dstname, after, lat):
-        add("n%d%s" % (t, what), None, [], [(dstname, 0, SCRATCH[dstname][1][1])], lat, kind="arr", sem="a%s%d" % (what, t),
-            after=after)
+    IDr, nIDr = ("ID", 0, 128), ("nID", 0, 128)
+    D = ("DD", 0, 4096)
+    Z = 4096
 
-    IDr = ("ID", 0, 128)
+    def halves(lay, flat):
+        return [(lay[32 * a + l:32 * a + 32:2, :, 16 * h:16 * h + 16], flat[32 * a + 16 * h:32 * a + 16 * h + 16, 128 * l:128 * l + 128])
+                for a in range(4) for h in range(2) for l in range(2)]
 
-    dma("y", lambda: T.wti[:, 0:1], lambda: T.wt[:, 0:1], [], [("wti", 0, 1)], 1900)
-    dma("y", lambda: T.XI[:], lambda: T.ef[:], [], [("XI", 0, 256)], 2000)
-    dma("y", lambda: T.AB0[:, 768:1024], lambda: T.zv[:], [], [("AB0", 768, 1024)], 2000)
-    dma("s", lambda: T.XJ[:], lambda: T.ef[:], [], [("XJ", 0, 256)], 2000)
-    dma("s", lambda: T.DD[:], lambda: T.dv[:], [], [("DD", 0, 4096)], 5000)
-
-    def swap(q, dst, src, gi, h, dd):
-        o = gi ^ 1
-        dma(q, lambda: T[dst][16 * gi:16 * gi + 16, :, 16 * (1 - h):16 * (1 - h) + 16],
-            lambda: T[src][16 * o:16 * o + 16, :, 16 * h:16 * h + 16], [(src, 0, 256)], [(dst, 32 * gi + 1000, 32 * gi + 1032)], 1900)
-    ops[3]["wr"].append(("XJ", 1000, 1256))
-    for gi in range(8):
-        swap("y" if gi % 2 else "s", "XJ", "XI", gi, gi % 2, None)
-
+    cls[0] = "ld"
+    dma("y", [(T.wti[:, 0:1], T.wt[:, 0:1])], [], [("wti", 0, 1)], 1900)
+    dma("y", [(T.AB0[:, Z:Z + 256], T.zv[:])], [], [("AB0", Z, Z + 256)], 2000)
+    pr = halves(T.XJ, T.ef)
+    dma("y", pr[:8], [], [("XJ", 0, 256, 1, 0, 64)], 2000)
+    dma("s", pr[8:], [], [("XJ", 0, 256, 1, 64, 128)], 2000)
+    dma("s", [(T.DD[:], T.dv[:])], [], [D], 4500)
+    cls[0] = "-"
     fill(("on8", 0, 8), 1.0)
     fill(("one", 0, 256), 1.0)
-    gop(lambda e: e.affine_select(T.b8a[:, 0:8], T.on8[:, 0:8], [[-16, 8]], A.is_ge, 0.0, 0, 1), [("on8", 0, 8)], [("b8a", 0, 8)], 190)
-    gop(lambda e: e.affine_select(T.b8[:, 0:8], T.b8a[:, 0:8], [[16, 8]], A.is_ge, 0.0, 15, -1), [("b8a", 0, 8)], [("b8", 0, 8)], 190)
-    gop(lambda e: e.affine_select(T.ID[:, 0:128], T.one[:, 0:128], [[-1, 128]], A.is_equal, 0.0, 0, 1), [("one", 0, 128)], [IDr], 400)
-    gop(lambda e: e.iota(T.KI[:, 0:256], [[1, 16], [0, 16]], 4, 0, allow_small_or_imprecise_dtypes=True), [], [("KI", 0, 256)], 600)
-    gop(lambda e: e.iota(T.it0[:, 0:16], [[0, 16]], 0, 1), [], [("it0", 0, 16)], 180)
-    gop(lambda e: e.iota(T.it1[:, 0:16], [[16, 16]], 0, 0), [], [("it1", 0, 16)], 180)
-    fill(("WW", 0, 2048), 0.0)
-    fill(("OV", 0, 2048), 0.0)
-    fill(("on16", 0, 16), 1.0)
+    fill(("neg", 0, 128), -1.0)
+    select(("b8a", 0, 8), ("on8", 0, 8), [[-16, 8]], A.is_ge, 0, 1)
+    select(("b8", 0, 8), ("b8a", 0, 8), [[16, 8]], A.is_ge, 15, -1)
+    select(IDr, ("one", 0, 128), [[-1, 128]], A.is_equal, 0, 1)
+    iota(("it", 0, 256, 1, 0, 32), [[0, 16], [-1, 16]], 0, 1)
+    iota(("kf", 0, 256), [[1, 16], [0, 16]], 0, 0)
+    iota(("pi", 0, 1), [[0, 1]], 0, 1)
     cp(("wtf", 0, 1), ("wti", 0, 1))
-    ts(("wb8", 0, 8), ("b8", 0, 8), ("wtf", 0, 1), A.mult)
-    for j in range(8):
-        act(("WW", 16 * j, 16 * j + 1936, 129), ("on16", 0, 16), F.Copy, scale=("wb8", j, j + 1))
-        ops[-1]["wr"] = [("WW", 3000 + j, 3001 + j)]
-        ops[-1]["rd"] += [("WW", 0, 2048)]
-        ts(("OV", 16 * j, 16 * j + 1936, 129), ("on16", 0, 16), ("b8", j, j + 1), A.mult, BIG, A.mult)
-        ops[-1]["wr"] = [("OV", 3000 + j, 3001 + j)]
-        ops[-1]["rd"] += [("OV", 0, 2048)]
-    act(("OS", 0, 2048), ("OV", 0, 2048), F.Copy, scale=0.5)
-    ops[-1]["rd"] += [("OV", 3000, 3008)]
-    ts(("nID", 0, 128), IDr, -1.0, A.mult)
-    ts(("I22", 0, 128), IDr, 2.0 ** 22, A.mult)
-    ts(("IP", 0, 128), IDr, 2.0 ** 14, A.mult)
-    ts(("IN", 0, 128), IDr, -2.0 ** 14, A.mult)
-    ts(("pC", 256, 512), ("KI", 0, 256), 4096.0, A.mult)
-    fill(("pC", 256, 272), 3 * 4096.0)
-    ts(("KC", 0, 256), ("KI", 0, 256), -0.5, A.add)
-    fill(("KC", 0, 16), 23.5)
-    ts(("it2", 0, 16), ("it0", 0, 16), 15, A.bitwise_and)
-    tt(("sl", 0, 16), ("it2", 0, 16), ("it1", 0, 16), A.add)
-    ts(("sl16", 0, 16), ("sl", 0, 16), 16, A.mult)
-    fill(("tb", 0, 1), -7.5 * BIG)
+    fill(("OB", 0, 144), 0.0)
+    ts(("OB", 15, 143, 16), ("b8", 0, 8), W1, A.mult)
+    ts(("O8", 0, 8), ("b8", 0, 8), W1, A.mult)
+    ts(("W16", 0, 8), ("b8", 0, 8), ("wtf", 0, 1), A.mult)
+    ts(("W16", 8, 16), ("b8", 0, 8), ("wtf", 0, 1), A.mult, -1.0, A.mult)
+    ts(("W16", 16, 24), ("b8", 0, 8), ("wtf", 0, 1), A.mult)
+    act(nIDr, IDr, F.Copy, scale=-1.0)
+    act(("hID", 0, 128), IDr, F.Copy, scale=0.5)
+    act(("I32", 0, 128), IDr, F.Copy)
+    act(("nI32", 0, 128), IDr, F.Copy, scale=-1.0)
+    row("rb", 128, -2048.0, 0.5)
+    row("rz", 128, 0.0, 0.0)
+    row("m1", 128, magic(4096))
+    row("m2", 128, magic(64))
+    row("rn", 128, -magic(64), 2048.0)
+    for j in range(3):
+        row("u%d" % j, 128, magic(UNITS[j]))
+    row("m16", 16, magic(16))
+    row("7.5", 16, 7.5)
+    row("1/4", 256, 0.25)
+    row("m0", 128, magic(1))
+    ts(("iu", 0, 256, 1, 0, 32), ("it", 0, 256, 1, 0, 32), 15, A.bitwise_and)
+    ts(("SL", 0, 256, 1, 0, 32), ("iu", 0, 256, 1, 0, 32), 0.0, A.is_equal)
+    act(("nSL", 0, 256, 1, 0, 16), ("SL", 0, 256, 1, 0, 16), F.Copy, scale=-1.0)
+    ts(("pj", 0, 1), ("pi", 0, 1), 15, A.bitwise_and)
+    cp(("pf", 0, 1), ("pj", 0, 1))
+    fill(("BL", 0, 128, 1, 0, 64), 0.0)
+    fill(("BL", 0, 128, 1, 64, 128), 1.0)
+    fill(("BL", 0, 128, 1, 64, 65), 0.0)
+    fill(("CB", 0, 1040), 0.0)
+    CA, CC, CBB, CK, C0 = 0, 256, 512, 768, 1024
 
-    def bias_mats():
-        act(("tb2", 0, 1), ("tb", 0, 1), F.Identity, bias=8.0 * BIG)
-        act(("NBV", 0, 128), IDr, F.Copy, scale=("tb", 0, 1))
-        act(("NBS", 0, 128), IDr, F.Copy, scale=("tb2", 0, 1))
-    bias_mats()
+    def bias(c0, lo, hi, par, one, sg=None):
+        r = ("CB", c0 + 16 * lo, c0 + 16 * hi)
+        fill(on(r, 64, 66), one)
+        fill(on(r, 64, 65), par)
+        if sg is not None:
+            act(on(r, 0, 16), ("SL", 16 * lo, 16 * hi, 1, 0, 16), F.Copy, scale=sg)
+
+    def runs(lst):
+        out = []
+        for lo, hi, k in sorted(lst):
+            if out and out[-1][1] == lo and out[-1][2] == k:
+                out[-1] = (out[-1][0], hi, k)
+            else:
+                out.append((lo, hi, k))
+        return out
+    def kinds(x, lst):
+        return runs([(k, k + 1, (q, UNITS[ORDER[k // 8].index(x)])) for lo, hi, q in lst for k in range(lo, hi)])
+    for lo, hi, (q, u) in kinds("a", A_V + A_S):
+        bias(CA, lo, hi, -2 * W1, (-15 * W1 if q == "v" else W1) - u / 2)
+    for lo, hi, (q, u) in kinds("c", [x + ("v",) for x in C_V] + [x + ("s",) for x in C_S if x[0] < C_LATE[0]]):
+        bias(CC, lo, hi, -W1 if q == "v" else -2 * W1, (-7.5 * W1 if q == "v" else W1) - u / 4, -u / 4)
+    bias(CC, C_LATE[0], C_LATE[1], 2 * W1, -17 * W1, 16 * W1)
+    bias(CC, C_LAST[0], C_LAST[1], W1, -16.5 * W1, 8 * W1)
+    for lo, hi, (q, u) in kinds("b", [(1, 16, "v")]):
+        bias(CBB, lo, hi, -W1, -7.5 * W1, u / 2)
+    bias(C0, 0, 1, -2 * W1, -15 * W1)
+    ts(("CB", CK, CK + 256, 1, 64, 66), ("kf", 0, 256, 1, 64, 66), -1.0, A.add, 65536.0, A.mult)
+    bias(CK, 0, 1, 0.0, 15.5 * 65536, -32768.0)
+    fill(("CB", CK, CK + 256, 1, 64, 65), 0.0)
+    iota(("CB", CK, CK + 256, 1, 96, 97), [[0, 16], [4096, 16]], 0, 0)
+    fill(("qc", 0, 1, 1, 0, 32), 33 * SQ)
+    fill(("qc", 0, 1, 1, 0, 16), SQ)
+    ts(("QP", 0, 256, 1, 0, 32), ("SL", 0, 256, 1, 0, 32), ("qc", 0, 1, 1, 0, 32), A.mult)
+    ts(("QP", 0, 256, 1, 32, 33), ("kf", 0, 256, 1, 32, 33), 145.0, A.add, -SQ, A.mult)
+    act(("QN", 0, 256, 1, 0, 33), ("QP", 0, 256, 1, 0, 33), F.Copy, scale=-1.0)
+    fill(("TT", 0, 128, 1, 32, 64), 1.0)
+    fill(("HF", 0, 128, 1, 0, 32), 0.5)
+    fill(("HF", 128, 256, 1, 0, 32), -0.5)
+    fill(("HF", 0, 256, 1, 0, 16), 0.0)
+    iota(("CL", 0, 128, 1, 0, 2), [[0, 8], [16, 16]], 0, 0)
+    fill(("CL", 0, 128, 1, 0, 1), 1.0)
+    fill(("CR", 0, 16, 1, 0, 2), 1.0)
+    iota(("CR", 0, 16, 1, 0, 1), [[256, 16]], 0, 0)
+    cls[0] = "ld"
+    add("v", [lambda e: e.tensor_scalar(T.XF[:], T.XJ[:], 1184.0, None, A.add)], [("XJ", 0, 256)], [("XF", 0, 256)], ("fv", 256, 0, 0, 0))
     for b in range(8):
-        add("v", (lambda b: lambda e: e.tensor_scalar(T.XF[:, 32 * b:32 * b + 32], T.XJ[:, b], 1184.0, None, A.add))(b),
-            [("XJ", 0, 256), ("XJ", 1000, 1256)], [("XF", 32 * b, 32 * b + 32)], cost1(32, False))
-    add("v", lambda e: e.transpose(T.RT[:, 0:256], T.XF[:, 0:256]), [("XF", 0, 256)], [("RT", 0, 256)], cost1(256, False))
+        add("v", [(lambda b: lambda e: e.transpose(ap(("EL0", b, 256, 8)), T.XF[:, b]))(b)], [("XF", 32 * b, 32 * b + 32)],
+            [("EL0", 1000 + b, 1001 + b)], ("fv", 64, 0, 0, 0))
 
-    def blk(k):
-        return 0 if k == 0 else 16 - k
-    for k in range(16):
-        b = blk(k)
-        o, a = ("EB0", 16 + 16 * b, 32 + 16 * b), ("RT", k, 256, 16)
-        if k % 2:
-            act(o, a, F.Copy)
+    def spread(buf, col, evac, n):
+        HL, H = ("pW", 0, 256, 1, 0, 16), ("pW", 0, 128, 1, 0, 16)
+        mms([const(HL, 1, "rb", rows=2)], last=False)
+        mms(sums_t("pW", 0, 256, buf, col, ("W16", 0, 16)) + rounded(HL, "m1"), first=False, last=False)
+        mms(sums_t("pW", 0, 256, buf, col, ("W16", 8, 24)) + [const(H, 1, "m2"), const(H, 1, "rn", rows=2)], first=False)
+        act((evac, 0, 256, 1, 0, 16), HL, F.Copy)
+        o = ("pW", 256, 256 + n)
+        mms([(o, (evac, 0, 128, 1, 0, 16), ("nSL", 0, n, 1, 0, 16)), (o, (evac, 128, 256, 1, 0, 16), ("SL", 0, n, 1, 0, 16))])
+        return o
+
+    def hashed(v, el, c, d, x, n, u):
+        tt(v, v, (el, c, d), A.mult)
+        if el == "EL0":
+            ops[-1]["rd"].append(full(("EL0", 1000, 1008)))
+        tt((x, c, d), v, (el, 256 + c, 256 + d), A.add)
+        ts((n, c, d), (x, c, d), 5, A.arith_shift_right, 4095, A.bitwise_and)
+        if x in G_CONV:
+            select((u, c, d), (n, c, d), [[0, d - c]], A.is_gt, 1, 0)
         else:
-            cp(o, a)
-    act(("EB0", 0, 16), ("RT", 1, 256, 16), F.Copy)
+            cp((u, c, d), (n, c, d))
 
-    def wrefs(mat):
-        ops[-1]["rd"].append((mat, 3000, 3008))
-    C2 = -6722560.0
+    def R(lo, hi):
+        return ("pR1", 16 * lo + 128, 16 * hi + 128) if lo < 8 else ("pR2", 16 * lo, 16 * hi)
 
-    def effects(eb):
-        act(("pE", 0, 256), (eb, 16, 272), F.Copy)
-        act(("pF", 0, 256), (eb, 16, 272), F.Identity, bias=C2, scale=2080.0)
+    def RT(lo, hi):
+        return ("pR1", 0, 128, 1, 16 * lo - 16, 16 * hi - 16) if lo < 8 else ("pR2", 0, 128, 1, 16 * lo - 128, 16 * hi - 128)
 
-    def first_effect(eb):
-        act(("pE", 272, 288), (eb, 16, 32), F.Copy)
-        act(("pE", 288, 304), (eb, 16, 32), F.Copy)
-        act(("pE", 304, 336), ("pE", 272, 304), F.Copy)
-        act(("pE", 336, 400), ("pE", 272, 336), F.Copy)
-        act(("pE", 400, 512), ("pE", 272, 384), F.Copy)
-        act(("pF", 272, 512), ("pE", 272, 512), F.Identity, bias=C2, scale=2080.0)
+    def turned(c0, lo, hi, p0=0):
+        return (RT(lo, hi), ("CB", c0 + 16 * lo, c0 + 16 * hi, 1, p0, 97), ("BL", 0, 128, 1, p0, 97))
+
+    def biased(o, c0, lo, hi, p0=0):
+        return (o, ("BL", 0, 128, 1, p0, 97), ("CB", c0 + 16 * lo, c0 + 16 * hi, 1, p0, 97))
+
+    def update(t):
+        el = ("EL%d" % (t + 1), 240, 256)
+        o = ("pU2", 256, 272)
+        mms([const(o, 1, "7.5")], last=False)
+        mms([(o, ("nI32", 0, 128), el)] + rounded(o, "m16") + [(o, ("I32", 0, 128), el), (o, ("CL", 0, 128, 1, 0, 2), ("CR", 0, 16, 1, 0, 2))],
+            first=False)
+        cp(("cu", 0, 16), o)
+        gact(("DG", 0, 256), D, ("cu", 0, 16))
+        o = ("pG", 0, 256)
+        mms([const(o, -1, "1/4")], last=False)
+        mms([(o, ("hID", 0, 128), ("DG", 0, 256))], first=False)
+        tt(("dh", 0, 256), o, ("hl%d" % t, 0, 256), A.add)
+        scat(D, ("cu", 0, 16), ("dh", 0, 256))
 
     for t in range(RO):
         AB, AN = "AB%d" % (t % 2), "AB%d" % ((t + 1) % 2)
-        EB, EN = "EB%d" % (t % 2), "EB%d" % ((t + 1) % 2)
-        DF = "df%d" % (t % 2)
-        D = ("DD", 0, 4096)
+        EL, EN = "EL%d" % t, "EL%d" % (t + 1)
+        rnd[0] = t
+
+        def blk(lo, hi):
+            return (AB, 256 * (lo - 1), 256 * (hi - 1)) if lo else (AB, 3840, 4096)
         cls[0] = "hs"
-        act((AB, 512, 768), (AB, 768, 1024), F.Copy)
-        act((AB, 0, 512), (AB, 512, 1024), F.Copy)
-        sums(("pU", 256, 320), "WW", AB, 0, 1024)
-        wrefs("WW")
-        cp(("ui", 0, 64), ("pU", 256, 320))
-        ts(("va", 0, 64), ("ui", 0, 64), 4095, A.bitwise_and)
-        ts(("vx", 0, 64), ("va", 0, 64), -2048.0, A.add)
-        if t > 0:
-            nl = ("nl%d" % (t - 1), 0, 16)
-            ts((EB, 32, 48), nl, 1184.0, A.add)
-            ts(("k1", 0, 16), nl, 15, A.bitwise_and)
-            tt(("k2", 0, 16), ("k1", 0, 16), ("sl16", 0, 16), A.add)
-            cp(("cu", 0, 16), ("k2", 0, 16))
-        cls[0] = "ef"
-        effects(EB)
-        first_effect(EB)
+        cut = ((0, 240), (240, 256)) if t else ((0, 256),)
+        for c, d in cut:
+            cls[0] = "li" if c == 0 else "ly"
+            act((EL, 256 + c, 256 + d), (EL, c, d), F.Identity, bias=C2, scale=2080.0)
+        if t == 0:
+            ops[-1]["rd"].append(full(("EL0", 1000, 1008)))
         cls[0] = "hs"
-        for j in range(4):
-            tt(("x1", 64 * j, 64 * j + 64), ("pE", 64 * j, 64 * j + 64), ("vx", 0, 64), A.mult)
-        tt(("x2", 0, 256), ("pF", 0, 256), ("x1", 0, 256), A.add)
-        ts(("nn", 0, 256), ("x2", 0, 256), 5, A.arith_shift_right, 4095, A.bitwise_and)
-        cp(("nu", 0, 256), ("nn", 0, 256))
-        cls[0] = "q0"
-        tt(("q0", 0, 256), ("pC", 256, 512), ("nn", 0, 256), A.add)
+        v = spread(AB, Z, "VA", 256)
+        cls[0] = "zr"
+        act((AB, Z + 256, Z + 512), (AB, Z, Z + 256), F.Copy)
+        act((AB, Z + 512, Z + 1024), (AB, Z, Z + 512), F.Copy)
         cls[0] = "up"
         if t > 0:
-            gtt(("ds", 0, 256), D, ("cu", 0, 16), ("zl%d" % (t - 1), 0, 256), A.add)
-            ts(("dh", 0, 256), ("ds", 0, 256), 1, A.arith_shift_right)
-            scat(D, ("cu", 0, 16), ("dh", 0, 256))
+            update(t - 1)
+        for c, d in cut:
+            cls[0] = "hs" if c == 0 else "hy"
+            hashed(("pW", 256 + c, 256 + d), EL, c, d, "xa", "na", "ua")
+        cls[0] = "er"
+        n = 16
+        src = EL
+        while n < 256:
+            m = min(n, 256 - n) if src == "ER" else 16
+            lo = 16 if src == "ER" else 0
+            to = lo + n if src == "ER" else 16
+            m = min(m, 256 - to)
+            if m <= 0:
+                break
+            gop((lambda src, lo, to, m: lambda e: e.affine_select(T.ER[:, :, to:to + m], T[src][:, :, lo:lo + m], [[0, 2 * m]], A.is_gt,
+                                                                 0.0, 1, 0))(src, lo, to, m),
+                [(src, lo, lo + m), (src, 256 + lo, 256 + lo + m)], [("ER", to, to + m), ("ER", 256 + to, 256 + to + m)], 2 * m)
+            if src == "ER":
+                n *= 2
+            src = "ER"
+        cls[0] = "ca"
+        for lo, hi in PIECES:
+            mms([turned(CA, lo, hi, 64)], last=False)
 
         def gather_a(lo, hi):
-            gtt((DF, 256 * lo, 256 * hi), D, ("nu", 16 * lo, 16 * hi), (AB, 1024 - 256 * (hi - lo), 1024), A.subtract)
+            gtt(("df", 256 * lo, 256 * hi), D, ("ua", 16 * lo, 16 * hi), (AB, Z, Z + 256 * (hi - lo)), A.subtract)
+            act(blk(lo, hi), ("df", 256 * lo, 256 * hi), F.Abs)
 
-        def absd(lo, hi):
-            act((AB, 1024 + 256 * lo, 1024 + 256 * hi), (DF, 256 * lo, 256 * hi), F.Abs)
-
-        def mask_a(lo, hi):
-            if lo in M_S:
-                act(("ma", 256 * lo, 256 * hi), (DF, 256 * lo, 256 * hi), F.Sign, bias=-0.5)
+        def mask_a(lo, hi, k, src):
+            if k == "s":
+                act(("ma", 256 * lo, 256 * hi), src, F.Sign, bias=-0.5)
             else:
-                ts(("ma", 256 * lo, 256 * hi), (DF, 256 * lo, 256 * hi), 0.0, A.is_gt)
-
-        def count(bank, buf, lo, hi, sgn, extra=()):
-            if sgn:
-                sums((bank, 16 * lo, 16 * hi), "OS", buf, 256 * lo, 256 * hi, [(("NBS", 0, 128), ("one", 0, 16 * (hi - lo)))] + list(extra))
-            else:
-                sums((bank, 16 * lo, 16 * hi), "OV", buf, 256 * lo, 256 * hi, [(("NBV", 0, 128), ("one", 0, 16 * (hi - lo)))] + list(extra))
-                wrefs("OV")
-
-        def sums_u(lo, hi):
-            sums(("pU", 16 * lo, 16 * hi), "WW", AB, 1024 + 256 * lo, 1024 + 256 * hi)
-            wrefs("WW")
+                ts(("ma", 256 * lo, 256 * hi), src, 0.0, A.is_gt, 2.0, A.mult)
         cls[0] = "a0"
         gather_a(0, 1)
-        absd(0, 1)
-        sums_u(0, 1)
-        cls[0] = "m0"
-        mask_a(0, 1)
-        count("pA", "ma", 0, 1, 0 in M_S)
         cls[0] = "hc"
-        cp(("uic", 0, 16), ("pU", 0, 16))
-        ts(("vac", 0, 16), ("uic", 0, 16), 4095, A.bitwise_and)
-        ts(("vxc", 0, 16), ("vac", 0, 16), -2048.0, A.add)
-        cp(("vxc", 16, 32), ("vxc", 0, 16))
-        cp(("vxc", 32, 64), ("vxc", 0, 32))
-        for c, d in C_H:
-            for lo in range(c, d, 4):
-                hi = min(lo + 4, d)
-                tt(("x1c", 16 * lo, 16 * hi), ("pE", 16 * lo, 16 * hi), ("vxc", 0, 16 * (hi - lo)), A.mult)
-            c, d = 16 * c, 16 * d
-            tt(("x2c", c, d), ("pF", c, d), ("x1c", c, d), A.add)
-            ts(("nc", c, d), ("x2c", c, d), 5, A.arith_shift_right, 4095, A.bitwise_and)
-            cp(("ncu", c, d), ("nc", c, d))
-            cls[0] = "h2"
+        v = spread(AB, 3840, "VC", 240)
+        hashed(v, EL, 16, 256, "xc", "nc", "uc")
         cls[0] = "m0"
-        ts(("na0", 0, 16), ("pA", 0, 16), 0.0, A.is_lt)
-        mms([(("pA", 256 + 16 * b, 272 + 16 * b), IDr, ("na0", 0, 16), True, True) for b in range(1, 16)])
-        act(("nax", 16, 256), ("pA", 272, 512), F.Copy)
-        act(("s0", 16, 256), ("nax", 16, 256), F.Identity, bias=-1.0, scale=2.0)
-        ts(("c0", 0, 16), ("na0", 0, 16), -4096.0, A.mult, 4096.0, A.add)
-        tt(("c1", 0, 16), ("c0", 0, 16), ("q0", 0, 16), A.add)
+        dma("y", [(ap(("ZR", 256 * i, 256 * i + 256)), ap(blk(0, 1))) for i in range(4)], [blk(0, 1)], [("ZR", 0, 1024)], 2200)
+        mask_a(0, 1, "v", ("df", 0, 256))
+        o = ("pC", 128, 256, 1, 0, 16)
+        mms([(o, ("CB", C0, C0 + 16, 1, 64, 66), ("BL", 0, 128, 1, 64, 66))] + sums_t("pC", 128, 128, "ma", 0, ("O8", 0, 8)))
+        act(("BL", 0, 128, 1, 0, 16), o, F.Sign)
         nslot = [0]
 
-        def apart(buf, off, lo, hi, other):
-            bank = ("pG", "pH")[nslot[0] % 2]
-            nslot[0] += 1
-            gact((buf, 256 * lo, 256 * hi), D, (off, 16 * lo, 16 * hi))
-            for i, b in enumerate(range(lo, hi)):
-                mms([((bank, 256 * i, 256 * i + 256), IDr, (buf, 256 * b, 256 * b + 256), True, False),
-                     ((bank, 256 * i, 256 * i + 256), ("nID", 0, 128), other(b), False, True)])
-            return (bank, 0, 256 * (hi - lo))
-        for lo, hi in A_S:
-            cls[0] = "as"
-            p = apart("dg", "nu", lo, hi, lambda b: (AB, 768, 1024))
-            act((AB, 1024 + 256 * lo, 1024 + 256 * hi), p, F.Abs)
-            if lo in M_S:
-                act(("ma", 256 * lo, 256 * hi), p, F.Sign, bias=-0.5)
-            else:
-                ts(("ma", 256 * lo, 256 * hi), p, 0.0, A.is_gt)
-        for lo, hi in A_V[1:]:
-            cls[0] = "av"
+        def apart(buf, off, c, d, other):
+            gact((buf, 256 * c, 256 * d), D, (off, 16 * c, 16 * d))
+            for lo in range(c, d, 2):
+                hi = min(lo + 2, d)
+                bank = BANKS[nslot[0]]
+                nslot[0] += 1
+                o = (bank, 0, 256 * (hi - lo))
+                mms([(o, IDr, (buf, 256 * lo, 256 * hi))] + [((bank, 256 * i, 256 * i + 256), nIDr, other) for i in range(hi - lo)])
+                yield lo, hi, o
+        for i, (lo, hi, k) in enumerate(A_V):
+            cls[0] = "av%d" % i
             gather_a(lo, hi)
-            absd(lo, hi)
-            cls[0] = "am"
-            mask_a(lo, hi)
-
-        def hash_b(lo, hi):
-            c = 16 * lo
-            d = 16 * hi
-            sums_u(lo, hi)
-            cp(("uib", c, d), ("pU", c, d))
-            ts(("vab", c, d), ("uib", c, d), 4095, A.bitwise_and)
-            ts(("vxb", c, d), ("vab", c, d), -2048.0, A.add)
-            tt(("x1b", c, d), ("pE", 256 + c, 256 + d), ("vxb", c, d), A.mult)
-            tt(("x2b", c, d), ("pF", 256 + c, 256 + d), ("x1b", c, d), A.add)
-            ts(("nb", c, d), ("x2b", c, d), 5, A.arith_shift_right, 4095, A.bitwise_and)
-            cp(("nbu", c, d), ("nb", c, d))
-        cls[0] = "cs"
-        for lo, hi, sgn in C_C:
-            if sgn:
-                for b in range(lo, hi, 2):
-                    p = apart("dc", "ncu", b, min(b + 2, hi), lambda b: (AB, 1024, 1280))
-                    act(("mc", 256 * b, 256 * min(b + 2, hi)), p, F.Sign, bias=-0.5)
-            else:
-                for b in range(lo, hi):
-                    gtt(("mc", 256 * b, 256 * b + 256), D, ("ncu", 16 * b, 16 * b + 16), (AB, 1024, 1280), A.is_gt)
-            count("pC", "mc", lo, hi, sgn, [(("I22", 0, 128), ("nax", 16 * lo, 16 * hi))])
-        for lo, hi in B_H:
-            cls[0] = "hb"
-            hash_b(lo, hi)
-            cls[0] = "b"
-            for c, d, sgn in B_C:
-                if c < lo or c >= hi:
-                    continue
-                st = 2 if sgn else 4
-                for q in range(c, d, st):
-                    r = min(q + st, d)
-                    if sgn:
-                        p = apart("db", "nbu", q, r, lambda b: (AB, 1024 + 256 * b, 1280 + 256 * b))
-                        act(("mb", 256 * q, 256 * r), p, F.Sign, bias=-0.5)
-                    else:
-                        gtt(("mb", 256 * q, 256 * r), D, ("nbu", 16 * q, 16 * r), (AB, 1024 + 256 * q, 1024 + 256 * r), A.is_gt)
-        cls[0] = "ca"
-        for lo, hi, sgn in A_C:
-            count("pA", "ma", lo, hi, sgn)
-        for lo, hi in B_H:
-            tt(("q1", 16 * lo, 16 * hi), ("pA", 16 * lo, 16 * hi), ("q0", 16 * lo, 16 * hi), A.min)
-        cls[0] = "de"
-        for lo, hi in B_H:
-            c = 16 * lo
-            d = 16 * hi
-            tt(("q2", c, d), ("pC", c, d), ("q1", c, d), A.min)
-        for lo, hi, sgn in B_C:
-            c = 16 * lo
-            d = 16 * hi
-            count("pB", "mb", lo, hi, sgn)
-            z = ("pU", 256 + c, 256 + d)
-            tt(z, ("pB", c, d), ("s0", c, d), A.mult)
-            tt(("cd", c, d) if lo < 9 else z, z, ("q2", c, d), A.min)
+            cls[0] = "am%d" % i
+            mask_a(lo, hi, k, ("df", 256 * lo, 256 * hi))
+        for i, (c, d, k) in enumerate(A_S):
+            cls[0] = "as%d" % i
+            for lo, hi, p in apart("dg", "ua", c, d, (AB, Z, Z + 256)):
+                act(blk(lo, hi), p, F.Abs)
+                cls[0] = "sg%d" % i
+                mask_a(lo, hi, k, p)
+                cls[0] = "as%d" % i
+        for i, (lo, hi) in enumerate(C_V):
+            cls[0] = "cv%d" % i
+            gtt(("mc", 256 * lo, 256 * hi), D, ("uc", 16 * lo, 16 * hi), ("ZR", 0, 256 * (hi - lo)), A.is_gt)
+        for i, (c, d) in enumerate(C_S):
+            cls[0] = "cs%d" % i
+            for lo, hi, p in apart("dc", "uc", c, d, blk(0, 1)):
+                sg = -1.0 if lo >= C_LATE[0] else 1.0
+                act(("mc", 256 * lo, 256 * hi), p, F.Sign, bias=-0.5 * sg, scale=sg)
+        for i, (lo, hi) in enumerate(B_H):
+            cls[0] = "hb%d" % i
+            c, d = 16 * lo, 16 * hi
+            v = ("pU%d" % (i % 2 + 1), 0, d - c)
+            u = ("UT", 128 * i, 128 * i + 128, 1, 0, d - c)
+            mms(sums_t(v[0], 256, 128, AB, 256 * (lo - 1), ("W16", 0, 8), hi - lo))
+            act(u, (v[0], 256, 384, 1, 0, d - c), F.Copy)
+            mms([const(v, -1, "rb", rows=2), (v, u, ("nI32", 0, d - c, 1, 0, d - c))] + rounded(v, "m1")
+                + [const(v, 1, "rb"), (v, u, ("I32", 0, d - c, 1, 0, d - c))])
+            hashed(v, "ER", c, d, "xb", "nb", "ub")
+            cls[0] = "b%d" % i
+            for p, q in B_V:
+                if lo <= p < hi:
+                    last_b = len(ops)
+                    gtt(("mb", 256 * p, 256 * q), D, ("ub", 16 * p, 16 * q), blk(p, q), A.is_gt)
+        for i, (lo, hi) in enumerate(PIECES):
+            l0 = lo - lo % 8
+            for j, x in enumerate(ORDER[i]):
+                cls[0] = "c%s%d" % (x, i)
+                e = hi
+                if x != "a":
+                    mms([turned(CC if x == "c" else CBB, lo, e)], first=False, last=False)
+                for p, q in COUNTS[x]:
+                    if lo <= p < e:
+                        o = RT(p, q)
+                        mms(sums_t(o[0], 0, 128, "m" + x, 256 * p, ("O8", 0, 8), q - p, o[4]) + rounded(o, "u%d" % j), first=False,
+                            last=j == len(ORDER[i]) - 1 and q == e)
+            cls[0] = "v%d" % i
+            m = 16 * (hi - lo)
+            act(("AT", 128 * i, 128 * i + 128, 1, 0, m), RT(lo, hi), F.Abs)
+            mms([biased(R(l0, hi), CK, l0, hi)], last=False)
+            mms([(R(lo, hi), ("AT", 128 * i, 128 * i + 128, 1, 0, m), ("ID", 0, m, 1, 0, m))], first=False)
+            tt(("val", 16 * l0, 16 * hi), R(l0, hi), ("na", 16 * l0, 16 * hi), A.add)
+            if i == 0:
+                tt(("t1", 0, 64), ("val", 0, 64), ("val", 64, 128), A.min)
+        cls[0] = "ct"
+        lo, hi = C_LATE
+        o = ("pU1", 0, 64)
+        mms([biased(o, CC, lo, hi)], last=False)
+        mms(sums(o, "OB", "mc", 256 * lo, 256 * hi), first=False)
+        tt(o, o, ("val", 128, 192), A.max)
+        tt(("t2", 0, 64), o, ("t1", 0, 64), A.min)
+        cls[0] = "cl"
+        lo, hi = C_LAST
+        o = ("pC", 0, 64)
+        mms([biased(o, CC, lo, hi)], last=False)
+        gtt(("mc", 256 * lo, 256 * hi), D, ("uc", 16 * lo, 16 * hi), ("ZR", 0, 256 * (hi - lo)), A.is_le)
+        ops[-1]["soft"] = [last_b]
         cls[0] = "tl"
-        tt(("tr", 112, 128), ("c1", 0, 16), ("cd", 128, 144), A.max)
-        tt(("tr", 0, 112), ("pU", 400, 512), ("cd", 16, 128), A.max)
-        tt(("t64", 0, 64), ("tr", 0, 64), ("tr", 64, 128), A.max)
-        tt(("t32", 0, 32), ("t64", 0, 32), ("t64", 32, 64), A.max)
-        tt(("ci", 0, 16), ("t32", 0, 16), ("t32", 16, 32), A.max)
-        ns = "ns%d" % t
+        mms(sums(o, "OB", "mc", 256 * lo, 256 * hi), first=False)
+        tt(o, o, ("val", 192, 256), A.max)
+        tt(("t3", 0, 64), o, ("t2", 0, 64), A.min)
+        tt(("t4", 0, 32), ("t3", 0, 32), ("t3", 32, 64), A.min)
+        ci = ("ci", 0, 16)
+        tt(ci, ("t4", 0, 16), ("t4", 16, 32), A.min)
         dst = T.cores[(rank + 1 + t % 3) % len(T.cores)]
-        ts((ns, 0, 16), ("ci", 0, 16), 4095, A.bitwise_and)
-        i = send(t, "n", (ns, 0, 16), "nl%d" % t, dst, 900.0, 1500.0)
-        arrive(t, "n", "nl%d" % t, i, NET_N)
-        ts(("m1", 0, 16), ("ci", 0, 16), 4, A.arith_shift_right, 0x1F00, A.bitwise_and)
-        tt(("m2", 0, 16), ("m1", 0, 16), ("sl", 0, 16), A.add)
-        cp(("mu", 0, 16), ("m2", 0, 16))
-        gcp((AN, 768, 1024), (AB, 0, 5120), ("mu", 0, 16))
-        i = send(t, "z", (AN, 768, 1024), "zl%d" % t, dst, 900.0, 1700.0)
-        arrive(t, "z", "zl%d" % t, i, NET_Z)
+        cls[0] = "tn"
+        ts(("ni", 0, 16), ci, 4095, A.bitwise_and)
+        ts(("ns%d" % t, 0, 16), ("ni", 0, 16), 1184.0, A.add)
+        send(t, "n", ("ns%d" % t, 0, 16), (EN, 240, 256), dst)
+        cls[0] = "tz"
+        ts(("m1", 0, 16), ci, 8, A.arith_shift_right, 0x1FF0, A.bitwise_and)
+        ts(("mu", 0, 16), ("m1", 0, 16), ("pf", 0, 1), A.add)
+        gts(("hs%d" % t, 0, 256), (AB, 0, Z + 256), ("mu", 0, 16), 0.5)
+        send(t, "z", ("hs%d" % t, 0, 256), ("hl%d" % t, 0, 256), dst)
+        gact((AN, Z, Z + 256), (AB, 0, Z + 256), ("mu", 0, 16))
         if t == RO - 1:
-            dma("y", lambda: T.yz[:], lambda: T[AN][:, 768:1024], [(AN, 768, 1024)], [], 2000)
+            dma("y", [(T.yz[:], ap((AN, Z, Z + 256)))], [(AN, Z, Z + 256)], [], 2000)
+        cls[0] = "qu"
+        ts(("TH", 0, 16), ("m1", 0, 16), 1.0 / 256, A.mult, 128.53125, A.add)
+        ts(("TH", 16, 32), ("m1", 0, 16), 3840.0, A.is_lt, -0.5, A.add)
+        o = ("pU2", 0, 128, 1, 0, 32)
+        mms([(o, ("TH", 0, 32), IDr)])
+        act(("TT", 0, 128, 1, 0, 32), o, F.Copy, acc=("ac", 0, 1, 1, 0, 32) if t < RO - 1 else None)
+        tr = ("TT", 0, 128, 1, 0, 33)
+        mms([(("pU1", 0, 240), tr, ("QP", 0, 240, 1, 0, 33)), (("pU1", 256, 496), tr, ("QN", 0, 240, 1, 0, 33))])
+        tt(("y1", 0, 240), ("pU1", 0, 240), (EL, 0, 240), A.min)
+        tt(("pU1", 256, 496), ("pU1", 256, 496), (EL, 16, 256), A.min)
+        tt((EN, 0, 240), ("pU1", 256, 496), ("y1", 0, 240), A.max)
         cls[0] = "nt"
         if t < RO - 1:
-            ts(("g0", 0, 16), ("ci", 0, 16), 20480.0, A.is_ge)
-            mms([(("pU", 384, 400), ("one", 0, 128), ("g0", 0, 16), True, True)])
-            act(("gj", 0, 16), ("pU", 384, 400), F.Copy, acc=("ac", 0, 1))
-            cp(("ai", 0, 1), ("ac", 0, 1))
-            ts(("ap1", 0, 1), ("ai", 0, 1), 1, A.bitwise_and)
-            ts(("tb", 0, 1), ("ap1", 0, 1), -BIG, A.mult, -7.5 * BIG, A.add)
-            bias_mats()
-        cls[0] = "qu"
-        ts(("kp", 0, 16), ("ci", 0, 16), 12, A.arith_shift_right)
-        ts(("lt", 0, 16), ("ci", 0, 16), 20480.0, A.is_lt, 32.0, A.mult)
-        tt(("th", 0, 16), ("kp", 0, 16), ("lt", 0, 16), A.max)
-        act(("th", 16, 32), ("th", 0, 16), F.Copy)
-        act(("th", 32, 64), ("th", 0, 32), F.Copy)
-        for off, m, n in ((0, "IP", "IN"), (256, "IN", "IP")):
-            lst = []
-            for b in range(0, 256, 64):
-                o = ("pB", off + b, off + b + 64)
-                lst.append((o, (m, 0, 128), ("KC", b, b + 64), True, False))
-                lst.append((o, (n, 0, 128), ("th", 0, 64), False, True))
-            mms(lst)
-        tt(("y1", 0, 256), ("pB", 0, 256), (EB, 16, 272), A.min)
-        tt(("pB", 256, 512), ("pB", 256, 512), (EB, 0, 256), A.min)
-        tt((EN, 16, 32), ("pB", 256, 272), ("y1", 0, 16), A.max)
-        tt((EN, 48, 272), ("pB", 288, 512), ("y1", 32, 256), A.max)
-        act((EN, 0, 16), (EN, 256, 272), F.Copy)
+            o = ("pH", 0, 128, 1, 0, 1)
+            ac = ("ac", 0, 1, 1, 0, 32)
+            mms([const(o, -1, "1/4"), (o, ac, ("HF", 0, 128, 1, 0, 32))] + rounded(o, "m0") + [(o, ac, ("HF", 128, 256, 1, 0, 32))])
+            act(("BL", 0, 128, 1, 64, 65), o, F.Copy, scale=-2.0)
 
     cls[0] = "up"
-    nl = ("nl%d" % (RO - 1), 0, 16)
-    EB = "EB%d" % (RO % 2)
-    D = ("DD", 0, 4096)
-    ts(("k1", 0, 16), nl, 15, A.bitwise_and)
-    tt(("k2", 0, 16), ("k1", 0, 16), ("sl16", 0, 16), A.add)
-    cp(("cu", 0, 16), ("k2", 0, 16))
-    ts((EB, 32, 48), nl, 1184.0, A.add)
-    gtt(("ds", 0, 256), D, ("cu", 0, 16), ("zl%d" % (RO - 1), 0, 256), A.add)
-    ts(("dh", 0, 256), ("ds", 0, 256), 1, A.arith_shift_right)
-    scat(D, ("cu", 0, 16), ("dh", 0, 256))
-    dma("s", lambda: T.yd[:], lambda: T.DD[:], [D], [], 5000)
-    for k in range(16):
-        b = blk(k)
-        o, a = ("RT", k, 256, 16), (EB, 16 + 16 * b, 32 + 16 * b)
-        if k % 2:
-            act(o, a, F.Copy)
-        else:
-            cp(o, a)
-        ops[-1]["wr"] = [("RT", 3000 + k, 3001 + k)]
-    add("v", lambda e: e.transpose(T.XF[:, 0:256], T.RT[:, 0:256]), [("RT", 3000, 3016)], [("XF", 0, 256)], cost1(256, False))
+    rnd[0] = RO
+    update(RO - 1)
+    dma("s", [(T.yd[:], T.DD[:])], [D], [], 4500)
+    cls[0] = "end"
+    ts(("XE", 0, 256), ("EL%d" % RO, 0, 256), -1184.0, A.add)
     for b in range(8):
-        add("v", (lambda b: lambda e: e.tensor_scalar(T.YI[:, b], T.XF[:, 32 * b:32 * b + 32], -1184.0, None, A.add))(b),
-            [("XF", 32 * b, 32 * b + 32)], [("YI", 32 * b, 32 * b + 32)], cost1(32, False))
-        add("s", (lambda b: lambda e: e.activation(T.YJ[:, b], T.XF[:, 32 * b:32 * b + 32], F.Identity, bias=-1184.0))(b),
-            [("XF", 32 * b, 32 * b + 32)], [("YJ", 32 * b, 32 * b + 32), ("YJ", 1000 + 32 * b, 1032 + 32 * b)], 80 + CY * 64)
-    for gi in range(8):
-        o = gi ^ 1
-        h = gi % 2
-        dma("y", (lambda gi, o, h: lambda: T.YJ[16 * gi:16 * gi + 16, :, 16 * (1 - h):16 * (1 - h) + 16])(gi, o, h),
-            (lambda gi, o, h: lambda: T.YI[16 * o:16 * o + 16, :, 16 * h:16 * h + 16])(gi, o, h),
-            [("YI", 0, 256), ("YJ", 0, 256)], [("YJ", 2000 + gi, 2001 + gi)], 1900)
-    dma("y", lambda: T.ye[:], lambda: T.YJ[:], [("YJ", 0, 256), ("YJ", 2000, 2008)], [], 2000)
+        add("v", [(lambda b: lambda e: e.transpose(T.XF[:, b], ap(("XE", b, 256, 8))))(b)], [("XE", 0, 256)],
+            [("XF", 32 * b, 32 * b + 32)], ("fv", 64, 0, 0, 0))
+    dma("y", [(b, a) for a, b in halves(T.XF, T.ye)], [("XF", 0, 256)], [], 2000)
     return ops
 
 
@@ -542,73 +581,88 @@ def depend(ops):
     for i, op in enumerate(ops):
         need = set()
         for rw, regs in ((0, op["rd"]), (1, op["wr"])):
-            for name, lo, hi in regs:
+            for name, lo, hi, st, p0, p1 in regs:
                 bank = name in PSUM
-                for j, jw, jlo, jhi in hist.get(name, ()):
-                    if ((jw or rw) and jlo < hi and lo < jhi) or (bank and ops[j]["q"] != op["q"]):
+                for j, jw, jlo, jhi, q0, q1 in hist.get(name, ()):
+                    if ((jw or rw) and jlo < hi and lo < jhi and q0 < p1 and p0 < q1) or (bank and (ops[j]["q"] != op["q"] or op["q"] == "t")):
                         need.add(j)
-        for name, lo, hi in op["wr"]:
-            if name not in PSUM:
-                hist[name] = [x for x in hist.get(name, []) if not (lo <= x[2] and x[3] <= hi)]
+        for name, lo, hi, st, p0, p1 in op["wr"]:
+            if name not in PSUM and st == 1:
+                hist[name] = [x for x in hist.get(name, []) if not (lo <= x[2] and x[3] <= hi and p0 <= x[4] and x[5] <= p1)]
         for rw, regs in ((0, op["rd"]), (1, op["wr"])):
-            for name, lo, hi in regs:
-                hist.setdefault(name, []).append((i, rw, lo, hi))
-                if name in PSUM and len(hist[name]) > 160:
-                    hist[name] = hist[name][-160:]
+            for name, lo, hi, st, p0, p1 in regs:
+                h = hist.setdefault(name, [])
+                h.append((i, rw, lo, hi, p0, p1))
+                if name in PSUM:
+                    keep = sorted(set(x[0] for x in h))[-12:]
+                    hist[name] = [x for x in h if x[0] >= keep[0]]
         need.discard(i)
         deps.append(sorted(need))
     return deps
 
 
-def schedule(ops, deps):
+def schedule(ops, deps, P):
     n = len(ops)
+    cl = [cost(o, P) for o in ops]
+    pred = []
+    for j, op in enumerate(ops):
+        d = [(i, 0.0 if ops[i]["q"] == "t" == op["q"] else cl[i][1] + P["wake"]) for i in deps[j]]
+        pred.append(d + [(i, 0.0) for i in op["soft"]])
+    for q, seq in SEQ.items():
+        pool = {}
+        for i, op in enumerate(ops):
+            if op["q"] == q:
+                pool.setdefault((op["round"] + (op["cls"] in TAIL), op["cls"]), []).append(i)
+        chain = [pool[t, x].pop(0) for t in range(RO + 1) for x in seq if pool.get((t, x))]
+        for i, j in zip(chain, chain[1:]):
+            pred[j].append((i, 0.0))
     succ = [[] for _ in range(n)]
-    alld = []
-    for i in range(n):
-        d = list(deps[i])
-        if ops[i]["after"] is not None:
-            d.append(ops[i]["after"])
-        alld.append(d)
-        for j in d:
-            succ[j].append(i)
+    for j in range(n):
+        for i, x in pred[j]:
+            succ[i].append((j, x))
+    left = [len(d) for d in pred]
+    line = [i for i in range(n) if not left[i]]
+    for i in line:
+        for j, x in succ[i]:
+            left[j] -= 1
+            if not left[j]:
+                line.append(j)
+    assert len(line) == n
     pri = [0.0] * n
-    for i in range(n - 1, -1, -1):
-        m = 0.0
-        for j in succ[i]:
-            m = max(m, pri[j] + WAKE)
-        pri[i] = m + ops[i]["cost"] + ops[i]["lat"]
-    pri = [pri[i] + BONUS.get(ops[i]["cls"], 0.0) for i in range(n)]
-    left = [len(d) for d in alld]
+    for i in reversed(line):
+        pri[i] = cl[i][0] + max([pri[j] + x for j, x in succ[i]] + [cl[i][1]])
+    left = [len(d) for d in pred]
     est = [0.0] * n
     free = {}
     ready = {}
     for i in range(n):
-        if left[i] == 0:
+        if not left[i]:
             ready.setdefault(ops[i]["q"], []).append(i)
     order = []
-    start = [0.0] * n
     while len(order) < n:
         best = None
         for q, lst in ready.items():
-            if not lst:
-                continue
-            f = free.get(q, 0.0)
-            t0 = max(f, min(est[i] for i in lst))
-            c = max((i for i in lst if est[i] <= t0), key=lambda i: pri[i])
-            if best is None or (t0, -pri[c]) < best[0]:
-                best = ((t0, -pri[c]), q, c)
+            if lst:
+                t0 = max(free.get(q, 0.0), min(est[i] for i in lst))
+                c = max((i for i in lst if est[i] <= t0 + P["ahead"]), key=lambda i: pri[i] - 2 * max(0.0, est[i] - t0))
+                t0 = max(t0, est[c])
+                if best is None or (t0, -pri[c]) < best[0]:
+                    best = ((t0, -pri[c]), q, c)
         (t0, _p), q, c = best
         ready[q].remove(c)
-        start[c] = t0
         order.append(c)
-        free[q] = t0 + ops[c]["cost"]
-        for j in succ[c]:
-            e = t0 + ops[c]["cost"] + (0.0 if ops[j]["after"] == c else ops[c]["lat"] + WAKE)
-            est[j] = max(est[j], e)
+        free[q] = t0 + cl[c][0]
+        for j, x in succ[c]:
+            est[j] = max(est[j], free[q] + x)
             left[j] -= 1
-            if left[j] == 0:
+            if not left[j]:
                 ready.setdefault(ops[j]["q"], []).append(j)
-    return order, start, max(start[i] + ops[i]["cost"] + ops[i]["lat"] for i in range(n))
+    return order
+
+
+def plan(ops):
+    deps = depend(ops)
+    return deps, schedule(ops, deps, PLAN)
 
 
 def emit(g, T, ops, deps, order):
@@ -629,26 +683,29 @@ def emit(g, T, ops, deps, order):
             total[op["sem"]] = 16
             continue
         K = know[q]
-        ds = sorted(deps[i], key=lambda j: -sum(clock[j].values()))
-        for j in ds:
+        if q == "g" and op["kind"] == "c" and K.get("qg", 0) < count.get("qg", 0):
+            g.wait_ge(T.sem["qg"], count["qg"])
+            K["qg"] = waited["qg"] = count["qg"]
+        for j in sorted(deps[i], key=lambda j: -sum(clock[j].values())):
             s, v = token[j]
-            if K.get(s, 0) >= v:
+            if K.get(s, 0) >= v or (q == "t" and ops[j]["q"] == "t"):
                 continue
             eng[q].wait_ge(T.sem[s], v)
             waited[s] = max(waited.get(s, 0), v)
             for a, b in clock[j].items():
                 if K.get(a, 0) < b:
                     K[a] = b
-        ins = op["fn"](eng[q])
+        for fn in op["fn"]:
+            ins = fn(eng[q])
+            if op["kind"] == "dma":
+                ins.then_inc(T.sem[op["sem"]], 16)
         if op["kind"] == "c":
             s = qsem[q]
             count[s] = count.get(s, 0) + 1
             ins.then_inc(T.sem[s], 1)
             token[i] = (s, count[s])
         else:
-            if op["kind"] == "dma":
-                ins.then_inc(T.sem[op["sem"]], 16)
-            token[i] = (op["sem"], 16)
+            token[i] = (op["sem"], 16 * len(op["fn"]))
         total[token[i][0]] = token[i][1]
         c = dict(K)
         c[token[i][0]] = token[i][1]
@@ -662,6 +719,5 @@ def rank_program(g, core, T, topo):
     if T.rank_of(core) is None:
         return
     ops = build(T, core, topo)
-    deps = depend(ops)
-    order, start, span = schedule(ops, deps)
+    deps, order = plan(ops)
     emit(g, T, ops, deps, order)

@@ -21,15 +21,16 @@ C_LAST = (12, 16)
 B_V = ((1, 5), (5, 8), (8, 12), (12, 16))
 B_H = ((1, 8), (8, 16))
 G_CONV = ()
+SPLIT = False
 BANKS = ("pG", "pH", "pW", "pC", "pG", "pH", "pG", "pH", "pG", "pH")
 PIECES = ((1, 8), (8, 16))
 ORDER = ("abc", "ab")
 COUNTS = {"a": ((1, 8), (8, 16)), "b": ((1, 8), (8, 16)), "c": ((1, 8),)}
-SEQ = {"v": ("tl tl tl tl tn tz tn tz qu qu tz qu qu qu hs hs up hs hy hs up hy up hy a0 av0 av1 m0 am0 hc hy hc am1 hc hc cv0 hb0 cv1 "
-             "hb0 hb0 hb0 b0 b0 hb1 hb1 hb1 hb1 b1 b1 cl v0 v1 v0 ct ct").split(),
-       "s": ("tz qu hs zr li up ly zr nt as0 a0 av0 hc av1 as0 m0 hb0 as1 as0 as1 as1 sg0 sg0 hb1 sg1 cs0 sg1 cs1 cs0 cs1 v0 cs1 "
-             "v1").split(),
-       "t": ("tl qu hs qu hs nt hs up up as0 hc hc hc m0 hb0 as0 hb0 as1 as1 ca0 hb1 hb1 cb0 ca1 cs0 cs1 cc0 cs1 cb1 v0 ct v1").split()}
+SEQ = {"v": ("tl tl tl tl tn tz tn tz qu qu tz qu qu qu up hs hs hs hs up a0 av0 av1 m0 am0 hc hc am1 hc hc cv0 hb0 cv1 hb0 hb0 hb0 "
+             "b0 b0 hb1 hb1 hb1 hb1 b1 b1 cl v0 v1 v0 ct ct").split(),
+       "s": ("qu hs li up er zr er er up zr er nt er as0 a0 av0 hc av1 as0 m0 hb0 as1 as0 as1 as1 sg0 sg0 hb1 sg1 sg1 cs0 cs1 cs0 cs1 "
+             "v0 cs1 v1 late late late late late late late late late").split(),
+       "t": "tl qu qu hs up hs up up nt hc as0 hc m0 hb0 as0 hb0 as1 as1 ca0 hb1 hb1 ca1 cb0 cs0 cs1 cc0 cs1 v0 cb1 ct v1".split()}
 TAIL = ("tl", "tz", "tn", "qu", "nt")
 
 SCRATCH = {
@@ -47,13 +48,13 @@ SCRATCH = {
     "ID": ("sbuf", [128, 128], "bfloat16"), "nID": ("sbuf", [128, 128], "bfloat16"), "hID": ("sbuf", [128, 128], "bfloat16"),
     "I32": ("sbuf", [128, 128], "float32"), "nI32": ("sbuf", [128, 128], "float32"),
     "LV": ("sbuf", [128, 1600], "bfloat16"), "BL": ("sbuf", [128, 128], "bfloat16"), "CB": ("sbuf", [128, 1040], "bfloat16"),
-    "it": ("sbuf", [128, 256], "int32"), "iu": ("sbuf", [128, 256], "int32"), "kf": ("sbuf", [128, 256], "float32"),
-    "SL": ("sbuf", [128, 256], "bfloat16"), "nSL": ("sbuf", [128, 256], "bfloat16"),
-    "QP": ("sbuf", [128, 256], "bfloat16"), "QN": ("sbuf", [128, 256], "bfloat16"), "qc": ("sbuf", [128, 1], "float32"),
+    "zero": ("sbuf", [128, 256], "bfloat16"), "kf": ("sbuf", [128, 256], "float32"),
+    "SL": ("sbuf", [128, 256], "float32"),
+    "QP": ("sbuf", [128, 256], "bfloat16"), "QN": ("sbuf", [128, 256], "bfloat16"),
     "HF": ("sbuf", [128, 256], "float32"), "CL": ("sbuf", [128, 128], "bfloat16"), "CR": ("sbuf", [128, 16], "bfloat16"),
     "pi": ("sbuf", [128, 1], "int32"), "pj": ("sbuf", [128, 1], "int32"), "pf": ("sbuf", [128, 1], "float32"),
     "ER": ("sbuf", [128, 2, 256], "float32"),
-    "VA": ("sbuf", [128, 256], "bfloat16"), "VC": ("sbuf", [128, 256], "bfloat16"),
+    "VA": ("sbuf", [128, 128], "float32"), "VC": ("sbuf", [128, 128], "float32"),
     "xa": ("sbuf", [128, 256], "int32"), "na": ("sbuf", [128, 256], "int32"), "ua": ("sbuf", [128, 256], "uint16"),
     "xc": ("sbuf", [128, 256], "int32"), "nc": ("sbuf", [128, 256], "int32"), "uc": ("sbuf", [128, 256], "uint16"),
     "xb": ("sbuf", [128, 256], "int32"), "nb": ("sbuf", [128, 256], "int32"), "ub": ("sbuf", [128, 256], "uint16"),
@@ -62,7 +63,7 @@ SCRATCH = {
     "m1": ("sbuf", [128, 16], "int32"), "mu": ("sbuf", [128, 16], "uint16"), "ni": ("sbuf", [128, 16], "int32"),
     "TH": ("sbuf", [128, 32], "bfloat16"), "TT": ("sbuf", [128, 128], "bfloat16"), "ac": ("sbuf", [128, 1], "float32"),
     "y1": ("sbuf", [128, 256], "float32"), "cu": ("sbuf", [128, 16], "uint16"), "DG": ("sbuf", [128, 256], "bfloat16"),
-    "dh": ("sbuf", [128, 256], "int32"),
+    "dh": ("sbuf", [128, 256], "bfloat16"),
 }
 PSUM = ("pR1", "pR2", "pC", "pW", "pU1", "pU2", "pG", "pH")
 for _p in PSUM:
@@ -71,15 +72,14 @@ for _t in range(RO + 1):
     SCRATCH["EL%d" % _t] = ("sbuf", [128, 2, 256], "float32")
 for _t in range(RO):
     SCRATCH["hl%d" % _t] = ("sbuf", [128, 256], "bfloat16")
-    SCRATCH["hs%d" % _t] = ("sbuf", [128, 256], "bfloat16")
     SCRATCH["ns%d" % _t] = ("sbuf", [128, 16], "float32")
 SEMAPHORES = ["qv", "qs", "qt", "qg"]
 for _t in range(RO):
     SEMAPHORES += ["an%d" % _t, "az%d" % _t, "ln%d" % _t, "lz%d" % _t]
 SEMAPHORES += ["dm%d" % _i for _i in range(24)]
 
-PLAN = {"f": 1.1, "G": 1.56, "SC": 3.8, "wake": 60.0, "issue": 700.0, "net_n": 2000.0, "net_z": 2300.0, "fv": 55.0, "fs": 70.0,
-        "ft": 40.0, "mm": 5.0, "ahead": 300.0}
+PLAN = {"f": 1.15, "G": 1.56, "SC": 3.8, "wake": 60.0, "issue": 400.0, "net_n": 1500.0, "net_z": 1700.0, "fv": 55.0, "fs": 70.0,
+        "ft": 40.0, "mm": 5.0, "ahead": 300.0, "early": 5000.0}
 
 
 def cost(op, P):
@@ -147,9 +147,8 @@ def build(T, core, topo):
         add("v", [lambda e: e.tensor_tensor(ap(o), ap(win).indirect(ap(off)), ap(b), op)], [win, off, b], [o],
             ("fv", 0, width(o), 0, 0))
 
-    def gts(o, win, off, s):
-        add("v", [lambda e: e.tensor_scalar(ap(o), ap(win).indirect(ap(off)), s, None, A.mult)], [win, off], [o],
-            ("fv", 0, width(o), 0, 0))
+    def gcp(o, win, off):
+        add("v", [lambda e: e.tensor_copy(ap(o), ap(win).indirect(ap(off)))], [win, off], [o], ("fv", 0, width(o), 0, 0))
 
     def scat(win, off, a):
         add("v", [lambda e: e.tensor_copy(ap(win).indirect(ap(off)), ap(a))], [off, a], [win], ("fv", 0, 0, width(a), 0))
@@ -165,6 +164,10 @@ def build(T, core, topo):
                 k["accum_out"] = ap(acc)
             return e.activation(ap(o), ap(a), func, **k)
         add("s", [fn], [a], [o] + ([acc] if acc is not None else []), ("fs", max(64, width(o)), 0, 0, 0))
+
+    def sfill(o, c):
+        o = full(o)
+        act(o, ("one", 0, width(o), 1, o[4], o[5]), F.Copy, scale=c)
 
     def gact(o, win, off):
         add("s", [lambda e: e.activation(ap(o), ap(win).indirect(ap(off)), F.Copy)], [win, off], [o], ("fs", 0, width(o), 0, 0))
@@ -186,12 +189,13 @@ def build(T, core, topo):
 
     lv = {}
 
-    def row(name, n, value, second=None):
+    def row(name, n, value, second=None, put=fill):
         c = sum(v[1] for v in lv.values())
         lv[name] = (c, n)
         if second is not None:
-            fill(("LV", c, c + n, 1, 0, 2), second)
-        fill(("LV", c, c + n, 1, 0, 1), value)
+            put(("LV", c, c + n, 1, 0, 2), second)
+        if second != value:
+            put(("LV", c, c + n, 1, 0, 1), value)
 
     def const(o, sign, name, n=None, rows=1, at=0):
         c = lv[name][0] + at
@@ -202,7 +206,7 @@ def build(T, core, topo):
         return [const(o, 1, name), const(o, -1, name)]
 
     def gop(fn, rd, wr, n, fix=170.0):
-        add("g", [fn], rd, wr, (fix, 2 * n, 0, 0, 0))
+        add("g", [fn], rd, wr, (fix + 300.0, 2 * n, 0, 0, 0))
 
     def iota(o, pattern, base, cm):
         if SCRATCH[o[0]][2] == "int32":
@@ -212,6 +216,15 @@ def build(T, core, topo):
 
     def select(o, a, pattern, op, base, cm):
         gop(lambda e: e.affine_select(ap(o), ap(a), pattern, op, 0.0, base, cm), [a], [o], width(o))
+
+    def gfill(o, c):
+        o = full(o)
+        a = ("kf" if SCRATCH[o[0]][2] == "float32" else "one", 0, width(o), 1, o[4], o[5])
+        gop(lambda e: e.affine_select(ap(o), ap(a), [[0, width(o)]], A.is_gt, c, 0, 0), [a], [o], width(o))
+
+    def diagonal(o, c, n, base=0):
+        a = ("zero", 0, width(o), 1, o[4], o[5])
+        gop(lambda e: e.affine_select(ap(o), ap(a), [[0, width(o) // n], [-1, n]], A.not_equal, c, base, 1), [a], [o], width(o))
 
     def dma(q, pairs, rd, wr, lat):
         s = "dm%d" % ndma[0]
@@ -231,15 +244,15 @@ def build(T, core, topo):
     Z = 4096
 
     def halves(lay, flat):
-        return [(lay[32 * a + l:32 * a + 32:2, :, 16 * h:16 * h + 16], flat[32 * a + 16 * h:32 * a + 16 * h + 16, 128 * l:128 * l + 128])
-                for a in range(4) for h in range(2) for l in range(2)]
+        return [(lay[32 * a:32 * a + 32, :, 16 * h:16 * h + 16], flat[32 * a + 16 * h:32 * a + 16 * h + 16, :])
+                for a in range(4) for h in range(2)]
 
     cls[0] = "ld"
     dma("y", [(T.wti[:, 0:1], T.wt[:, 0:1])], [], [("wti", 0, 1)], 1900)
     dma("y", [(T.AB0[:, Z:Z + 256], T.zv[:])], [], [("AB0", Z, Z + 256)], 2000)
     pr = halves(T.XJ, T.ef)
-    dma("y", pr[:8], [], [("XJ", 0, 256, 1, 0, 64)], 2000)
-    dma("s", pr[8:], [], [("XJ", 0, 256, 1, 64, 128)], 2000)
+    dma("y", pr[:4], [], [("XJ", 0, 256, 1, 0, 64)], 2000)
+    dma("s", pr[4:], [], [("XJ", 0, 256, 1, 64, 128)], 2000)
     dma("s", [(T.DD[:], T.dv[:])], [], [D], 4500)
     cls[0] = "-"
     fill(("on8", 0, 8), 1.0)
@@ -248,48 +261,50 @@ def build(T, core, topo):
     select(("b8a", 0, 8), ("on8", 0, 8), [[-16, 8]], A.is_ge, 0, 1)
     select(("b8", 0, 8), ("b8a", 0, 8), [[16, 8]], A.is_ge, 15, -1)
     select(IDr, ("one", 0, 128), [[-1, 128]], A.is_equal, 0, 1)
-    iota(("it", 0, 256, 1, 0, 32), [[0, 16], [-1, 16]], 0, 1)
+    fill(("zero", 0, 256), 0.0)
     iota(("kf", 0, 256), [[1, 16], [0, 16]], 0, 0)
     iota(("pi", 0, 1), [[0, 1]], 0, 1)
+    zero_first = len(ops)
     cp(("wtf", 0, 1), ("wti", 0, 1))
-    fill(("OB", 0, 144), 0.0)
-    ts(("OB", 15, 143, 16), ("b8", 0, 8), W1, A.mult)
-    ts(("O8", 0, 8), ("b8", 0, 8), W1, A.mult)
+    sfill(("OB", 0, 144), 0.0)
+    act(("OB", 15, 143, 16), ("b8", 0, 8), F.Copy, scale=W1)
+    act(("O8", 0, 8), ("b8", 0, 8), F.Copy, scale=W1)
     ts(("W16", 0, 8), ("b8", 0, 8), ("wtf", 0, 1), A.mult)
     ts(("W16", 8, 16), ("b8", 0, 8), ("wtf", 0, 1), A.mult, -1.0, A.mult)
-    ts(("W16", 16, 24), ("b8", 0, 8), ("wtf", 0, 1), A.mult)
     act(nIDr, IDr, F.Copy, scale=-1.0)
-    act(("hID", 0, 128), IDr, F.Copy, scale=0.5)
     act(("I32", 0, 128), IDr, F.Copy)
     act(("nI32", 0, 128), IDr, F.Copy, scale=-1.0)
     row("rb", 128, -2048.0, 0.5)
-    row("rz", 128, 0.0, 0.0)
     row("m1", 128, magic(4096))
-    row("m2", 128, magic(64))
-    row("rn", 128, -magic(64), 2048.0)
     for j in range(3):
-        row("u%d" % j, 128, magic(UNITS[j]))
-    row("m16", 16, magic(16))
-    row("7.5", 16, 7.5)
-    row("1/4", 256, 0.25)
-    row("m0", 128, magic(1))
-    ts(("iu", 0, 256, 1, 0, 32), ("it", 0, 256, 1, 0, 32), 15, A.bitwise_and)
-    ts(("SL", 0, 256, 1, 0, 32), ("iu", 0, 256, 1, 0, 32), 0.0, A.is_equal)
-    act(("nSL", 0, 256, 1, 0, 16), ("SL", 0, 256, 1, 0, 16), F.Copy, scale=-1.0)
+        row("u%d" % j, 128, magic(UNITS[j]), put=sfill)
+    cls[0] = "late"
+    row("m16", 16, magic(16), put=sfill)
+    row("7.5", 16, 7.5, put=sfill)
+    row("1/4", 256, 0.25, put=sfill)
+    row("m0", 256, magic(1), put=sfill)
+    act(("hID", 0, 128), IDr, F.Copy, scale=0.5)
+    sfill(("TT", 0, 128, 1, 32, 64), 1.0)
+    sfill(("HF", 0, 128, 1, 0, 16), 0.5)
+    sfill(("HF", 128, 256, 1, 0, 16), -0.5)
+    cls[0] = "-"
+    diagonal(("SL", 0, 256, 1, 0, 16), 1.0, 16)
     ts(("pj", 0, 1), ("pi", 0, 1), 15, A.bitwise_and)
     cp(("pf", 0, 1), ("pj", 0, 1))
     fill(("BL", 0, 128, 1, 0, 64), 0.0)
     fill(("BL", 0, 128, 1, 64, 128), 1.0)
     fill(("BL", 0, 128, 1, 64, 65), 0.0)
-    fill(("CB", 0, 1040), 0.0)
     CA, CC, CBB, CK, C0 = 0, 256, 512, 768, 1024
+    ops[zero_first]["soft"].append(len(ops))
+    fill(("CB", 0, 1024), 0.0)
 
     def bias(c0, lo, hi, par, one, sg=None):
         r = ("CB", c0 + 16 * lo, c0 + 16 * hi)
-        fill(on(r, 64, 66), one)
-        fill(on(r, 64, 65), par)
+        put = sfill if c0 in (CA, C0) else gfill
+        put(on(r, 64, 66), one)
+        put(on(r, 64, 65), par)
         if sg is not None:
-            act(on(r, 0, 16), ("SL", 16 * lo, 16 * hi, 1, 0, 16), F.Copy, scale=sg)
+            diagonal(on(r, 0, 16), sg, 16)
 
     def runs(lst):
         out = []
@@ -310,22 +325,19 @@ def build(T, core, topo):
     for lo, hi, (q, u) in kinds("b", [(1, 16, "v")]):
         bias(CBB, lo, hi, -W1, -7.5 * W1, u / 2)
     bias(C0, 0, 1, -2 * W1, -15 * W1)
-    ts(("CB", CK, CK + 256, 1, 64, 66), ("kf", 0, 256, 1, 64, 66), -1.0, A.add, 65536.0, A.mult)
+    act(("CB", CK, CK + 256, 1, 64, 66), ("kf", 0, 256, 1, 64, 66), F.Identity, bias=-65536.0, scale=65536.0)
     bias(CK, 0, 1, 0.0, 15.5 * 65536, -32768.0)
-    fill(("CB", CK, CK + 256, 1, 64, 65), 0.0)
+    gfill(("CB", CK, CK + 256, 1, 64, 65), 0.0)
     iota(("CB", CK, CK + 256, 1, 96, 97), [[0, 16], [4096, 16]], 0, 0)
-    fill(("qc", 0, 1, 1, 0, 32), 33 * SQ)
-    fill(("qc", 0, 1, 1, 0, 16), SQ)
-    ts(("QP", 0, 256, 1, 0, 32), ("SL", 0, 256, 1, 0, 32), ("qc", 0, 1, 1, 0, 32), A.mult)
-    ts(("QP", 0, 256, 1, 32, 33), ("kf", 0, 256, 1, 32, 33), 145.0, A.add, -SQ, A.mult)
+    diagonal(("QP", 0, 256, 1, 0, 32), SQ, 16, -16)
+    diagonal(("QP", 0, 256, 1, 0, 16), 33 * SQ, 16)
+    iota(("QP", 0, 256, 1, 32, 33), [[-int(SQ), 16], [0, 16]], -145 * int(SQ), 0)
+    cls[0] = "late"
     act(("QN", 0, 256, 1, 0, 33), ("QP", 0, 256, 1, 0, 33), F.Copy, scale=-1.0)
-    fill(("TT", 0, 128, 1, 32, 64), 1.0)
-    fill(("HF", 0, 128, 1, 0, 32), 0.5)
-    fill(("HF", 128, 256, 1, 0, 32), -0.5)
-    fill(("HF", 0, 256, 1, 0, 16), 0.0)
+    cls[0] = "-"
     iota(("CL", 0, 128, 1, 0, 2), [[0, 8], [16, 16]], 0, 0)
-    fill(("CL", 0, 128, 1, 0, 1), 1.0)
-    fill(("CR", 0, 16, 1, 0, 2), 1.0)
+    gfill(("CL", 0, 128, 1, 0, 1), 1.0)
+    gfill(("CR", 0, 16, 1, 0, 2), 1.0)
     iota(("CR", 0, 16, 1, 0, 1), [[256, 16]], 0, 0)
     cls[0] = "ld"
     add("v", [lambda e: e.tensor_scalar(T.XF[:], T.XJ[:], 1184.0, None, A.add)], [("XJ", 0, 256)], [("XF", 0, 256)], ("fv", 256, 0, 0, 0))
@@ -334,13 +346,12 @@ def build(T, core, topo):
             [("EL0", 1000 + b, 1001 + b)], ("fv", 64, 0, 0, 0))
 
     def spread(buf, col, evac, n):
-        HL, H = ("pW", 0, 256, 1, 0, 16), ("pW", 0, 128, 1, 0, 16)
-        mms([const(HL, 1, "rb", rows=2)], last=False)
-        mms(sums_t("pW", 0, 256, buf, col, ("W16", 0, 16)) + rounded(HL, "m1"), first=False, last=False)
-        mms(sums_t("pW", 0, 256, buf, col, ("W16", 8, 24)) + [const(H, 1, "m2"), const(H, 1, "rn", rows=2)], first=False)
-        act((evac, 0, 256, 1, 0, 16), HL, F.Copy)
+        H = ("pW", 0, 128, 1, 0, 16)
+        mms([const(H, -1, "rb", rows=2)], last=False)
+        mms(sums_t("pW", 0, 128, buf, col, ("W16", 8, 16)) + rounded(H, "m1") + sums_t("pW", 0, 128, buf, col, ("W16", 0, 8)), first=False)
+        act((evac, 0, 128, 1, 0, 16), H, F.Identity, bias=-2048.0)
         o = ("pW", 256, 256 + n)
-        mms([(o, (evac, 0, 128, 1, 0, 16), ("nSL", 0, n, 1, 0, 16)), (o, (evac, 128, 256, 1, 0, 16), ("SL", 0, n, 1, 0, 16))])
+        mms([(o, (evac, 0, 128, 1, 0, 16), ("SL", 0, n, 1, 0, 16))])
         return o
 
     def hashed(v, el, c, d, x, n, u):
@@ -376,8 +387,10 @@ def build(T, core, topo):
         gact(("DG", 0, 256), D, ("cu", 0, 16))
         o = ("pG", 0, 256)
         mms([const(o, -1, "1/4")], last=False)
-        mms([(o, ("hID", 0, 128), ("DG", 0, 256))], first=False)
-        tt(("dh", 0, 256), o, ("hl%d" % t, 0, 256), A.add)
+        mms([(o, ("hID", 0, 128), ("DG", 0, 256))], first=False, last=False)
+        ops[-1]["cls"] = cls[0]
+        mms([(o, ("hID", 0, 128), ("hl%d" % t, 0, 256))] + rounded(o, "m0"), first=False)
+        act(("dh", 0, 256), o, F.Copy)
         scat(D, ("cu", 0, 16), ("dh", 0, 256))
 
     for t in range(RO):
@@ -388,7 +401,7 @@ def build(T, core, topo):
         def blk(lo, hi):
             return (AB, 256 * (lo - 1), 256 * (hi - 1)) if lo else (AB, 3840, 4096)
         cls[0] = "hs"
-        cut = ((0, 240), (240, 256)) if t else ((0, 256),)
+        cut = ((0, 240), (240, 256)) if t and SPLIT else ((0, 256),)
         for c, d in cut:
             cls[0] = "li" if c == 0 else "ly"
             act((EL, 256 + c, 256 + d), (EL, c, d), F.Identity, bias=C2, scale=2080.0)
@@ -415,9 +428,9 @@ def build(T, core, topo):
             m = min(m, 256 - to)
             if m <= 0:
                 break
-            gop((lambda src, lo, to, m: lambda e: e.affine_select(T.ER[:, :, to:to + m], T[src][:, :, lo:lo + m], [[0, 2 * m]], A.is_gt,
-                                                                 0.0, 1, 0))(src, lo, to, m),
-                [(src, lo, lo + m), (src, 256 + lo, 256 + lo + m)], [("ER", to, to + m), ("ER", 256 + to, 256 + to + m)], 2 * m)
+            add("s", [(lambda src, lo, to, m: lambda e: e.activation(T.ER[:, :, to:to + m], T[src][:, :, lo:lo + m], F.Copy))(src, lo, to, m)],
+                [(src, lo, lo + m), (src, 256 + lo, 256 + lo + m)], [("ER", to, to + m), ("ER", 256 + to, 256 + to + m)],
+                ("fs", max(64, 2 * m), 0, 0, 0))
             if src == "ER":
                 n *= 2
             src = "ER"
@@ -539,14 +552,13 @@ def build(T, core, topo):
         cls[0] = "tz"
         ts(("m1", 0, 16), ci, 8, A.arith_shift_right, 0x1FF0, A.bitwise_and)
         ts(("mu", 0, 16), ("m1", 0, 16), ("pf", 0, 1), A.add)
-        gts(("hs%d" % t, 0, 256), (AB, 0, Z + 256), ("mu", 0, 16), 0.5)
-        send(t, "z", ("hs%d" % t, 0, 256), ("hl%d" % t, 0, 256), dst)
-        gact((AN, Z, Z + 256), (AB, 0, Z + 256), ("mu", 0, 16))
+        gcp((AN, Z, Z + 256), (AB, 0, Z + 256), ("mu", 0, 16))
+        send(t, "z", (AN, Z, Z + 256), ("hl%d" % t, 0, 256), dst)
         if t == RO - 1:
             dma("y", [(T.yz[:], ap((AN, Z, Z + 256)))], [(AN, Z, Z + 256)], [], 2000)
         cls[0] = "qu"
-        ts(("TH", 0, 16), ("m1", 0, 16), 1.0 / 256, A.mult, 128.53125, A.add)
-        ts(("TH", 16, 32), ("m1", 0, 16), 3840.0, A.is_lt, -0.5, A.add)
+        ts(("TH", 16, 32), ("m1", 0, 16), 1.0 / 256, A.mult, 128.53125, A.add)
+        ts(("TH", 0, 16), ("m1", 0, 16), 3840.0, A.is_lt, -0.5, A.add)
         o = ("pU2", 0, 128, 1, 0, 32)
         mms([(o, ("TH", 0, 32), IDr)])
         act(("TT", 0, 128, 1, 0, 32), o, F.Copy, acc=("ac", 0, 1, 1, 0, 32) if t < RO - 1 else None)
@@ -558,8 +570,8 @@ def build(T, core, topo):
         cls[0] = "nt"
         if t < RO - 1:
             o = ("pH", 0, 128, 1, 0, 1)
-            ac = ("ac", 0, 1, 1, 0, 32)
-            mms([const(o, -1, "1/4"), (o, ac, ("HF", 0, 128, 1, 0, 32))] + rounded(o, "m0") + [(o, ac, ("HF", 128, 256, 1, 0, 32))])
+            ac = ("ac", 0, 1, 1, 0, 16)
+            mms([const(o, -1, "1/4"), (o, ac, ("HF", 0, 128, 1, 0, 16))] + rounded(o, "m0") + [(o, ac, ("HF", 128, 256, 1, 0, 16))])
             act(("BL", 0, 128, 1, 64, 65), o, F.Copy, scale=-2.0)
 
     cls[0] = "up"
@@ -571,7 +583,9 @@ def build(T, core, topo):
     for b in range(8):
         add("v", [(lambda b: lambda e: e.transpose(T.XF[:, b], ap(("XE", b, 256, 8))))(b)], [("XE", 0, 256)],
             [("XF", 32 * b, 32 * b + 32)], ("fv", 64, 0, 0, 0))
-    dma("y", [(b, a) for a, b in halves(T.XF, T.ye)], [("XF", 0, 256)], [], 2000)
+    pr = [(b, a) for a, b in halves(T.XF, T.ye)]
+    dma("y", pr[:4], [("XF", 0, 256)], [], 2000)
+    dma("s", pr[4:], [("XF", 0, 256)], [], 2000)
     return ops
 
 
@@ -631,6 +645,7 @@ def schedule(ops, deps, P):
     pri = [0.0] * n
     for i in reversed(line):
         pri[i] = cl[i][0] + max([pri[j] + x for j, x in succ[i]] + [cl[i][1]])
+    pri = [x + (P["early"] if op["cls"] == "-" else 0.0) for x, op in zip(pri, ops)]
     left = [len(d) for d in pred]
     est = [0.0] * n
     free = {}

import numpy as np
from concourse.mybir import dt, AluOpType, AxisListType, ActivationFunctionType

RO = 6
W1 = 2.0 ** 23
UNITS = (256 * W1, 128 * W1, 64 * W1)
SQ = 2.0 ** 14
C2 = -6722560.0


def magic(step):
    return 1.5 * 2.0 ** 23 * step


A_V = ((1, 5, "v"), (5, 8, "v"))
A_S = ((8, 12, "s"), (12, 16, "s"))
C_V = ((1, 5), (5, 6))
C_S = ((6, 8), (8, 12))
C_LATE = (8, 12)
C_LAST = (12, 16)
B_V = ((1, 5), (5, 8), (8, 12), (12, 16))
B_H = ((1, 8), (8, 16))
G_CONV = ()
SPLIT = False
BANKS = ("pG", "pH", "pW", "pC", "pG", "pH", "pG", "pH", "pG", "pH")
PIECES = ((1, 8), (8, 16))
ORDER = ("abc", "ab")
COUNTS = {"a": ((1, 8), (8, 16)), "b": ((1, 8), (8, 16)), "c": ((1, 8),)}
SEQ = {"v": ("tl tl tl tl tn tz tn tz qu qu tz qu qu qu up hs hs hs hs up a0 av0 av1 m0 am0 hc hc am1 hc hc cv0 hb0 cv1 hb0 hb0 hb0 "
             "b0 b0 hb1 hb1 hb1 hb1 b1 b1 cl v0 v1 v0 ct ct").split(),
       "s": ("qu hs li up er zr er er up zr er nt er as0 a0 av0 hc av1 as0 m0 hb0 as1 as0 as1 as1 sg0 sg0 hb1 sg1 sg1 cs0 cs1 cs0 cs1 "
             "v0 cs1 v1 late late late late late late late late late").split(),
       "t": "tl qu qu hs up hs up up nt hc as0 hc m0 hb0 as0 hb0 as1 as1 ca0 hb1 hb1 ca1 cb0 cs0 cs1 cc0 cs1 v0 cb1 ct v1".split()}
TAIL = ("tl", "tz", "tn", "qu", "nt")

SCRATCH = {
    "XJ": ("sbuf", [128, 8, 32], "int32"), "XF": ("sbuf", [128, 8, 32], "float32"), "XE": ("sbuf", [128, 256], "float32"),
    "wti": ("sbuf", [128, 1], "int32"), "wtf": ("sbuf", [128, 1], "float32"),
    "DD": ("sbuf", [128, 4096], "bfloat16"),
    "AB0": ("sbuf", [128, 5120], "bfloat16"), "AB1": ("sbuf", [128, 5120], "bfloat16"),
    "ZR": ("sbuf", [128, 1024], "bfloat16"), "df": ("sbuf", [128, 4096], "bfloat16"),
    "ma": ("sbuf", [128, 4096], "bfloat16"), "mb": ("sbuf", [128, 4096], "bfloat16"), "mc": ("sbuf", [128, 4096], "bfloat16"),
    "dg": ("sbuf", [128, 4096], "bfloat16"), "dc": ("sbuf", [128, 4096], "bfloat16"),
    "on8": ("sbuf", [128, 8], "float32"), "b8a": ("sbuf", [128, 8], "float32"), "b8": ("sbuf", [128, 8], "float32"),
    "OB": ("sbuf", [128, 144], "bfloat16"), "UT": ("sbuf", [128, 512], "float32"), "AT": ("sbuf", [128, 256], "bfloat16"),
    "W16": ("sbuf", [128, 24], "bfloat16"), "O8": ("sbuf", [128, 8], "bfloat16"),
    "one": ("sbuf", [128, 256], "bfloat16"), "neg": ("sbuf", [128, 128], "bfloat16"),
    "ID": ("sbuf", [128, 128], "bfloat16"), "nID": ("sbuf", [128, 128], "bfloat16"), "hID": ("sbuf", [128, 128], "bfloat16"),
    "I32": ("sbuf", [128, 128], "float32"), "nI32": ("sbuf", [128, 128], "float32"),
    "LV": ("sbuf", [128, 1600], "bfloat16"), "BL": ("sbuf", [128, 128], "bfloat16"), "CB": ("sbuf", [128, 1040], "bfloat16"),
    "zero": ("sbuf", [128, 256], "bfloat16"), "kf": ("sbuf", [128, 256], "float32"),
    "SL": ("sbuf", [128, 256], "float32"),
    "QP": ("sbuf", [128, 256], "bfloat16"), "QN": ("sbuf", [128, 256], "bfloat16"),
    "HF": ("sbuf", [128, 256], "float32"), "CL": ("sbuf", [128, 128], "bfloat16"), "CR": ("sbuf", [128, 16], "bfloat16"),
    "pi": ("sbuf", [128, 1], "int32"), "pj": ("sbuf", [128, 1], "int32"), "pf": ("sbuf", [128, 1], "float32"),
    "ER": ("sbuf", [128, 2, 256], "float32"),
    "VA": ("sbuf", [128, 128], "float32"), "VC": ("sbuf", [128, 128], "float32"),
    "xa": ("sbuf", [128, 256], "int32"), "na": ("sbuf", [128, 256], "int32"), "ua": ("sbuf", [128, 256], "uint16"),
    "xc": ("sbuf", [128, 256], "int32"), "nc": ("sbuf", [128, 256], "int32"), "uc": ("sbuf", [128, 256], "uint16"),
    "xb": ("sbuf", [128, 256], "int32"), "nb": ("sbuf", [128, 256], "int32"), "ub": ("sbuf", [128, 256], "uint16"),
    "val": ("sbuf", [128, 256], "float32"), "t1": ("sbuf", [128, 64], "float32"), "t2": ("sbuf", [128, 64], "float32"),
    "t3": ("sbuf", [128, 64], "float32"), "t4": ("sbuf", [128, 32], "float32"), "ci": ("sbuf", [128, 16], "int32"),
    "m1": ("sbuf", [128, 16], "int32"), "mu": ("sbuf", [128, 16], "uint16"), "ni": ("sbuf", [128, 16], "int32"),
    "TH": ("sbuf", [128, 32], "bfloat16"), "TT": ("sbuf", [128, 128], "bfloat16"), "ac": ("sbuf", [128, 1], "float32"),
    "y1": ("sbuf", [128, 256], "float32"), "cu": ("sbuf", [128, 16], "uint16"), "DG": ("sbuf", [128, 256], "bfloat16"),
    "dh": ("sbuf", [128, 256], "bfloat16"),
}
PSUM = ("pR1", "pR2", "pC", "pW", "pU1", "pU2", "pG", "pH")
for _p in PSUM:
    SCRATCH[_p] = ("psum", [128, 512], "float32")
for _t in range(RO + 1):
    SCRATCH["EL%d" % _t] = ("sbuf", [128, 2, 256], "float32")
for _t in range(RO):
    SCRATCH["hl%d" % _t] = ("sbuf", [128, 256], "bfloat16")
    SCRATCH["ns%d" % _t] = ("sbuf", [128, 16], "float32")
SEMAPHORES = ["qv", "qs", "qt", "qg"]
for _t in range(RO):
    SEMAPHORES += ["an%d" % _t, "az%d" % _t, "ln%d" % _t, "lz%d" % _t]
SEMAPHORES += ["dm%d" % _i for _i in range(24)]

PLAN = {"f": 1.15, "G": 1.56, "SC": 3.8, "wake": 60.0, "issue": 400.0, "net_n": 1500.0, "net_z": 1700.0, "fv": 55.0, "fs": 70.0,
        "ft": 40.0, "mm": 5.0, "ahead": 300.0, "early": 5000.0}


def cost(op, P):
    fix, cyc, ga, sc, te = op["c"]
    fix = P.get(fix, fix) + (P["mm"] * len(op["fn"]) if op["q"] == "t" else 0.0)
    return fix + P["f"] * (0.83 * (cyc + P["G"] * ga + P["SC"] * sc) + 0.42 * te), P.get(op["lat"], op["lat"])


def build(T, core, topo):
    A = AluOpType
    F = ActivationFunctionType
    rank = T.rank_of(core)
    ops = []
    ndma = [0]
    cls = ["-"]
    rnd = [0]

    def full(r):
        return (tuple(r) + (1, 0, 128)[len(r) - 3:]) if len(r) < 6 else r

    def on(r, p0, p1):
        return full(r)[:4] + (p0, p1)

    def ap(r):
        b, lo, hi, st, p0, p1 = full(r)
        sh = SCRATCH[b][1]
        if len(sh) == 3:
            pl = lo // sh[2]
            return T[b][p0:p1, pl, lo - pl * sh[2]:hi - pl * sh[2]:st]
        return T[b][p0:p1, lo:hi:st]

    def add(q, fn, rd, wr, c, kind="c", lat=0.0, sem=None, after=None):
        ops.append({"q": q, "fn": fn, "rd": [full(r) for r in rd], "wr": [full(r) for r in wr], "c": c, "kind": kind,
                    "lat": lat, "sem": sem, "after": after, "cls": cls[0], "round": rnd[0], "soft": [] if after is None else [after]})
        return len(ops) - 1

    def width(r):
        return len(range(*full(r)[1:4]))

    def cyc(o, *rs):
        two = all(r[0] not in PSUM and SCRATCH[r[0]][2] in ("bfloat16", "uint16") for r in (o,) + rs)
        return ("fv", max(64, width(o) * (0.5 if two else 1.0)), 0, 0, 0)

    def tt(o, a, b, op):
        f = 1 if (a[0] in PSUM or b[0] in PSUM) else 2
        add("v", [lambda e: e.tensor_tensor(ap(o), ap(a), ap(b), op)], [a, b], [o], ("fv", max(64, f * width(o)), 0, 0, 0))

    def ts(o, a, s1, op0, s2=None, op1=None):
        cols = [s for s in (s1, s2) if isinstance(s, tuple)]

        def fn(e):
            x, y = [ap(s) if isinstance(s, tuple) else s for s in (s1, s2)]
            if op1 is None:
                return e.tensor_scalar(ap(o), ap(a), x, None, op0)
            return e.tensor_scalar(ap(o), ap(a), x, y, op0, op1)
        add("v", [fn], [a] + cols, [o], cyc(o, a))

    def cp(o, a):
        add("v", [lambda e: e.tensor_copy(ap(o), ap(a))], [a], [o], cyc(o, a))

    def fill(o, c):
        add("v", [lambda e: e.memset(ap(o), c)], [], [o], cyc(o))

    def gtt(o, win, off, b, op):
        add("v", [lambda e: e.tensor_tensor(ap(o), ap(win).indirect(ap(off)), ap(b), op)], [win, off, b], [o],
            ("fv", 0, width(o), 0, 0))

    def gcp(o, win, off):
        add("v", [lambda e: e.tensor_copy(ap(o), ap(win).indirect(ap(off)))], [win, off], [o], ("fv", 0, width(o), 0, 0))

    def scat(win, off, a):
        add("v", [lambda e: e.tensor_copy(ap(win).indirect(ap(off)), ap(a))], [off, a], [win], ("fv", 0, 0, width(a), 0))

    def act(o, a, func, bias=None, scale=None, acc=None):
        def fn(e):
            k = {}
            if bias is not None:
                k["bias"] = bias
            if scale is not None:
                k["scale"] = scale
            if acc is not None:
                k["accum_out"] = ap(acc)
            return e.activation(ap(o), ap(a), func, **k)
        add("s", [fn], [a], [o] + ([acc] if acc is not None else []), ("fs", max(64, width(o)), 0, 0, 0))

    def sfill(o, c):
        o = full(o)
        act(o, ("one", 0, width(o), 1, o[4], o[5]), F.Copy, scale=c)

    def gact(o, win, off):
        add("s", [lambda e: e.activation(ap(o), ap(win).indirect(ap(off)), F.Copy)], [win, off], [o], ("fs", 0, width(o), 0, 0))

    def mms(lst, first=True, last=True):
        fns = [(lambda o, l, x, st, sp: lambda e: e.matmul(ap(o), ap(l), ap(x), st, sp))(
            o, l, x, first and i == 0, last and i == len(lst) - 1) for i, (o, l, x) in enumerate(lst)]
        te = sum(max(min(64, width(l)), width(x)) * (4 if SCRATCH[x[0]][2] == "float32" else 1) for o, l, x in lst)
        rd = sorted(set(full(r) for o, l, x in lst for r in (l, x)))
        add("t", fns, rd, sorted(set(full(o) for o, l, x in lst)), ("ft", 0, 0, 0, te))
        if len(lst) == 1 and not last:
            ops[-1]["cls"] = "op"

    def sums(o, band, buf, lo, hi):
        return [(o, (band, 15 - p, 143 - p), (buf, lo + p, hi, 16)) for p in range(16)]

    def sums_t(bank, o0, n, buf, lo, mat, nb=1, p0=0):
        return [((bank, o0 + p, o0 + n, 16, p0, p0 + 16 * nb), (buf, lo + p, lo + 256 * nb, 16), mat) for p in range(16)]

    lv = {}

    def row(name, n, value, second=None, put=fill):
        c = sum(v[1] for v in lv.values())
        lv[name] = (c, n)
        if second is not None:
            put(("LV", c, c + n, 1, 0, 2), second)
        if second != value:
            put(("LV", c, c + n, 1, 0, 1), value)

    def const(o, sign, name, n=None, rows=1, at=0):
        c = lv[name][0] + at
        o = full(o)
        return (o, ("one" if sign > 0 else "neg", 0, o[5] - o[4], 1, 0, rows), ("LV", c, c + width(o), 1, 0, rows))

    def rounded(o, name):
        return [const(o, 1, name), const(o, -1, name)]

    def gop(fn, rd, wr, n, fix=170.0):
        add("g", [fn], rd, wr, (fix + 300.0, 2 * n, 0, 0, 0))

    def iota(o, pattern, base, cm):
        if SCRATCH[o[0]][2] == "int32":
            gop(lambda e: e.iota(ap(o), pattern, base, cm), [], [o], width(o), 130.0)
        else:
            gop(lambda e: e.iota(ap(o), pattern, base, cm, allow_small_or_imprecise_dtypes=True), [], [o], width(o), 130.0)

    def select(o, a, pattern, op, base, cm):
        gop(lambda e: e.affine_select(ap(o), ap(a), pattern, op, 0.0, base, cm), [a], [o], width(o))

    def gfill(o, c):
        o = full(o)
        a = ("kf" if SCRATCH[o[0]][2] == "float32" else "one", 0, width(o), 1, o[4], o[5])
        gop(lambda e: e.affine_select(ap(o), ap(a), [[0, width(o)]], A.is_gt, c, 0, 0), [a], [o], width(o))

    def diagonal(o, c, n, base=0):
        a = ("zero", 0, width(o), 1, o[4], o[5])
        gop(lambda e: e.affine_select(ap(o), ap(a), [[0, width(o) // n], [-1, n]], A.not_equal, c, base, 1), [a], [o], width(o))

    def dma(q, pairs, rd, wr, lat):
        s = "dm%d" % ndma[0]
        ndma[0] += 1
        return add(q, [(lambda o, i: lambda e: e.dma_start(o, i))(o, i) for o, i in pairs], rd, wr, (60.0 * len(pairs), 0, 0, 0, 0),
                   kind="dma", lat=lat, sem=s)

    def send(t, what, src, land, dst):
        rid, pid, _e = topo.addr(dst)
        m = topo.mask(core, dst)
        i = add("g", [lambda e: e.remote_dma(ap(land), ap(src), T.sem["a%s%d" % (what, t)], T.sem["l%s%d" % (what, t)], pid, rid, m)],
                [src], [], ("issue", 0, 0, 0, 0), kind="send", lat=1500.0, sem="l%s%d" % (what, t))
        add("n%d%s" % (t, what), None, [], [land], ("net_" + what, 0, 0, 0, 0), kind="arr", sem="a%s%d" % (what, t), after=i)

    IDr, nIDr = ("ID", 0, 128), ("nID", 0, 128)
    D = ("DD", 0, 4096)
    Z = 4096

    def halves(lay, flat):
        return [(lay[32 * a:32 * a + 32, :, 16 * h:16 * h + 16], flat[32 * a + 16 * h:32 * a + 16 * h + 16, :])
                for a in range(4) for h in range(2)]

    cls[0] = "ld"
    dma("y", [(T.wti[:, 0:1], T.wt[:, 0:1])], [], [("wti", 0, 1)], 1900)
    dma("y", [(T.AB0[:, Z:Z + 256], T.zv[:])], [], [("AB0", Z, Z + 256)], 2000)
    pr = halves(T.XJ, T.ef)
    dma("y", pr[:4], [], [("XJ", 0, 256, 1, 0, 64)], 2000)
    dma("s", pr[4:], [], [("XJ", 0, 256, 1, 64, 128)], 2000)
    dma("s", [(T.DD[:], T.dv[:])], [], [D], 4500)
    cls[0] = "-"
    fill(("on8", 0, 8), 1.0)
    fill(("one", 0, 256), 1.0)
    fill(("neg", 0, 128), -1.0)
    select(("b8a", 0, 8), ("on8", 0, 8), [[-16, 8]], A.is_ge, 0, 1)
    select(("b8", 0, 8), ("b8a", 0, 8), [[16, 8]], A.is_ge, 15, -1)
    select(IDr, ("one", 0, 128), [[-1, 128]], A.is_equal, 0, 1)
    fill(("zero", 0, 256), 0.0)
    iota(("kf", 0, 256), [[1, 16], [0, 16]], 0, 0)
    iota(("pi", 0, 1), [[0, 1]], 0, 1)
    zero_first = len(ops)
    cp(("wtf", 0, 1), ("wti", 0, 1))
    sfill(("OB", 0, 144), 0.0)
    act(("OB", 15, 143, 16), ("b8", 0, 8), F.Copy, scale=W1)
    act(("O8", 0, 8), ("b8", 0, 8), F.Copy, scale=W1)
    ts(("W16", 0, 8), ("b8", 0, 8), ("wtf", 0, 1), A.mult)
    ts(("W16", 8, 16), ("b8", 0, 8), ("wtf", 0, 1), A.mult, -1.0, A.mult)
    act(nIDr, IDr, F.Copy, scale=-1.0)
    act(("I32", 0, 128), IDr, F.Copy)
    act(("nI32", 0, 128), IDr, F.Copy, scale=-1.0)
    row("rb", 128, -2048.0, 0.5)
    row("m1", 128, magic(4096))
    for j in range(3):
        row("u%d" % j, 128, magic(UNITS[j]), put=sfill)
    cls[0] = "late"
    row("m16", 16, magic(16), put=sfill)
    row("7.5", 16, 7.5, put=sfill)
    row("1/4", 256, 0.25, put=sfill)
    row("m0", 256, magic(1), put=sfill)
    act(("hID", 0, 128), IDr, F.Copy, scale=0.5)
    sfill(("TT", 0, 128, 1, 32, 64), 1.0)
    sfill(("HF", 0, 128, 1, 0, 16), 0.5)
    sfill(("HF", 128, 256, 1, 0, 16), -0.5)
    cls[0] = "-"
    diagonal(("SL", 0, 256, 1, 0, 16), 1.0, 16)
    ts(("pj", 0, 1), ("pi", 0, 1), 15, A.bitwise_and)
    cp(("pf", 0, 1), ("pj", 0, 1))
    fill(("BL", 0, 128, 1, 0, 64), 0.0)
    fill(("BL", 0, 128, 1, 64, 128), 1.0)
    fill(("BL", 0, 128, 1, 64, 65), 0.0)
    CA, CC, CBB, CK, C0 = 0, 256, 512, 768, 1024
    ops[zero_first]["soft"].append(len(ops))
    fill(("CB", 0, 1024), 0.0)

    def bias(c0, lo, hi, par, one, sg=None):
        r = ("CB", c0 + 16 * lo, c0 + 16 * hi)
        put = sfill if c0 in (CA, C0) else gfill
        put(on(r, 64, 66), one)
        put(on(r, 64, 65), par)
        if sg is not None:
            diagonal(on(r, 0, 16), sg, 16)

    def runs(lst):
        out = []
        for lo, hi, k in sorted(lst):
            if out and out[-1][1] == lo and out[-1][2] == k:
                out[-1] = (out[-1][0], hi, k)
            else:
                out.append((lo, hi, k))
        return out
    def kinds(x, lst):
        return runs([(k, k + 1, (q, UNITS[ORDER[k // 8].index(x)])) for lo, hi, q in lst for k in range(lo, hi)])
    for lo, hi, (q, u) in kinds("a", A_V + A_S):
        bias(CA, lo, hi, -2 * W1, (-15 * W1 if q == "v" else W1) - u / 2)
    for lo, hi, (q, u) in kinds("c", [x + ("v",) for x in C_V] + [x + ("s",) for x in C_S if x[0] < C_LATE[0]]):
        bias(CC, lo, hi, -W1 if q == "v" else -2 * W1, (-7.5 * W1 if q == "v" else W1) - u / 4, -u / 4)
    bias(CC, C_LATE[0], C_LATE[1], 2 * W1, -17 * W1, 16 * W1)
    bias(CC, C_LAST[0], C_LAST[1], W1, -16.5 * W1, 8 * W1)
    for lo, hi, (q, u) in kinds("b", [(1, 16, "v")]):
        bias(CBB, lo, hi, -W1, -7.5 * W1, u / 2)
    bias(C0, 0, 1, -2 * W1, -15 * W1)
    act(("CB", CK, CK + 256, 1, 64, 66), ("kf", 0, 256, 1, 64, 66), F.Identity, bias=-65536.0, scale=65536.0)
    bias(CK, 0, 1, 0.0, 15.5 * 65536, -32768.0)
    gfill(("CB", CK, CK + 256, 1, 64, 65), 0.0)
    iota(("CB", CK, CK + 256, 1, 96, 97), [[0, 16], [4096, 16]], 0, 0)
    diagonal(("QP", 0, 256, 1, 0, 32), SQ, 16, -16)
    diagonal(("QP", 0, 256, 1, 0, 16), 33 * SQ, 16)
    iota(("QP", 0, 256, 1, 32, 33), [[-int(SQ), 16], [0, 16]], -145 * int(SQ), 0)
    cls[0] = "late"
    act(("QN", 0, 256, 1, 0, 33), ("QP", 0, 256, 1, 0, 33), F.Copy, scale=-1.0)
    cls[0] = "-"
    iota(("CL", 0, 128, 1, 0, 2), [[0, 8], [16, 16]], 0, 0)
    gfill(("CL", 0, 128, 1, 0, 1), 1.0)
    gfill(("CR", 0, 16, 1, 0, 2), 1.0)
    iota(("CR", 0, 16, 1, 0, 1), [[256, 16]], 0, 0)
    cls[0] = "ld"
    add("v", [lambda e: e.tensor_scalar(T.XF[:], T.XJ[:], 1184.0, None, A.add)], [("XJ", 0, 256)], [("XF", 0, 256)], ("fv", 256, 0, 0, 0))
    for b in range(8):
        add("v", [(lambda b: lambda e: e.transpose(ap(("EL0", b, 256, 8)), T.XF[:, b]))(b)], [("XF", 32 * b, 32 * b + 32)],
            [("EL0", 1000 + b, 1001 + b)], ("fv", 64, 0, 0, 0))

    def spread(buf, col, evac, n):
        H = ("pW", 0, 128, 1, 0, 16)
        mms([const(H, -1, "rb", rows=2)], last=False)
        mms(sums_t("pW", 0, 128, buf, col, ("W16", 8, 16)) + rounded(H, "m1") + sums_t("pW", 0, 128, buf, col, ("W16", 0, 8)), first=False)
        act((evac, 0, 128, 1, 0, 16), H, F.Identity, bias=-2048.0)
        o = ("pW", 256, 256 + n)
        mms([(o, (evac, 0, 128, 1, 0, 16), ("SL", 0, n, 1, 0, 16))])
        return o

    def hashed(v, el, c, d, x, n, u):
        tt(v, v, (el, c, d), A.mult)
        if el == "EL0":
            ops[-1]["rd"].append(full(("EL0", 1000, 1008)))
        tt((x, c, d), v, (el, 256 + c, 256 + d), A.add)
        ts((n, c, d), (x, c, d), 5, A.arith_shift_right, 4095, A.bitwise_and)
        if x in G_CONV:
            select((u, c, d), (n, c, d), [[0, d - c]], A.is_gt, 1, 0)
        else:
            cp((u, c, d), (n, c, d))

    def R(lo, hi):
        return ("pR1", 16 * lo + 128, 16 * hi + 128) if lo < 8 else ("pR2", 16 * lo, 16 * hi)

    def RT(lo, hi):
        return ("pR1", 0, 128, 1, 16 * lo - 16, 16 * hi - 16) if lo < 8 else ("pR2", 0, 128, 1, 16 * lo - 128, 16 * hi - 128)

    def turned(c0, lo, hi, p0=0):
        return (RT(lo, hi), ("CB", c0 + 16 * lo, c0 + 16 * hi, 1, p0, 97), ("BL", 0, 128, 1, p0, 97))

    def biased(o, c0, lo, hi, p0=0):
        return (o, ("BL", 0, 128, 1, p0, 97), ("CB", c0 + 16 * lo, c0 + 16 * hi, 1, p0, 97))

    def update(t):
        el = ("EL%d" % (t + 1), 240, 256)
        o = ("pU2", 256, 272)
        mms([const(o, 1, "7.5")], last=False)
        mms([(o, ("nI32", 0, 128), el)] + rounded(o, "m16") + [(o, ("I32", 0, 128), el), (o, ("CL", 0, 128, 1, 0, 2), ("CR", 0, 16, 1, 0, 2))],
            first=False)
        cp(("cu", 0, 16), o)
        gact(("DG", 0, 256), D, ("cu", 0, 16))
        o = ("pG", 0, 256)
        mms([const(o, -1, "1/4")], last=False)
        mms([(o, ("hID", 0, 128), ("DG", 0, 256))], first=False, last=False)
        ops[-1]["cls"] = cls[0]
        mms([(o, ("hID", 0, 128), ("hl%d" % t, 0, 256))] + rounded(o, "m0"), first=False)
        act(("dh", 0, 256), o, F.Copy)
        scat(D, ("cu", 0, 16), ("dh", 0, 256))

    for t in range(RO):
        AB, AN = "AB%d" % (t % 2), "AB%d" % ((t + 1) % 2)
        EL, EN = "EL%d" % t, "EL%d" % (t + 1)
        rnd[0] = t

        def blk(lo, hi):
            return (AB, 256 * (lo - 1), 256 * (hi - 1)) if lo else (AB, 3840, 4096)
        cls[0] = "hs"
        cut = ((0, 240), (240, 256)) if t and SPLIT else ((0, 256),)
        for c, d in cut:
            cls[0] = "li" if c == 0 else "ly"
            act((EL, 256 + c, 256 + d), (EL, c, d), F.Identity, bias=C2, scale=2080.0)
        if t == 0:
            ops[-1]["rd"].append(full(("EL0", 1000, 1008)))
        cls[0] = "hs"
        v = spread(AB, Z, "VA", 256)
        cls[0] = "zr"
        act((AB, Z + 256, Z + 512), (AB, Z, Z + 256), F.Copy)
        act((AB, Z + 512, Z + 1024), (AB, Z, Z + 512), F.Copy)
        cls[0] = "up"
        if t > 0:
            update(t - 1)
        for c, d in cut:
            cls[0] = "hs" if c == 0 else "hy"
            hashed(("pW", 256 + c, 256 + d), EL, c, d, "xa", "na", "ua")
        cls[0] = "er"
        n = 16
        src = EL
        while n < 256:
            m = min(n, 256 - n) if src == "ER" else 16
            lo = 16 if src == "ER" else 0
            to = lo + n if src == "ER" else 16
            m = min(m, 256 - to)
            if m <= 0:
                break
            add("s", [(lambda src, lo, to, m: lambda e: e.activation(T.ER[:, :, to:to + m], T[src][:, :, lo:lo + m], F.Copy))(src, lo, to, m)],
                [(src, lo, lo + m), (src, 256 + lo, 256 + lo + m)], [("ER", to, to + m), ("ER", 256 + to, 256 + to + m)],
                ("fs", max(64, 2 * m), 0, 0, 0))
            if src == "ER":
                n *= 2
            src = "ER"
        cls[0] = "ca"
        for lo, hi in PIECES:
            mms([turned(CA, lo, hi, 64)], last=False)

        def gather_a(lo, hi):
            gtt(("df", 256 * lo, 256 * hi), D, ("ua", 16 * lo, 16 * hi), (AB, Z, Z + 256 * (hi - lo)), A.subtract)
            act(blk(lo, hi), ("df", 256 * lo, 256 * hi), F.Abs)

        def mask_a(lo, hi, k, src):
            if k == "s":
                act(("ma", 256 * lo, 256 * hi), src, F.Sign, bias=-0.5)
            else:
                ts(("ma", 256 * lo, 256 * hi), src, 0.0, A.is_gt, 2.0, A.mult)
        cls[0] = "a0"
        gather_a(0, 1)
        cls[0] = "hc"
        v = spread(AB, 3840, "VC", 240)
        hashed(v, EL, 16, 256, "xc", "nc", "uc")
        cls[0] = "m0"
        dma("y", [(ap(("ZR", 256 * i, 256 * i + 256)), ap(blk(0, 1))) for i in range(4)], [blk(0, 1)], [("ZR", 0, 1024)], 2200)
        mask_a(0, 1, "v", ("df", 0, 256))
        o = ("pC", 128, 256, 1, 0, 16)
        mms([(o, ("CB", C0, C0 + 16, 1, 64, 66), ("BL", 0, 128, 1, 64, 66))] + sums_t("pC", 128, 128, "ma", 0, ("O8", 0, 8)))
        act(("BL", 0, 128, 1, 0, 16), o, F.Sign)
        nslot = [0]

        def apart(buf, off, c, d, other):
            gact((buf, 256 * c, 256 * d), D, (off, 16 * c, 16 * d))
            for lo in range(c, d, 2):
                hi = min(lo + 2, d)
                bank = BANKS[nslot[0]]
                nslot[0] += 1
                o = (bank, 0, 256 * (hi - lo))
                mms([(o, IDr, (buf, 256 * lo, 256 * hi))] + [((bank, 256 * i, 256 * i + 256), nIDr, other) for i in range(hi - lo)])
                yield lo, hi, o
        for i, (lo, hi, k) in enumerate(A_V):
            cls[0] = "av%d" % i
            gather_a(lo, hi)
            cls[0] = "am%d" % i
            mask_a(lo, hi, k, ("df", 256 * lo, 256 * hi))
        for i, (c, d, k) in enumerate(A_S):
            cls[0] = "as%d" % i
            for lo, hi, p in apart("dg", "ua", c, d, (AB, Z, Z + 256)):
                act(blk(lo, hi), p, F.Abs)
                cls[0] = "sg%d" % i
                mask_a(lo, hi, k, p)
                cls[0] = "as%d" % i
        for i, (lo, hi) in enumerate(C_V):
            cls[0] = "cv%d" % i
            gtt(("mc", 256 * lo, 256 * hi), D, ("uc", 16 * lo, 16 * hi), ("ZR", 0, 256 * (hi - lo)), A.is_gt)
        for i, (c, d) in enumerate(C_S):
            cls[0] = "cs%d" % i
            for lo, hi, p in apart("dc", "uc", c, d, blk(0, 1)):
                sg = -1.0 if lo >= C_LATE[0] else 1.0
                act(("mc", 256 * lo, 256 * hi), p, F.Sign, bias=-0.5 * sg, scale=sg)
        for i, (lo, hi) in enumerate(B_H):
            cls[0] = "hb%d" % i
            c, d = 16 * lo, 16 * hi
            v = ("pU%d" % (i % 2 + 1), 0, d - c)
            u = ("UT", 128 * i, 128 * i + 128, 1, 0, d - c)
            mms(sums_t(v[0], 256, 128, AB, 256 * (lo - 1), ("W16", 0, 8), hi - lo))
            act(u, (v[0], 256, 384, 1, 0, d - c), F.Copy)
            mms([const(v, -1, "rb", rows=2), (v, u, ("nI32", 0, d - c, 1, 0, d - c))] + rounded(v, "m1")
                + [const(v, 1, "rb"), (v, u, ("I32", 0, d - c, 1, 0, d - c))])
            hashed(v, "ER", c, d, "xb", "nb", "ub")
            cls[0] = "b%d" % i
            for p, q in B_V:
                if lo <= p < hi:
                    last_b = len(ops)
                    gtt(("mb", 256 * p, 256 * q), D, ("ub", 16 * p, 16 * q), blk(p, q), A.is_gt)
        for i, (lo, hi) in enumerate(PIECES):
            l0 = lo - lo % 8
            for j, x in enumerate(ORDER[i]):
                cls[0] = "c%s%d" % (x, i)
                e = hi
                if x != "a":
                    mms([turned(CC if x == "c" else CBB, lo, e)], first=False, last=False)
                for p, q in COUNTS[x]:
                    if lo <= p < e:
                        o = RT(p, q)
                        mms(sums_t(o[0], 0, 128, "m" + x, 256 * p, ("O8", 0, 8), q - p, o[4]) + rounded(o, "u%d" % j), first=False,
                            last=j == len(ORDER[i]) - 1 and q == e)
            cls[0] = "v%d" % i
            m = 16 * (hi - lo)
            act(("AT", 128 * i, 128 * i + 128, 1, 0, m), RT(lo, hi), F.Abs)
            mms([biased(R(l0, hi), CK, l0, hi)], last=False)
            mms([(R(lo, hi), ("AT", 128 * i, 128 * i + 128, 1, 0, m), ("ID", 0, m, 1, 0, m))], first=False)
            tt(("val", 16 * l0, 16 * hi), R(l0, hi), ("na", 16 * l0, 16 * hi), A.add)
            if i == 0:
                tt(("t1", 0, 64), ("val", 0, 64), ("val", 64, 128), A.min)
        cls[0] = "ct"
        lo, hi = C_LATE
        o = ("pU1", 0, 64)
        mms([biased(o, CC, lo, hi)], last=False)
        mms(sums(o, "OB", "mc", 256 * lo, 256 * hi), first=False)
        tt(o, o, ("val", 128, 192), A.max)
        tt(("t2", 0, 64), o, ("t1", 0, 64), A.min)
        cls[0] = "cl"
        lo, hi = C_LAST
        o = ("pC", 0, 64)
        mms([biased(o, CC, lo, hi)], last=False)
        gtt(("mc", 256 * lo, 256 * hi), D, ("uc", 16 * lo, 16 * hi), ("ZR", 0, 256 * (hi - lo)), A.is_le)
        ops[-1]["soft"] = [last_b]
        cls[0] = "tl"
        mms(sums(o, "OB", "mc", 256 * lo, 256 * hi), first=False)
        tt(o, o, ("val", 192, 256), A.max)
        tt(("t3", 0, 64), o, ("t2", 0, 64), A.min)
        tt(("t4", 0, 32), ("t3", 0, 32), ("t3", 32, 64), A.min)
        ci = ("ci", 0, 16)
        tt(ci, ("t4", 0, 16), ("t4", 16, 32), A.min)
        dst = T.cores[(rank + 1 + t % 3) % len(T.cores)]
        cls[0] = "tn"
        ts(("ni", 0, 16), ci, 4095, A.bitwise_and)
        ts(("ns%d" % t, 0, 16), ("ni", 0, 16), 1184.0, A.add)
        send(t, "n", ("ns%d" % t, 0, 16), (EN, 240, 256), dst)
        cls[0] = "tz"
        ts(("m1", 0, 16), ci, 8, A.arith_shift_right, 0x1FF0, A.bitwise_and)
        ts(("mu", 0, 16), ("m1", 0, 16), ("pf", 0, 1), A.add)
        gcp((AN, Z, Z + 256), (AB, 0, Z + 256), ("mu", 0, 16))
        send(t, "z", (AN, Z, Z + 256), ("hl%d" % t, 0, 256), dst)
        if t == RO - 1:
            dma("y", [(T.yz[:], ap((AN, Z, Z + 256)))], [(AN, Z, Z + 256)], [], 2000)
        cls[0] = "qu"
        ts(("TH", 16, 32), ("m1", 0, 16), 1.0 / 256, A.mult, 128.53125, A.add)
        ts(("TH", 0, 16), ("m1", 0, 16), 3840.0, A.is_lt, -0.5, A.add)
        o = ("pU2", 0, 128, 1, 0, 32)
        mms([(o, ("TH", 0, 32), IDr)])
        act(("TT", 0, 128, 1, 0, 32), o, F.Copy, acc=("ac", 0, 1, 1, 0, 32) if t < RO - 1 else None)
        tr = ("TT", 0, 128, 1, 0, 33)
        mms([(("pU1", 0, 240), tr, ("QP", 0, 240, 1, 0, 33)), (("pU1", 256, 496), tr, ("QN", 0, 240, 1, 0, 33))])
        tt(("y1", 0, 240), ("pU1", 0, 240), (EL, 0, 240), A.min)
        tt(("pU1", 256, 496), ("pU1", 256, 496), (EL, 16, 256), A.min)
        tt((EN, 0, 240), ("pU1", 256, 496), ("y1", 0, 240), A.max)
        cls[0] = "nt"
        if t < RO - 1:
            o = ("pH", 0, 128, 1, 0, 1)
            ac = ("ac", 0, 1, 1, 0, 16)
            mms([const(o, -1, "1/4"), (o, ac, ("HF", 0, 128, 1, 0, 16))] + rounded(o, "m0") + [(o, ac, ("HF", 128, 256, 1, 0, 16))])
            act(("BL", 0, 128, 1, 64, 65), o, F.Copy, scale=-2.0)

    cls[0] = "up"
    rnd[0] = RO
    update(RO - 1)
    dma("s", [(T.yd[:], T.DD[:])], [D], [], 4500)
    cls[0] = "end"
    ts(("XE", 0, 256), ("EL%d" % RO, 0, 256), -1184.0, A.add)
    for b in range(8):
        add("v", [(lambda b: lambda e: e.transpose(T.XF[:, b], ap(("XE", b, 256, 8))))(b)], [("XE", 0, 256)],
            [("XF", 32 * b, 32 * b + 32)], ("fv", 64, 0, 0, 0))
    pr = [(b, a) for a, b in halves(T.XF, T.ye)]
    dma("y", pr[:4], [("XF", 0, 256)], [], 2000)
    dma("s", pr[4:], [("XF", 0, 256)], [], 2000)
    return ops


def depend(ops):
    hist = {}
    deps = []
    for i, op in enumerate(ops):
        need = set()
        for rw, regs in ((0, op["rd"]), (1, op["wr"])):
            for name, lo, hi, st, p0, p1 in regs:
                bank = name in PSUM
                for j, jw, jlo, jhi, q0, q1 in hist.get(name, ()):
                    if ((jw or rw) and jlo < hi and lo < jhi and q0 < p1 and p0 < q1) or (bank and (ops[j]["q"] != op["q"] or op["q"] == "t")):
                        need.add(j)
        for name, lo, hi, st, p0, p1 in op["wr"]:
            if name not in PSUM and st == 1:
                hist[name] = [x for x in hist.get(name, []) if not (lo <= x[2] and x[3] <= hi and p0 <= x[4] and x[5] <= p1)]
        for rw, regs in ((0, op["rd"]), (1, op["wr"])):
            for name, lo, hi, st, p0, p1 in regs:
                h = hist.setdefault(name, [])
                h.append((i, rw, lo, hi, p0, p1))
                if name in PSUM:
                    keep = sorted(set(x[0] for x in h))[-12:]
                    hist[name] = [x for x in h if x[0] >= keep[0]]
        need.discard(i)
        deps.append(sorted(need))
    return deps


def schedule(ops, deps, P):
    n = len(ops)
    cl = [cost(o, P) for o in ops]
    pred = []
    for j, op in enumerate(ops):
        d = [(i, 0.0 if ops[i]["q"] == "t" == op["q"] else cl[i][1] + P["wake"]) for i in deps[j]]
        pred.append(d + [(i, 0.0) for i in op["soft"]])
    for q, seq in SEQ.items():
        pool = {}
        for i, op in enumerate(ops):
            if op["q"] == q:
                pool.setdefault((op["round"] + (op["cls"] in TAIL), op["cls"]), []).append(i)
        chain = [pool[t, x].pop(0) for t in range(RO + 1) for x in seq if pool.get((t, x))]
        for i, j in zip(chain, chain[1:]):
            pred[j].append((i, 0.0))
    succ = [[] for _ in range(n)]
    for j in range(n):
        for i, x in pred[j]:
            succ[i].append((j, x))
    left = [len(d) for d in pred]
    line = [i for i in range(n) if not left[i]]
    for i in line:
        for j, x in succ[i]:
            left[j] -= 1
            if not left[j]:
                line.append(j)
    assert len(line) == n
    pri = [0.0] * n
    for i in reversed(line):
        pri[i] = cl[i][0] + max([pri[j] + x for j, x in succ[i]] + [cl[i][1]])
    pri = [x + (P["early"] if op["cls"] == "-" else 0.0) for x, op in zip(pri, ops)]
    left = [len(d) for d in pred]
    est = [0.0] * n
    free = {}
    ready = {}
    for i in range(n):
        if not left[i]:
            ready.setdefault(ops[i]["q"], []).append(i)
    order = []
    while len(order) < n:
        best = None
        for q, lst in ready.items():
            if lst:
                t0 = max(free.get(q, 0.0), min(est[i] for i in lst))
                c = max((i for i in lst if est[i] <= t0 + P["ahead"]), key=lambda i: pri[i] - 2 * max(0.0, est[i] - t0))
                t0 = max(t0, est[c])
                if best is None or (t0, -pri[c]) < best[0]:
                    best = ((t0, -pri[c]), q, c)
        (t0, _p), q, c = best
        ready[q].remove(c)
        order.append(c)
        free[q] = t0 + cl[c][0]
        for j, x in succ[c]:
            est[j] = max(est[j], free[q] + x)
            left[j] -= 1
            if not left[j]:
                ready.setdefault(ops[j]["q"], []).append(j)
    return order


def plan(ops):
    deps = depend(ops)
    return deps, schedule(ops, deps, PLAN)


def emit(g, T, ops, deps, order):
    eng = {"v": g.vector, "s": g.scalar, "t": g.tensor, "g": g, "y": g.sync}
    qsem = {"v": "qv", "s": "qs", "t": "qt", "g": "qg"}
    count = {}
    know = {q: {} for q in eng}
    waited = {}
    total = {}
    clock = [None] * len(ops)
    token = [None] * len(ops)
    for i in order:
        op = ops[i]
        q = op["q"]
        if op["kind"] == "arr":
            token[i] = (op["sem"], 16)
            clock[i] = {op["sem"]: 16}
            total[op["sem"]] = 16
            continue
        K = know[q]
        if q == "g" and op["kind"] == "c" and K.get("qg", 0) < count.get("qg", 0):
            g.wait_ge(T.sem["qg"], count["qg"])
            K["qg"] = waited["qg"] = count["qg"]
        for j in sorted(deps[i], key=lambda j: -sum(clock[j].values())):
            s, v = token[j]
            if K.get(s, 0) >= v or (q == "t" and ops[j]["q"] == "t"):
                continue
            eng[q].wait_ge(T.sem[s], v)
            waited[s] = max(waited.get(s, 0), v)
            for a, b in clock[j].items():
                if K.get(a, 0) < b:
                    K[a] = b
        for fn in op["fn"]:
            ins = fn(eng[q])
            if op["kind"] == "dma":
                ins.then_inc(T.sem[op["sem"]], 16)
        if op["kind"] == "c":
            s = qsem[q]
            count[s] = count.get(s, 0) + 1
            ins.then_inc(T.sem[s], 1)
            token[i] = (s, count[s])
        else:
            token[i] = (op["sem"], 16 * len(op["fn"]))
        total[token[i][0]] = token[i][1]
        c = dict(K)
        c[token[i][0]] = token[i][1]
        clock[i] = c
    for s, v in total.items():
        if waited.get(s, 0) < v:
            g.wait_ge(T.sem[s], v)


def rank_program(g, core, T, topo):
    if T.rank_of(core) is None:
        return
    ops = build(T, core, topo)
    deps, order = plan(ops)
    emit(g, T, ops, deps, order)
